import numpy as np, ml_dtypes
CORES = [2,3,42,43,82,83,122,123]
N = 8
BF = ml_dtypes.bfloat16
V, A, M, RO, BN = 3072, 3072, 224, 3, 4
HOPS = [1, 3, 6]
def parts(rng):
    x = rng.integers(0, 256, (N, 8, 16, V)); sb = rng.integers(0, V, (N, 8, 16, A)); la = rng.integers(0, A, (N, 8, 16, M)); lw = rng.integers(0, A, (N, 8, 16, M))
    z = rng.integers(0, 256, (N, 8, 16, M)); b = rng.integers(0, 16, (N, 8, M)); th = rng.integers(1420, 1680, (N, 8, 1)) - 60 * (BN - 3)
    return x, sb, la, lw, z, b, th
def pack(x, sb, la, lw, z, b, th):
    return {"xs": x.reshape(N, 128, V).astype(np.float32).astype(BF), "sb": np.ascontiguousarray(sb.reshape(N, 128, A)).astype(np.int32),
            "la": np.ascontiguousarray(la.reshape(N, 128, M)).astype(np.int32), "lw": np.ascontiguousarray(lw.reshape(N, 128, M)).astype(np.int32),
            "z0": z.reshape(N, 128, M).astype(np.float32).astype(BF), "b0": b.astype(np.int32), "th": th.astype(np.int32)}
def setup_inputs(rng):
    return pack(*parts(rng))
def setup_inputs_spread(rng):
    x, sb, la, lw, z, b, th = parts(rng)
    x = (np.exp2(8 * rng.random((N, 8, 1, V))) * rng.random((N, 8, 16, V))).astype(np.int64)
    z = (np.exp2(8 * rng.random((N, 8, 1, M))) * rng.random((N, 8, 16, M))).astype(np.int64)
    th = np.minimum(np.exp2(4 + 8 * rng.random((N, 8, 1))).astype(np.int64), 4080)
    sb = (V * rng.random((N, 8, 16, A)) ** 2).astype(np.int64); la = (A * rng.random((N, 8, 16, M)) ** 2).astype(np.int64)
    lw = A - 1 - (A * rng.random((N, 8, 16, M)) ** 3).astype(np.int64)
    return pack(np.minimum(x, 255), np.minimum(sb, V - 1), np.minimum(la, A - 1), np.maximum(lw, 0), np.minimum(z, 255), b, th)
def edge(rng, hi, shape):
    return np.where(rng.random(shape) < 0.7, hi * rng.integers(0, 2, shape), rng.integers(0, hi + 1, shape))
def setup_inputs_ends(rng):
    kind = rng.integers(0, 4, (N, 8, 1, V)); x = 255 * np.where(kind == 0, 0, np.where(kind < 3, 1, rng.integers(0, 2, (N, 8, 16, V))))
    kind = rng.integers(0, 4, (N, 8, 1, M)); z = 255 * np.where(kind == 0, 0, np.where(kind == 1, 1, rng.integers(0, 2, (N, 8, 16, M))))
    sb = edge(rng, V - 1, (N, 8, 16, A)); la = edge(rng, A - 1, (N, 8, 16, M)); lw = edge(rng, A - 1, (N, 8, 16, M)); b = 15 * rng.integers(0, 2, (N, 8, M))
    m = rng.random((N, 8, 1, M)); la = np.where(m < 0.1, 0, np.where(m < 0.2, A - 1, la)); m = rng.random((N, 8, 1, M)); lw = np.where(m < 0.1, 0, np.where(m < 0.2, A - 1, lw))
    th = np.zeros((N, 8, 1), np.int64); th[:, :6, 0] = np.where(np.argsort(rng.random((N, 6)), axis=1) < 3, 1, 4080); th[:, 6] = 1; th[:, 7] = 4080
    x[:, 6:, :, 0] = 0; x[:, 6:, :, V - 1] = 255; x[:, 6:, :, A - 1] = 255; sb[:, 6:, :, A - 1] = V - 1
    for c in (0, 1, M - 2, M - 1):
        la[:, 6:, :, c] = A - 1; lw[:, 6:, :, c] = (A - 1) * (c % 2); z[:, 6, :, c] = 255; z[:, 7, :, c] = 0
    return pack(x, sb, la, lw, z, b, th)
def setup_inputs_corners(rng):
    x, sb, la, lw, z, b, th = parts(rng); odd = np.arange(V) & 1
    th[:, 0] = 1; b[:, 0] = 0
    th[:, 1] = 4080; b[:, 1] = 15
    x[:, 2] = 85 * rng.integers(0, 4, (N, 1, V)); z[:, 2] = 85 * rng.integers(0, 4, (N, 1, M)); th[:, 2] = rng.choice(np.array([1360, 1361, 2720]), (N, 1)); th[0, 2] = 1360; th[N - 1, 2] = 2720
    sb[:, 3] = sb[:, 3, :1]
    la[:, 4] = la[:, 4, :1]; lw[:, 4] = la[:, 4]; z[:, 4] = 255 * rng.integers(0, 2, (N, 1, M))
    x[:, 5] = np.where(odd == 0, 255, 0); th[:, 5, 0] = 3072 + (np.arange(N) & 1)
    n = rng.choice(np.array([0, BN - 1, BN, BN + 1, 16]), (N, 1, A))
    sb[:, 5] = 2 * rng.integers(0, V // 2, (N, 16, A)) + (np.argsort(rng.random((N, 16, A)), axis=1) >= n)
    la[:, 5] = 2 * rng.integers(0, A // 2, (N, 16, M)) + (rng.random((N, 16, M)) < 0.125)
    x[:, 6] = np.where(odd == 0, rng.integers(0, 8, (N, 16, V)), rng.integers(248, 256, (N, 16, V))); th[:, 6] = 40
    sb[:, 6] = 2 * rng.integers(0, V // 2, (N, 16, A)); la[:, 6] = 2 * rng.integers(0, A // 2, (N, 16, M)) + 1
    la[:, 7] = rng.choice(np.array([0, A - 1, A // 2]), (N, 16, M)); lw[:, 7] = rng.choice(np.array([0, A - 1, A // 2 + 1, 1]), (N, 16, M))
    sb[:, 7] = rng.choice(np.array([0, V - 1, 1, V // 2]), (N, 16, A)); sb[:, 7, :8] = np.arange(A)
    return pack(x, sb, la, lw, z, b, th)
def setup_inputs_crowd(rng):
    x, sb, la, lw, z, b, th = parts(rng); q = np.arange(V - 20, V - 4)
    o = np.arange(V) & 3; turn = ((np.arange(16)[None, :] + np.arange(N)[:, None]) & 15) < BN
    x[:, 3] = np.where(o == 0, x[:, 3], np.where(o == 1, rng.integers(110, 128, (N, 16, V)), np.where(o == 2, rng.integers(0, 41, (N, 16, V)), rng.integers(250, 256, (N, 16, V)))))
    sb[:, 3] = np.where(turn[:, :, None] & (o[:A] == 1), 4 * rng.integers(0, A // 4 - 5, (N, 16, A)) + 3, 4 * rng.integers(0, V // 4 - 5, (N, 16, A)) + 2)
    x[..., 0] = 0; x[..., A - 1] = 255; x[..., q] = 255; sb[..., A - 1] = q
    hot = np.zeros((8, M), bool); hot[1, M - 1] = True; hot[2] = True; hot[3] = True; hot[5] = rng.random(M) < 0.5; hot[6, M - 1] = True; hot[7, :M - 1] = True
    for e in (2, 4, 6):
        la[:, e] = la[:, e, :, :1]; lw[:, e] = lw[:, e, :, :1]; z[:, e] = z[:, e, :, :1]; b[:, e] = b[:, e, :1]
    la[:, 5] = rng.choice(np.array([1, 3, A // 2, A - 2]), (N, 16, M)); lw[:, 5] = rng.choice(np.array([0, 2, A // 2 + 1, A - 3]), (N, 16, M))
    la = np.where(np.arange(16)[None, None, :, None] == b[:, :, None, :], np.where(hot[None, :, None, :], A - 1, 0), la)
    kinds = rng.permutation(N) & 3
    for r in range(N):
        n, k = ((1, 2), (3, 1), (0, 3), (2, 2))[int(kinds[r])]; p = rng.permutation(M)
        for c, i in ((p[:n], 0), (p[n:n + k], 1)):
            la[r, 3][:, c] = 4 * rng.integers(0, A // 4 - 5, (16, c.size)) + i; lw[r, 3][:, c] = 4 * rng.integers(0, A // 4 - 5, (16, c.size)) + i
    return pack(x, sb, la, lw, z, b, th)
def setup_inputs_full(rng):
    x, sb, la, lw, z, b, th = parts(rng); n = np.arange(V) & 3; c = np.arange(M); v = np.arange(2, V, 4)
    for r in range(N):
        for e in (0, 7):
            x[r, e] = np.where(n == 3, rng.integers(250, 256, (16, V)), np.where(n == 1, rng.integers(228, 250, (16, V)), rng.integers(208, 256, (16, V))))
            x[r, e, (v >> 2) & 15, v] = rng.integers(208, 228, v.size)
            p = 4 * rng.permutation(A // 4)[:M] + 1
            sb[r, e] = 4 * rng.integers(0, V // 4, (16, A)) + 2
            sb[r, e, rng.integers(0, 16, M), p] = 4 * rng.permutation(V // 4)[:M] + 3
            la[r, e, b[r, e], c] = p; th[r, e, 0] = rng.integers(3300, 3329)
        for e in (1, 4):
            x[r, e] = np.where(n == 0, rng.integers(0, 64, (16, V)), np.where(n == 3, rng.integers(240, 256, (16, V)), rng.integers(128, 240, (16, V))))
            u = 4 * rng.permutation(A // 4)[:M] + 1; k = rng.integers(0, 16, M)
            sb[r, e] = 4 * rng.integers(0, V // 4, (16, A)) + np.where(n[:A] == 0, 0, 2)
            sb[r, e, k, u] = 4 * rng.permutation(V // 4)[:M] + 3
            la[r, e] = 4 * rng.integers(0, A // 4, (16, M)) + 2; lw[r, e] = 4 * rng.integers(0, A // 4, (16, M)) + 2
            la[r, e, b[r, e], c] = 4 * rng.integers(0, A // 4, M); la[r, e, (b[r, e] + rng.integers(1, 16, M)) & 15, c] = u
            lw[r, e, k, c] = 4 * rng.integers(0, A // 4, M)
            z[r, e] = x[r, e][:, u]; th[r, e, 0] = rng.integers(1800, 2049)
    for e in (2, 5):
        x[:, e] = rng.integers(208, 256, (N, 16, V)); z[:, e] = rng.integers(208, 256, (N, 16, M)); th[:, e] = rng.integers(3560, 3640, (N, 1))
    side = rng.integers(0, 2, (N, 1, M)); side[:, 0, 0] = 0; side[:, 0, M - 1] = 1
    x[:, 6] = 255 * (np.arange(V) & 1); z[:, 6] = 255 * side; b[:, 6] = 0
    la[:, 6] = 2 * rng.integers(0, A // 2, (N, 16, M)) + np.where(np.arange(16)[None, :, None] == 0, side, 1 - side)
    return pack(x, sb, la, lw, z, b, th)
def check_inputs(d):
    bad = []
    for k, lo, hi in (("xs", 0, 255), ("sb", 0, V - 1), ("la", 0, A - 1), ("lw", 0, A - 1), ("z0", 0, 255), ("b0", 0, 15), ("th", 1, 4080)):
        a = np.asarray(d[k]).astype(np.float64)
        if not np.all((a >= lo) & (a <= hi)): bad.append("range of " + k)
        elif not np.all(a == np.floor(a)): bad.append("whole numbers of " + k)
    return bad
def pick(x, ix):
    return np.stack([np.stack([np.take(x[r, e], ix[r, e].reshape(-1), axis=1).reshape(16, 16, M) for e in range(8)]) for r in range(N)])
def slot_of(a, k):
    return np.take_along_axis(a, k[:, :, None, :], 2)[:, :, 0]
def first(p, m):
    c = np.flatnonzero(m)
    return c[np.unique(p[c], return_index=True)[1]]
def reference(xs, sb, la, lw, z0, b0, th):
    x = xs.astype(np.float32).astype(np.int32).reshape(N, 8, 16, V); t = sb.astype(np.int64).reshape(N, 8, 16, A)
    l = la.astype(np.int64).reshape(N, 8, 16, M); w = lw.astype(np.int64).reshape(N, 8, 16, M)
    z = z0.astype(np.float32).astype(np.int32).reshape(N, 8, 16, M); b = b0.astype(np.int64).reshape(N, 8, M); h = th.astype(np.int64).reshape(N, 8, 1, 1)
    al = np.zeros((N, 8), np.int64); slot = np.arange(16)[None, None, :, None]
    for rnd in range(RO):
        hop = HOPS[rnd]
        y = pick(x, l); d = np.add.reduce(np.abs(y - z[:, :, :, None, :]), axis=2)
        j = np.argmin(np.where(slot == b[:, :, None], 9999, d), axis=2)
        yj = np.take_along_axis(y, j[:, :, None, None, :], 3)[:, :, :, 0]
        yb = np.take_along_axis(y, b[:, :, None, None, :], 3)[:, :, :, 0]
        lb = slot_of(l, b); lj = slot_of(l, j)
        s = np.take_along_axis(t, lb[:, :, None, :], 3)
        xc = np.roll(x, -hop, axis=0); hc = np.roll(h, -hop, axis=0); need = (BN + (al & 1))[:, :, None]
        g = np.add.reduce(np.minimum(pick(xc, s), yb[:, :, :, None, :]), axis=2)
        occ = np.add.reduce((g >= hc).astype(np.int64), axis=2) >= need
        place = slot_of(s, np.argmax(g, axis=2))
        new = np.maximum(np.take_along_axis(xc, place[:, :, None, :], 3) - (yb >> 2), 0)
        for r in range(N):
            for e in range(8):
                c = first(place[r, e], occ[r, e]); xc[r, e][:, place[r, e, c]] = new[r, e][:, c]
        q = pick(xc, s); g = np.add.reduce(np.minimum(q, yb[:, :, :, None, :]), axis=2)
        keep = occ & (np.add.reduce((g >= hc).astype(np.int64), axis=2) >= need); out = ~keep
        f = np.maximum.reduce(q, axis=3); xk = np.take_along_axis(xc, place[:, :, None, :], 3)
        x = np.roll(xc, hop, axis=0)
        u = np.argmin(np.add.reduce(np.abs(pick(x, w) - f[:, :, :, None, :]), axis=2), axis=2)
        wu = slot_of(w, u); su = slot_of(s, u)
        l = np.where((slot == b[:, :, None]) & out[:, :, None], wu[:, :, None], l)
        w = np.where((slot == u[:, :, None]) & out[:, :, None], lb[:, :, None], w)
        if rnd < RO - 1:
            for r in range(N):
                for e in range(8):
                    c = first(lj[r, e], out[r, e]); t[r, e][u[r, e, c], lj[r, e, c]] = su[r, e, c]
        z = np.where(keep[:, :, None], (z + xk) >> 1, (z + yj) >> 1)
        b = np.where(out, j, b); al = np.add.reduce(out.astype(np.int64), axis=2)
    return {"yx": x.reshape(N, 128, V).astype(np.float32).astype(BF), "yl": l.reshape(N, 128, M).astype(np.float32), "yw": w.reshape(N, 128, M).astype(np.float32),
            "yz": z.reshape(N, 128, M).astype(np.float32).astype(BF), "yb": b.astype(np.float32)}

@@ -1,0 +1,795 @@
+import numpy as np
+from concourse.bass import DstId, RemoteDMATransfer
+from concourse.mybir import dt, AluOpType, AxisListType, ActivationFunctionType
+
+AL = AluOpType
+AF = ActivationFunctionType
+s_ = np.s_
+V, M, RO, NA = 3072, 224, 3, 14
+HOPS = [1, 3, 6]
+VW = V + M
+W1 = 65536.0
+NV2, NV4, NV5, NV1 = 10, 7, 8, 0
+CH5, ABS5, REL4, FS_S = 4, 0, 0, 0
+YW, XW = 232, 240
+BF, F32, I32, U16 = "bfloat16", "float32", "int32", "uint16"
+
+SB = {
+    "x": (VW, BF), "tile": (VW, I32), "iot": (VW, F32),
+    "lai": (M, I32), "lwi": (M, I32), "bi": (M, I32), "thi": (4, I32), "z": (M, BF),
+    "bb": (M, BF), "thf": (4, F32), "thw": (4, F32),
+    "qi": (4, I32), "qj": (4, I32), "col": (16, F32), "i144": (144, F32), "gm16": (128, F32), "kidx": (M, F32), "c14": (16, F32),
+    "zp": (144, BF), "zn": (144, BF), "z2p": (144, BF), "z2n": (144, BF), "z8": (144, BF), "bo8": (128, F32), "bo": (128, BF),
+    "i32": (128, F32), "ib": (128, BF), "nib": (128, BF), "nbi": (128, BF), "mh": (M, BF),
+    "kcb": (M, BF), "kcth": (M, F32), "rst": (M, F32), "cmask": (M, BF), "poison": (M, F32), "dd0": (M, F32), "id16": (16, F32),
+    "cidx": (16, F32), "dummy": (16, F32), "t1": (16, F32), "t2": (16, F32), "t3": (16, F32), "ti": (16, I32), "tj": (16, I32),
+    "cA": (16, U16), "cS": (16, U16), "pK": (16, U16), "pA": (16, U16), "pKA": (16, U16), "pAK": (16, U16), "rep4": (4, U16),
+    "L": (256, F32), "W": (256, F32), "ssl": (256, F32), "lp": (256, F32), "wp": (256, F32),
+    "t12a": (480, F32), "t12b": (480, F32), "t12c": (480, F32), "Lu": (M, U16), "Wu": (M, U16), "oh": (M, BF), "ohw": (M, BF),
+    "n4": (64 * (RO + 1), F32), "n4u": (64 * (RO + 1), U16), "n4t": (64, F32), "base4": (64, F32), "delta4": (64, F32),
+    "ys": (YW * RO, BF), "yr": (YW * RO, BF), "ss": (M * RO, U16), "sr": (M * RO, U16), "xks": (XW * RO, BF), "yx2": ((M + XW) * RO, BF),
+    "fs": (M * RO, BF), "fr": (M * RO, BF),
+    "rawy": (16 * M, BF), "raws": (16 * M, BF), "D": (16 * M, BF), "D0": (16 * M, BF), "Do": (16 * M, BF),
+    "sf": (M, F32), "sa": (M, F32), "ywin": (16, F32), "add2": (M, F32), "thr16": (M, F32), "qq": (M, BF), "xsel": (M, BF), "new": (M, BF),
+    "key1": (M, F32), "run1": (M, F32), "u1": (M, F32), "e1": (M, F32), "sel1": (M, F32),
+    "key2": (M, F32), "run2": (M, F32), "u2": (M, F32), "e2": (M, F32), "sel2": (M, F32),
+    "key5": (M, F32), "run5": (M, F32), "u5": (M, F32), "e5": (M, F32), "sel5": (M, F32),
+    "bind": (M, BF), "cnt": (M, BF), "nocc": (16, F32), "nd": (16, F32), "need2": (16, F32), "P": (16, F32), "Pu": (16, U16),
+    "row": (M, F32), "eq": (M, BF), "dsc": (M, F32), "P2": (16, F32), "P2u": (32, U16), "T2u": (32, U16),
+    "ji": (16, I32), "jj": (16, I32), "jt": (16, F32), "jt2": (16, F32), "ju": (16, U16), "lju": (16, U16), "tlj": (M, F32), "dlt": (M, F32),
+    "wi": (16, I32), "wj": (16, I32), "wf": (16, F32), "wu": (16, U16), "tc": (M, F32), "tcol": (M, F32),
+    "ep": (16, F32), "eq1": (16, F32), "l12": (32, F32), "l12u": (32, U16), "ee": (16, F32), "tl": (M, F32), "tw": (M, F32),
+    "nf": (4, F32), "ni": (4, I32), "nj": (4, I32), "zsel": (M, BF), "zt": (M, F32),
+    "ni32": (128, F32), "ynew": (M, BF), "plu": (16, U16), "mb": (M, F32), "l0": (M, F32), "wsl": (M, F32), "lsl": (M, F32), "ol": (M, F32), "ow": (M, F32), "ob": (M, F32),
+}
+SHARED = {}
+SCRATCH = {}
+_fill = {}
+for _n, (_w, _d) in SB.items():
+    if _w <= 32:
+        _o = _fill.get(_d, 0)
+        SHARED[_n] = ("small_" + _d, _o)
+        _fill[_d] = _o + (_w + 15) // 16 * 16
+    else:
+        SCRATCH[_n] = ("sbuf", [128, _w], _d)
+for _d, _o in _fill.items():
+    SCRATCH["small_" + _d] = ("sbuf", [128, _o], _d)
+SCRATCH["thi2"] = ("sbuf", [128, 4], I32)
+for _n in ("m1", "m2", "m5", "rawv"):
+    SCRATCH[_n] = ("sbuf", [128, M, 16], BF)
+for _n in ("pka", "pkb"):
+    SCRATCH[_n] = ("psum", [128, 32, 16], F32)
+for _n in ("pd0", "pd1", "pd2", "pd3", "pm", "pf"):
+    SCRATCH[_n] = ("psum", [128, 512], F32)
+MSG = ["y", "s", "f", "k"]
+NDMA = 16
+SEMAPHORES = ["qV", "qS", "qP", "qG", "sent"] + ["dma%d" % i for i in range(NDMA)] + ["%s%d" % (m, r) for m in MSG for r in range(RO)]
+IO = {"xs": [128, V], "sb": [128, V], "la": [128, M], "lw": [128, M], "z0": [128, M], "b0": [8, M], "th": [8, 1],
+      "yx": [128, V], "yl": [128, M], "yw": [128, M], "yz": [128, M], "yb": [8, M]}
+ALL = slice(None)
+FIGURES = [(1.04, 1.56, 3.8, 0.52, 1.0), (0.95, 1.2, 2.5, 0.5, 1.4), (1.15, 1.95, 5.0, 0.6, 0.9)]
+KEY_S = "1"
+TRIES = 600
+TILE_FIRST = False
+
+
+def a(name, lo=None, hi=None, st=None, part=ALL):
+    if name in SHARED:
+        big, o = SHARED[name]
+        return (big, (part, slice(o + (lo or 0), o + (SB[name][0] if hi is None else hi), st)))
+    return (name, (part, slice(lo, hi, st)))
+
+
+def a3(name, i, j):
+    return (name, (ALL, i, j))
+
+
+def ind(win, off):
+    return ("*", win, off)
+
+
+def foot(ap):
+    name, idx = ap
+    shape = IO[name][1:] if name in IO else SCRATCH[name][1][1:]
+    n = int(np.prod(shape))
+    if name not in IO and SCRATCH[name][0] == "psum":
+        return np.arange(n)
+    return np.arange(n).reshape(shape)[idx[1:]].reshape(-1)
+
+
+def count(ap):
+    if ap[0] == "*":
+        return 16 * count(ap[2])
+    name, idx = ap
+    shape = IO[name][1:] if name in IO else SCRATCH[name][1][1:]
+    return int(np.empty(shape, np.int8)[idx[1:]].size)
+
+
+def is_ap(v):
+    return isinstance(v, tuple)
+
+
+def psum(ap):
+    return ap[0] in SCRATCH and SCRATCH[ap[0]][0] == "psum"
+
+
+def narrow(ap):
+    return SCRATCH[ap[0]][2] in (BF, U16)
+
+
+def build(CY, GA, SC, PE, LAT):
+    ops = []
+    lastw, readers = {}, {}
+
+    def add(eng, calls, outs, ins, cost, lat=0.0, tag=None, after=()):
+        me = len(ops)
+        deps = {d: True for d in after}
+        rd, wr = [], []
+        for p in ins:
+            if is_ap(p):
+                rd += [p[1], p[2]] if p[0] == "*" else [p]
+        for p in outs:
+            if p[0] == "*":
+                wr.append(p[1]); rd.append(p[2])
+            else:
+                wr.append(p)
+        excl = [p for p in rd if psum(p)]
+        rd = [p for p in rd if not psum(p)]
+        for p in rd:
+            f = foot(p)
+            lw = lastw.get(p[0])
+            if lw is not None:
+                for d in np.unique(lw[f]):
+                    if d >= 0:
+                        deps[int(d)] = True
+        for p in wr + excl:
+            f = foot(p)
+            n = foot((p[0], (ALL,))).size
+            lw = lastw.setdefault(p[0], np.full(n, -1))
+            for d in np.unique(lw[f]):
+                if d >= 0:
+                    deps.setdefault(int(d), not psum(p))
+            mark = np.zeros(n, bool); mark[f] = True
+            left = []
+            for (d, rf) in readers.get(p[0], []):
+                hit = mark[rf]
+                if hit.any():
+                    deps[d] = True
+                if not hit.all():
+                    left.append((d, rf[~hit]))
+            readers[p[0]] = left
+            lw[f] = me
+        for p in rd:
+            readers.setdefault(p[0], []).append((me, foot(p)))
+        deps.pop(me, None)
+        ops.append({"eng": eng, "calls": calls, "deps": deps, "cost": cost, "lat": lat, "tag": tag})
+        return me
+
+    def vcost(out, ins, plain):
+        if out[0] == "*":
+            return 50 + count(out) * SC * CY
+        if ins[0][0] == "*":
+            return 50 + count(out) * GA * CY
+        return 30 + max(64, plain) * CY
+
+    def half(*aps):
+        return 0.5 if all(p[0] != "*" and narrow(p) for p in aps) else 1.0
+
+    def cp(out, in_):
+        return add("V", [("tensor_copy", (out, in_), {})], [out], [in_], vcost(out, [in_], count(out) * half(out, in_)))
+
+    def tt(out, i0, i1, op):
+        two = 1.0 if (i0[0] != "*" and (psum(i0) or psum(i1))) else 2.0
+        return add("V", [("tensor_tensor", (out, i0, i1, op), {})], [out], [i0, i1], vcost(out, [i0], count(out) * two))
+
+    def ts(out, i0, s1, op0, s2=None, op1=None):
+        args = (out, i0, s1, s2, op0) + (() if op1 is None else (op1,))
+        return add("V", [("tensor_scalar", args, {})], [out], [i0, s1, s2], vcost(out, [i0], count(out) * half(out, i0)))
+
+    def scan(out, d0, d1, op0, op1):
+        return add("V", [("tensor_tensor_scan", (out, d0, d1, 0.0, op0, op1), {})], [out], [d0, d1], vcost(out, [d0], count(out) * half(out, d0, d1)))
+
+    def ms(out, c):
+        return add("V", [("memset", (out, c), {})], [out], [], vcost(out, [out], count(out) * half(out)))
+
+    def tr(out, in_):
+        return add("V", [("transpose", (out, in_), {})], [out], [in_], vcost(out, [in_], count(out)))
+
+    def act(out, in_, func=AF.Copy, **kw):
+        cost = 65 + count(out) * GA * CY if in_[0] == "*" else 65 + max(64, count(out)) * CY
+        return add("S", [("activation", (out, in_, func), kw)], [out], [in_] + list(kw.values()), cost)
+
+    def mm(items):
+        cost = sum(max(64, count(i[2])) * PE * (1 if narrow(i[2]) else 4) for i in items) + 60
+        return add("P", [("matmul", i, {}) for i in items], [i[0] for i in items], [i[1] for i in items] + [i[2] for i in items], cost)
+
+    def iota(out, pat, base, cm):
+        kw = {} if SCRATCH[out[0]][2] == I32 else {"allow_small_or_imprecise_dtypes": True}
+        return add("G", [("iota", (out, pat, base, cm), kw)], [out], [], 130 + 2 * CY * count(out))
+
+    ndma = [0]
+
+    def dma(eng, out, in_, lat, behind=False):
+        ndma[0] += 1
+        me = add(eng, [("dma_start", (out, in_), {})], [out], [in_], 60, lat, ("dma", ndma[0] - 1))
+        if behind:
+            ops[me]["behind"] = max(i for i in range(me) if ops[i]["eng"] == eng)
+        return me
+
+    def send(msg, r, src, dst, lat):
+        s = add("G", [("send", (msg, r, src, dst), {})], [], [src], 500)
+        return add("R", [], [dst], [], 0, lat * LAT, ("msg", "%s%d" % (msg, r)), after=[s])
+
+    def scatter(win, lst, vals):
+        for b in range(NA - 1, -1, -1):
+            cp(ind(win, a(lst, 2 * b, 2 * b + 1)), a(vals, 16 * b, 16 * b + 16))
+
+    def c1(name):
+        return a(name, 0, NA)
+
+    def ends(name):
+        return a(name, 15, M, 16)
+
+    def bank3(name, k0=0, k1=16):
+        return a3(name, slice(0, NA), slice(k0, k1))
+
+    def reduce(bank, zw, m, k0, k1, first, last):
+        mm([(bank3(bank, k0, k1), a(zw, 15 - p, 143 - p), a3(m, slice(p, None, 16), slice(k0, k1)), first and p == 0, last and p == 15) for p in range(16)])
+
+    turn = [0]
+
+    def diff(ks, plus, minus, func, m, first=0):
+        bank = "pd%d" % (first + turn[0] % 2); turn[0] += 1
+        n = len(ks)
+        it = []
+        for i, k in enumerate(ks):
+            o = a(bank, i, n * M, n)
+            it += [(o, a("ib"), plus(k), True, False), (o, a("nib"), minus(k), False, True)]
+        mm(it)
+        act(a3(m, ALL, slice(ks[0], ks[0] + n)), a(bank, 0, n * M), func)
+
+    def pairs(k0, k1):
+        return [list(range(k, min(k + 2, k1))) for k in range(k0, k1, 2)]
+
+    def chunks(k0, k1, n):
+        c = -(-(k1 - k0) // n)
+        e = [k0 + (k1 - k0) * i // c for i in range(c + 1)]
+        return list(zip(e[:-1], e[1:]))
+
+    def turn16(src, t12):
+        tr(a(t12, 0, M), a(src, 16, 240))
+        tr(a(t12, M, 480), a(src, 0, 256))
+
+    def gather_y():
+        for k0, k1 in chunks(0, 16, 2):
+            (cp if k0 < NV1 else act)(a("rawy", M * k0, M * k1), ind(a("x"), a("Lu", NA * k0, NA * k1)))
+
+    def running(n, bank):
+        (act if n in KEY_S else cp)(a("key" + n), bank3(bank))
+        scan(a("run" + n), a("rst"), a("key" + n), AL.add, AL.max)
+
+    def choose(n, bank, val):
+        mm([(a("pf", 0, M), a("i32"), val, True, True)])
+        tt(a("u" + n), a("run" + n), bank3(bank), AL.subtract)
+        tt(a("e" + n), a("pf", 0, M), a("u" + n), AL.subtract)
+        scan(a("sel" + n), a("u" + n), a("e" + n), AL.min, AL.max)
+
+    def slot(n, ti, tj):
+        ts(c1(ti), ends("run" + n), -1.0 / 4096, AL.mult, 131072.0, AL.add)
+        ts(c1(tj), c1(ti), 15, AL.bitwise_and)
+
+    def lowest(pw, p14, pu, outu):
+        tt(a("row"), ind(a("iot"), pu), a("poison"), AL.add)
+        tt(a("eq"), ind(pw, c1("cA")), a("row"), AL.is_equal)
+        scan(a("dsc"), a("dd0"), a("eq"), AL.mult, AL.max)
+        tt(c1("P2"), ends("dsc"), p14, AL.max)
+        cp(a(outu, 0, 2 * NA, 2), c1("P2"))
+
+    X = a("x")
+    P8 = slice(0, 8)
+    whole = lambda n: (n, (ALL, ALL))
+    dma("Y", a("lai"), whole("la"), 2200)
+    dma("S", a("bi", part=P8), whole("b0"), 2000)
+    big = [(a("tile", 0, V), whole("sb"), 4500), (a("x", 0, V), whole("xs"), 2300)]
+    t = 2200
+    for o, i, d in (big if TILE_FIRST else big[::-1]):
+        t += d
+        dma("Y", o, i, t, True)
+    dma("S", a("thi2", 0, 1, part=P8), whole("th"), 2000)
+    dma("S", a("z"), whole("z0"), 2500)
+    dma("S", a("lwi"), whole("lw"), 2500)
+    iota(a("qi", 0, 1), [[0, 1]], 0, 1)
+    iota(a("i144"), [[1, 144]], 0, 0)
+    iota(a("gm16"), [[16, 8], [0, 16]], 0, 0)
+    iota(a("kidx"), [[0, NA], [1, 16]], 0, 0)
+    for i in range(4):
+        iota(a("iot", VW // 4 * i, VW // 4 * (i + 1)), [[1, VW // 4]], VW // 4 * i, 0)
+    cols = ["q", "p", "g16", "g16e", "q16", "q16e", "p14", "e", "fl", "ms"]
+    C = {n: a("col", i, i + 1) for i, n in enumerate(cols)}
+    c14 = a("i144", 0, NA)
+    cp(C["q"], a("qi", 0, 1))
+    ts(a("qj", 0, 1), a("qi", 0, 1), 15, AL.bitwise_and)
+    cp(C["p"], a("qj", 0, 1))
+    tt(C["g16"], C["q"], C["p"], AL.subtract)
+    ts(C["g16e"], C["g16"], 15.0, AL.add)
+    ts(C["q16"], C["q"], 16.0, AL.mult)
+    ts(C["q16e"], C["q"], 16.0, AL.mult, 15.0, AL.add)
+    ts(C["p14"], C["p"], 14.0, AL.mult)
+    ts(a("qj", 1, 2), a("qi", 0, 1), 4, AL.arith_shift_right, 1, AL.bitwise_and)
+    cp(C["e"], a("qj", 1, 2))
+    tt(a("qi", 1, 2), C["p"], C["e"], AL.add)
+    ts(a("qj", 2, 3), a("qi", 1, 2), 1, AL.bitwise_and)
+    ts(C["fl"], a("qj", 2, 3), 240.0, AL.mult)
+    ts(C["ms"], C["p"], float(NV2), AL.is_ge)
+    ts(c1("cidx"), c14, 16.0, AL.mult, C["p"], AL.add)
+    ts(c1("dummy"), c1("cidx"), float(V), AL.add)
+    cp(c1("cA"), c14)
+    ts(c1("pKA"), c14, C["p14"], AL.add)
+    ts(c1("ti"), c14, C["e"], AL.add)
+    ts(c1("tj"), c1("ti"), 1, AL.bitwise_and)
+    ts(c1("t1"), c1("tj"), 240.0, AL.mult)
+    tt(c1("t2"), c1("t1"), c1("cidx"), AL.add)
+    cp(c1("pA"), c1("t2"))
+    ts(c1("ji"), c1("cidx"), -6.5, AL.add, 1.0 / 14, AL.mult)
+    ts(c1("jt"), c1("ji"), -223.0, AL.mult)
+    ts(c1("jt2"), c1("cidx"), 16.0, AL.mult)
+    tt(c1("t3"), c1("jt"), c1("jt2"), AL.add)
+    cp(c1("pAK"), c1("t3"))
+    ts(c1("pK"), c1("t3"), C["fl"], AL.add)
+    ts(c1("wf"), c14, -14.0, AL.add, C["ms"], AL.mult)
+    ts(c1("cS"), c1("wf"), 14.0, AL.add)
+    ts(a("rep4"), a("i144", 0, 4), 0.0, AL.mult, C["p"], AL.add)
+    for n, w in (("zp", W1), ("zn", -W1), ("z2p", 2 * W1), ("z2n", -2 * W1)):
+        ts(a(n), a("i144"), C["g16e"], AL.is_equal, w, AL.mult)
+    ts(a("z8"), a("i144"), C["q16e"], AL.is_equal)
+    ts(a("bo8"), a("gm16"), C["q16"], AL.is_equal)
+    ts(a("bo"), a("gm16"), C["g16"], AL.is_equal)
+    ts(a("i32"), a("i144", 0, 128), C["q"], AL.is_equal)
+    cp(a("ib"), a("i32"))
+    ts(a("nib"), a("ib"), -1.0, AL.mult)
+    ts(a("nbi"), a("ib"), -2.0 ** 29, AL.mult)
+    ts(a("kcb"), a("kidx"), -4096.0, AL.mult)
+    ts(a("rst"), a("kidx"), 0.0, AL.is_equal, -2.0 ** 30, AL.mult)
+    ts(a("cmask"), a("kidx"), 0.0, AL.is_gt)
+    ts(a("poison"), a("kidx"), C["p"], AL.is_ge, 8192.0, AL.mult)
+    cp(a("dd0"), a("cmask"))
+    cp(ends("dd0"), c1("dummy"))
+    ts(a("id16"), a("kidx", 0, 16), C["p"], AL.is_equal)
+    ms(a("mh"), -0.5)
+    ms(a("x", V, VW), 0.0)
+    ms(a("tile", V, VW), 0)
+    for n in ("L", "W", "ssl", "lp", "wp"):
+        ms(a(n, 0, 256, 240), 0.0) if False else (ms(a(n, 0, 16), 0.0), ms(a(n, 240, 256), 0.0))
+    for r in range(RO):
+        ms(a("ys", YW * r + M, YW * (r + 1)), -8.0)
+    for r in range(RO):
+        ms(a("xks", XW * r + M + NA, XW * (r + 1)), 0.0)
+    ms(a("ywin"), 0.0)
+    ms(a("P"), 0.0)
+    ms(a("wf"), 0.0)
+    ms(a("ee"), 0.0)
+    ms(a("n4", 0, 64), 0.0)
+    ms(a("base4"), 0.0)
+    ms(a("delta4"), float(M))
+    cp(a("base4", 48, 48 + NA), c1("cidx"))
+    for i in range(4):
+        iota(a("D0", 4 * M * i, 4 * M * (i + 1)), [[0, 4 * M]], 0, 0)
+    ms(a("D0", 0, None, 16), -1024.0)
+    cp(a("lp", 16, 240), a("lai"))
+    turn16("lp", "t12a")
+    cp(a("Lu"), ind(a("t12a"), c1("pK")))
+    cp(a("L", 16, 240), ind(a("t12a"), c1("pA")))
+    cp(a("bb", part=P8), a("bi", part=P8))
+    mm([(a("pm", 0, NA), a("z8", 15 - p, 143 - p, part=P8), a("bb", p, M, 16, part=P8), p == 0, p == 15) for p in range(16)])
+    cp(a("n4", 16, 16 + NA), a("pm", 0, NA))
+    tt(a("oh"), ind(a("n4", 16, 32), c1("cA")), a("kidx"), AL.is_equal)
+    tt(a("tl"), a("oh"), a("L", 16, 240), AL.mult)
+    scan(a("tw"), a("cmask"), a("tl"), AL.mult, AL.add)
+    cp(a("n4", 0, NA), ends("tw"))
+    cp(a("n4u", 0, 64), a("n4", 0, 64))
+    cp(a("thf", 0, 1, part=P8), a("thi2", 0, 1, part=P8))
+    mm([(a("pm", 0, 1), a("bo8", part=P8), a("thf", 0, 1, part=P8), True, True)])
+    ts(a("thw", 0, 1), a("pm", 0, 1), -W1, AL.mult)
+    ts(a("kcth"), a("kidx"), -4096.0, AL.mult, a("thw", 0, 1), AL.add)
+    act(a("ni32"), a("i32"), AF.Identity, scale=-1.0)
+    cp(a("wp", 16, 240), a("lwi"))
+    turn16("wp", "t12b")
+    cp(a("Wu"), ind(a("t12b"), c1("pK")))
+    act(a("W", 16, 240), ind(a("t12b"), c1("pA")))
+
+    for r in range(RO):
+        last = r == RO - 1
+        n0, n1 = 64 * r, 64 * (r + 1)
+        LB, LBu, B = a("n4", n0, n0 + NA), a("n4u", n0, n0 + NA), a("n4", n0 + 16, n0 + 16 + NA)
+        yr, need = a("yr", YW * r, YW * r + M), a("yr", YW * r + M, YW * r + M + 1)
+        sl = lambda name, k, n=1, o=0: a(name, o + NA * k, o + NA * (k + n))
+        kb = lambda name, k, n=1: a(name, M * k, M * (k + n))
+        act(a("ys", YW * r, YW * r + M), ind(X, LBu))
+        send("y", r, a("ys", YW * r, YW * (r + 1)), a("yr", YW * r, YW * (r + 1)), 3000)
+        cp(a("ssl", 16, 240), ind(a("tile"), LBu))
+        turn16("ssl", "t12c")
+        cp(kb("ss", r), ind(a("t12c"), c1("pK")))
+        send("s", r, kb("ss", r), kb("sr", r), 3000)
+        if r == 0:
+            gather_y()
+        for ks in pairs(0, 16):
+            diff(ks, lambda k: kb("rawy", k), lambda k: a("z"), AF.Abs, "m1", 2)
+        mm([(bank3("pkb"), a("ib"), a("kcb"), True, False), (bank3("pkb"), a("nbi"), a("oh"), False, False)])
+        for k0, k1 in chunks(0, 16, 8):
+            reduce("pkb", "zn", "m1", k0, k1, False, k1 == 16)
+        mm([(a("pm", 0, NA), a("zp", 15 - p, 143 - p), a("yr", YW * r + p, YW * r + M, 16), p == 0, p == 15) for p in range(16)])
+        act(c1("ywin"), a("pm", 0, NA))
+        act(a("add2"), ind(a("ywin"), c1("cS")))
+        act(a("thr16"), ind(a("ywin"), c1("cA")), AF.Identity, bias=a("thw", 0, 1))
+        act(a("qq"), yr, AF.Identity, scale=0.25, bias=159.625)
+        act(a("D0", NV4, None, 16), yr)
+        mm([(bank3("pka"), a("i32"), a("kcth"), True, False)])
+        for k in range(NV2):
+            tt(a3("m2", ALL, k), ind(X, sl("sr", k, 1, M * r)), yr, AL.min)
+        for ks in pairs(NV2, 16):
+            act(kb("raws", ks[0], len(ks)), ind(X, sl("sr", ks[0], len(ks), M * r)))
+        for ks in pairs(NV2, 16):
+            diff(ks, lambda k: yr, lambda k: kb("raws", k), AF.Relu, "m2")
+        cv = chunks(0, NV2, 5)
+        for k0, k1 in cv[:-1]:
+            reduce("pka", "zp", "m2", k0, k1, False, False)
+        mm([(bank3("pka"), a("i32"), a("add2"), False, False)])
+        reduce("pka", "zn", "m2", NV2, 16, False, False)
+        reduce("pka", "zp", "m2", cv[-1][0], cv[-1][1], False, True)
+        cp(a("sf"), kb("sr", r))
+        act(a("sa"), ind(a("sf"), c1("pKA")))
+        running("2", "pka")
+        act(a("bind"), a("key2"), AF.Sign, bias=61440.5)
+        choose("2", "pka", a("sa"))
+        scan(a("cnt"), a("cmask"), a("bind"), AL.mult, AL.add)
+        ts(c1("nocc"), ends("cnt"), need, AL.is_lt)
+        tt(c1("nd"), c1("nocc"), c1("dummy"), AL.mult)
+        tt(c1("P"), ends("sel2"), c1("nd"), AL.max)
+        cp(c1("Pu"), c1("P"))
+        ts(c1("need2"), c1("nocc"), 99.0, AL.mult, need, AL.add)
+        act(a("xsel"), ind(X, c1("Pu")))
+        mm([(a("pm", 0, M), a("ib"), a("xsel"), True, False), (a("pm", 0, M), a("nib"), a("qq"), False, True)])
+        act(a("new"), a("pm", 0, M), AF.Relu, bias=160.0)
+        lowest(a("P"), c1("P"), c1("Pu"), "P2u")
+        scatter(X, "P2u", "new")
+        if last:
+            dma("Y", whole("yx"), a("x", 0, V), 4500)
+        for k in range(NV4):
+            tt(a("D", k, None, 16), ind(X, sl("sr", k, 1, M * r)), yr, AL.subtract)
+        for k in range(NV4, 16):
+            act(a("D", k, None, 16), ind(X, sl("sr", k, 1, M * r)))
+        for k in range(NV4):
+            if k < REL4:
+                act(a3("m2", ALL, k), a("D", k, None, 16), AF.Relu, scale=-1.0)
+            else:
+                ts(a3("m2", ALL, k), a("D", k, None, 16), -1.0, AL.mult, 0.0, AL.max)
+        for ks in pairs(NV4, 16):
+            diff(ks, lambda k: yr, lambda k: a("D", k, None, 16), AF.Relu, "m2")
+        scan(a("Do"), a("D0"), a("D"), AL.add, AL.max)
+        (act if FS_S else cp)(kb("fs", r), a("Do", 15, None, 16))
+        send("f", r, kb("fs", r), kb("fr", r), 3000)
+        mm([(bank3("pka"), a("i32"), a("thr16"), True, False)])
+        for k0, k1 in [(0, NV4)] + chunks(NV4, 16, 5):
+            reduce("pka", "zn", "m2", k0, k1, False, k1 == 16)
+        act(a("bind"), bank3("pka"), AF.Sign, bias=0.5)
+        scan(a("cnt"), a("cmask"), a("bind"), AL.mult, AL.add)
+        x0, y0 = XW * r, (M + XW) * r
+        tt(a("xks", x0 + M, x0 + M + NA), ends("cnt"), c1("need2"), AL.is_ge)
+        act(a("xks", x0, x0 + M), ind(X, c1("Pu")))
+        send("k", r, a("xks", x0, x0 + XW), a("yx2", y0 + M, y0 + M + XW), 3000)
+        running("1", "pkb")
+        choose("1", "pkb", a("L", 16, 240))
+        slot("1", "ji", "jj")
+        act(a("base4", 0, NA), ends("sel1"))
+        cp(a("base4", 16, 16 + NA), c1("jj"))
+        tt(a("delta4", 0, NA), LB, ends("sel1"), AL.subtract)
+        tt(a("delta4", 16, 16 + NA), B, a("base4", 16, 16 + NA), AL.subtract)
+        ts(c1("jt"), c1("jj"), float(M), AL.mult)
+        tt(c1("jt2"), c1("jt"), c1("cidx"), AL.add)
+        cp(c1("ju"), c1("jt2"))
+        act(a("yx2", y0, y0 + M), ind(a("rawy"), c1("ju")))
+        if not last:
+            act(a("base4", 32, 32 + NA), ends("sel1"))
+            tt(a("delta4", 32, 32 + NA), c1("dummy"), ends("sel1"), AL.subtract)
+            cp(c1("lju"), ends("sel1"))
+            cp(a("tlj"), ind(a("tile"), c1("lju")))
+            mm([(a("pm", 0, M), a("i32"), a("ssl", 16, 240), True, False), (a("pm", 0, M), a("ni32"), a("tlj"), False, True)])
+            act(a("dlt"), a("pm", 0, M))
+            ts(c1("t1"), B, float(M), AL.mult)
+            tt(c1("t2"), c1("t1"), c1("cidx"), AL.add)
+            cp(c1("plu"), c1("t2"))
+            gather_y()
+        else:
+            turn16("L", "t12a")
+            act(a("lsl"), ind(a("t12a"), c1("pA")))
+            turn16("W", "t12b")
+            act(a("wsl"), ind(a("t12b"), c1("pA")))
+            act(a("mb"), ind(a("id16"), a("n4u", n0 + 16, n0 + 16 + NA)))
+            act(a("tl"), a("mb"), AF.Identity, scale=-1.0, bias=1.0)
+            tt(a("l0"), a("lsl"), a("tl"), AL.mult)
+        fr = kb("fr", r)
+        for ks in pairs(NV5, 16):
+            act(kb("raws", ks[0], len(ks)), ind(X, sl("Wu", ks[0], len(ks))))
+        for k in range(NV5):
+            tt(a3("rawv", ALL, k), ind(X, sl("Wu", k)), fr, AL.subtract)
+        for n, ks in enumerate(pairs(NV5, 16)):
+            diff(ks, lambda k: kb("raws", k), lambda k: fr, AF.Abs, "m5", 2 * (n // 2 % 2))
+        mm([(bank3("pkb"), a("ib"), a("kcb"), True, False)])
+        cv, cs = chunks(0, NV5, CH5), chunks(NV5, 16, 5)
+        for n, (k0, k1) in enumerate(cv):
+            if n < ABS5:
+                act(a3("m5", ALL, slice(k0, k1)), a3("rawv", ALL, slice(k0, k1)), AF.Abs)
+            else:
+                ts(a3("m5", ALL, slice(k0, k1)), a3("rawv", ALL, slice(k0, k1)), 0.0, AL.max)
+        for k0, k1 in cs[:-1]:
+            reduce("pkb", "zn", "m5", k0, k1, False, False)
+        for n, (k0, k1) in enumerate(cv):
+            if n >= ABS5:
+                reduce("pkb", "zp", "rawv", k0, k1, False, False)
+            if k1 == NV5:
+                reduce("pkb", "zn", "m5", cs[-1][0], 16, False, False)
+            reduce("pkb", "zn" if n < ABS5 else "z2n", "m5", k0, k1, False, k1 == NV5)
+        kr, kr14 = a("yx2", y0 + 2 * M, y0 + 2 * M + 16), a("yx2", y0 + 2 * M, y0 + 2 * M + NA)
+        tt(a("n4t"), ind(kr, a("rep4")), a("delta4"), AL.mult)
+        tt(a("n4", n1, n1 + 64), a("n4t"), a("base4"), AL.add)
+        cp(a("n4u", n1, n1 + 64), a("n4", n1, n1 + 64))
+        if not last:
+            mm([(a("pm", 0, NA), a("bo"), kr14, True, True)])
+            add("V", [("tensor_reduce", (a("nf", 0, 1), a("pm", 0, NA), AxisListType.X, AL.add), {})], [a("nf", 0, 1)], [a("pm", 0, NA)], 100)
+            cp(a("ni", 0, 1), a("nf", 0, 1))
+            ts(a("nj", 0, 1), a("ni", 0, 1), 1, AL.bitwise_and)
+            ts(a("ys", YW * (r + 1) + M, YW * (r + 1) + M + 1), a("nj", 0, 1), 2.0, AL.mult, -8.0, AL.add)
+            lowest(a("n4", n1 + 32, n1 + 48), a("n4", n1 + 32, n1 + 32 + NA), a("n4u", n1 + 32, n1 + 32 + NA), "T2u")
+        act(a("zsel"), ind(a("yx2", y0, y0 + 2 * M), a("n4u", n1 + 48, n1 + 48 + NA)))
+        mm([(a("pm", 0, M), a("ib"), i, n == 0, n == 2) for n, i in enumerate((a("mh"), a("z"), a("zsel")))])
+        act(a("zt"), a("pm", 0, M), AF.Identity, bias=1.5 * 2.0 ** 24)
+        act(a("z"), a("zt"), AF.Identity, scale=0.5, bias=-1.5 * 2.0 ** 23)
+        running("5", "pkb")
+        slot("5", "wi", "wj")
+        cp(c1("wu"), c1("wj"))
+        if not last:
+            tt(a("tc"), ind(a("id16"), c1("wu")), a("dlt"), AL.mult)
+            mm([(a("pm", 0, M), a("i32"), a("tlj"), True, True)])
+            tt(a("tcol"), a("tc"), a("pm", 0, M), AL.add)
+            scatter(a("tile"), "T2u", "tcol")
+        choose("5", "pkb", a("W", 16, 240))
+        tt(c1("eq1"), LB, ends("sel5"), AL.subtract)
+        tt(c1("ep"), c1("eq1"), kr14, AL.mult)
+        if not last:
+            tt(c1("ee"), c1("ep"), c1("eq1"), AL.subtract)
+            tt(a("l12", 0, NA), ends("sel5"), c1("ep"), AL.add)
+            cp(a("l12u", 0, NA), a("l12", 0, NA))
+            act(a("ynew"), ind(X, a("l12u", 0, NA)))
+            cp(ind(a("rawy"), c1("plu")), a("ynew"))
+            tt(a("tl"), ind(a("ee"), c1("cA")), a("oh"), AL.mult)
+            mm([(a("pm", 0, M), a("i32"), a("L", 16, 240), True, False), (a("pm", 0, M), a("i32"), a("tl"), False, True)])
+            act(a("L", 16, 240), a("pm", 0, M))
+            if r < RO - 2:
+                cp(a("Lu"), ind(a("L", 16, 240), c1("pAK")))
+            cp(c1("wf"), c1("wj"))
+            tt(a("ohw"), ind(a("wf"), c1("cA")), a("kidx"), AL.is_equal)
+            tt(a("tw"), ind(a("ee"), c1("cA")), a("ohw"), AL.mult)
+            mm([(a("pm", 0, M), a("i32"), a("W", 16, 240), True, False), (a("pm", 0, M), a("ni32"), a("tw"), False, True)])
+            act(a("W", 16, 240), a("pm", 0, M))
+            cp(a("Wu"), ind(a("W", 16, 240), c1("pAK")))
+            tt(a("oh"), ind(a("n4", n1 + 16, n1 + 32), c1("cA")), a("kidx"), AL.is_equal)
+        else:
+            tt(a("l12", 0, NA), ends("sel5"), c1("ep"), AL.add)
+            tt(a("l12", 16, 16 + NA), LB, c1("ep"), AL.subtract)
+            cp(a("l12u", 0, NA), a("l12", 0, NA))
+            cp(a("l12u", 16, 16 + NA), a("l12", 16, 16 + NA))
+            tt(a("tw"), ind(a("iot"), a("l12u", 16, 16 + NA)), a("wsl"), AL.subtract)
+            tt(a("tc"), ind(a("id16"), c1("wu")), a("tw"), AL.mult)
+            tt(a("ow"), a("tc"), a("wsl"), AL.add)
+            tt(a("tl"), ind(a("iot"), a("l12u", 0, NA)), a("mb"), AL.mult)
+            tt(a("ol"), a("tl"), a("l0"), AL.add)
+            act(a("ob"), ind(a("iot"), a("n4u", n1 + 16, n1 + 16 + NA)))
+            dma("Y", whole("yb"), a("ob", part=slice(0, 128, 16)), 2000)
+            dma("Y", whole("yz"), a("z"), 2200)
+            dma("Y", whole("yw"), a("ow"), 2200)
+            dma("S", whole("yl"), a("ol"), 2200)
+    return ops
+
+
+def waits_for(o, d, raw):
+    if d["tag"] is not None or o["eng"] != d["eng"]:
+        return True
+    return raw and o["eng"] != "P"
+
+
+def arrange(plans):
+    ops = plans[0]
+    n = len(ops)
+    eng = [o["eng"] for o in ops]
+    cost = [[o["cost"] for o in pl] for pl in plans]
+    lat = [[o["lat"] for o in pl] for pl in plans]
+    pred = [[(d, 0 if not waits_for(o, ops[d], raw) else (SAME if o["eng"] == eng[d] else CROSS)) for d, raw in o["deps"].items()] for o in ops]
+    for i, o in enumerate(ops):
+        if "behind" in o:
+            pred[i].append((o["behind"], -o["lat"] - lat[0][o["behind"]]))
+    succ = [[] for _ in range(n)]
+    for i in range(n):
+        for d, gp in pred[i]:
+            succ[d].append((i, gp))
+
+    def remaining(c):
+        rest = [0.0] * n
+        for i in range(n - 1, -1, -1):
+            rest[i] = c[i] + lat[0][i] + max([gp + rest[j] for j, gp in succ[i]] + [0.0])
+        return rest
+
+    def lay(rest):
+        c0, l0 = cost[0], lat[0]
+        left = [len(p) for p in pred]
+        ready = [0.0] * n
+        free = {e: 0.0 for e in eng}
+        pool = {e: [] for e in eng}
+        for i in range(n):
+            if left[i] == 0:
+                pool[eng[i]].append(i)
+        seq = []
+        for _ in range(n):
+            t, e = min((max(free[e], min(ready[i] for i in p)), e) for e, p in pool.items() if p)
+            same = pool[e]
+            now = max((i for i in same if ready[i] <= t), key=lambda i: rest[i])
+            soon = [i for i in same if t < ready[i] < t + HOLD * c0[now] and rest[i] > rest[now] + c0[now]]
+            pick = max(soon, key=lambda i: rest[i]) if soon else now
+            free[e] = max(t, ready[pick]) + c0[pick]
+            seq.append(pick)
+            same.remove(pick)
+            for j, gp in succ[pick]:
+                ready[j] = max(ready[j], free[e] + l0[pick] + gp)
+                left[j] -= 1
+                if left[j] == 0:
+                    pool[eng[j]].append(j)
+        return seq
+
+    def span(seq, k):
+        c, l = cost[k], lat[k]
+        done = [0.0] * n
+        free = {e: 0.0 for e in eng}
+        for i in seq:
+            t = free[eng[i]]
+            for d, gp in pred[i]:
+                if done[d] + gp > t:
+                    t = done[d] + gp
+            free[eng[i]] = t + c[i]
+            done[i] = t + c[i] + l[i]
+        return max(done), done
+
+    def worth(rest):
+        seq = lay(rest)
+        return sum(span(seq, k)[0] for k in range(len(plans))), seq
+
+    def pack(prio, back):
+        c, l = cost[0], lat[0]
+        before, after = (succ, pred) if back else (pred, succ)
+        left = [len(p) for p in before]
+        pool = [i for i in range(n) if left[i] == 0]
+        at = [0.0] * n
+        busy = {e: [] for e in eng}
+        while pool:
+            i = min(pool, key=lambda j: prio[j])
+            pool.remove(i)
+            if back:
+                t = max([at[d] + c[d] + gp for d, gp in before[i]] + [0.0]) + l[i]
+            else:
+                t = max([at[d] + c[d] + l[d] + gp for d, gp in before[i]] + [0.0])
+            b = busy[eng[i]]
+            k = len(b)
+            while k and b[k - 1][1] > t:
+                k -= 1
+            while k < len(b) and b[k][0] < t + c[i]:
+                t = max(t, b[k][1])
+                k += 1
+            b.insert(k, (t, t + c[i]))
+            at[i] = t
+            for j, gp in after[i]:
+                left[j] -= 1
+                if left[j] == 0:
+                    pool.append(j)
+        return at
+
+    def justify(prio):
+        at = pack(prio, False)
+        at = pack([-(at[i] + cost[0][i]) for i in range(n)], True)
+        at = pack([-(at[i] + cost[0][i]) for i in range(n)], False)
+        s = sorted(range(n), key=lambda i: (at[i], i))
+        return sum(span(s, k)[0] for k in range(len(plans))), s, at
+
+    rng = np.random.default_rng(7)
+    best, seq = worth(remaining(cost[0]))
+    at = span(seq, 0)[1]
+    at = [at[i] - cost[0][i] - lat[0][i] for i in range(n)]
+    for _ in range(TRIES):
+        t0, wide = rng.random() * max(at), rng.choice([3000.0, 8000.0, 20000.0])
+        noise = rng.normal(0, rng.choice([300.0, 1000.0, 2500.0]), n)
+        w, s, a2 = justify([at[i] + (float(noise[i]) if t0 <= at[i] < t0 + wide else 0.0) for i in range(n)])
+        if w <= best:
+            best, seq, at = w, s, a2
+    ends_, done = span(seq, 0)
+    order = {}
+    for i in seq:
+        order.setdefault(eng[i], []).append(i)
+        ops[i]["at"] = done[i] - cost[0][i] - lat[0][i]
+    return order, [span(seq, k)[0] for k in range(len(plans))]
+
+
+HOLD, SAME, CROSS = 0.5, 60, 120
+PLAN = {}
+NE = 8
+
+
+def rank_program(g, core, T, topo):
+    rank = T.rank_of(core)
+    if rank is None:
+        return
+    if not PLAN:
+        plans = [build(*f) for f in FIGURES]
+        PLAN["ops"] = plans[0]
+        PLAN["order"], PLAN["end"] = arrange(plans)
+    ops, order = PLAN["ops"], PLAN["order"]
+    N = len(T.cores)
+    queue = {"V": g.vector, "S": g.scalar, "P": g.tensor, "G": g, "Y": g.sync}
+    call = {
+        "tensor_copy": g.vector.tensor_copy, "tensor_tensor": g.vector.tensor_tensor, "tensor_scalar": g.vector.tensor_scalar,
+        "tensor_tensor_scan": g.vector.tensor_tensor_scan, "memset": g.vector.memset, "transpose": g.vector.transpose,
+        "tensor_reduce": g.vector.tensor_reduce, "activation": g.scalar.activation, "matmul": g.tensor.matmul, "iota": g.iota,
+    }
+
+    def real(p):
+        if not is_ap(p):
+            return p
+        if p[0] == "*":
+            return real(p[1]).indirect(real(p[2]))
+        return T[p[0]][p[1]]
+
+    def peer(msg, r):
+        return T.cores[(rank + HOPS[r]) % N] if msg in ("y", "s") else T.cores[(rank - HOPS[r]) % N]
+
+    token = {}
+    for eng, lst in order.items():
+        c = 0
+        for i in lst:
+            tag = ops[i]["tag"]
+            if tag is not None:
+                token[i] = ("dma%d" % tag[1], 16) if tag[0] == "dma" else (tag[1], NE)
+            elif ops[i]["calls"][0][0] != "send":
+                c += 1
+                token[i] = ("q" + eng, c)
+    total = {}
+    for s, c in token.values():
+        total[s] = max(total.get(s, 0), c)
+    nsent = 0
+    for eng, lst in order.items():
+        if eng == "R":
+            continue
+        q = queue[eng]
+        seen = {}
+        for i in lst:
+            o = ops[i]
+            want = {}
+            for d, raw in o["deps"].items():
+                if waits_for(o, ops[d], raw):
+                    s, c = token[d]
+                    want[s] = max(want.get(s, 0), c)
+            for s, c in want.items():
+                if seen.get(s, 0) < c:
+                    q.wait_ge(T.sem[s], c)
+                    seen[s] = c
+            for name, args, kw in o["calls"]:
+                if name == "send":
+                    msg, r, src, dst = args
+                    to = peer(msg, r)
+                    rid, pid, _ = topo.addr(to)
+                    mask = sum(1 << e for e in topo.engines(core, to)[:NE])
+                    g.remote_dma(real(dst), real(src), T.sem["%s%d" % (msg, r)], T.sem.sent, pid, rid, mask)
+                    nsent += NE
+                    continue
+                fn = q.dma_start if name == "dma_start" else call[name]
+                ins = fn(*[real(p) for p in args], **{k: real(v) for k, v in kw.items()})
+            if i in token:
+                ins.then_inc(T.sem[token[i][0]], 16 if o["tag"] else 1)
+    for s, c in total.items():
+        g.sync.wait_ge(T.sem[s], c)
+    g.sync.wait_ge(T.sem.sent, nsent)

@@ -9,9 +9,9 @@ V, M, RO, NA = 3072, 224, 3, 14
 HOPS = [1, 3, 6]
 VW = V + M
 W1 = 65536.0
-NV2, NV4, NV5, NV1 = 10, 7, 8, 0
-CH5, ABS5, REL4, FS_S = 4, 0, 0, 0
-YW, XW = 232, 240
+NV2, NV4, NV5, NV1 = 11, 8, 7, 0
+CH5, ABS5, REL4, FS_S, BIND_V = 4, 1, 0, 0, 0
+YW, XW, M3 = 232, 240, 336
 BF, F32, I32, U16 = "bfloat16", "float32", "int32", "uint16"
 
 SB = {
@@ -21,7 +21,8 @@ SB = {
     "qi": (4, I32), "qj": (4, I32), "col": (16, F32), "i144": (144, F32), "gm16": (128, F32), "kidx": (M, F32), "c14": (16, F32),
     "zp": (144, BF), "zn": (144, BF), "z2p": (144, BF), "z2n": (144, BF), "z8": (144, BF), "bo8": (128, F32), "bo": (128, BF),
     "i32": (128, F32), "ib": (128, BF), "nib": (128, BF), "nbi": (128, BF), "mh": (M, BF),
-    "kcb": (M, BF), "kcth": (M, F32), "rst": (M, F32), "cmask": (M, BF), "poison": (M, F32), "dd0": (M, F32), "id16": (16, F32),
+    "kcb": (M, BF), "kcth": (M, F32), "rst": (M, F32), "cmask": (M, BF), "poison": (M3, F32), "dd0": (M3, F32), "id16": (32, F32),
+    "pu3": (32, U16), "rep3": (2, U16), "cA3": (32, U16), "end3": (2, U16), "l12i": (32, I32), "k16": (16, F32), "need3": (16, F32), "frac": (16, F32), "junk": (16, F32), "bk": (16, F32), "bku": (16, U16),
     "cidx": (16, F32), "dummy": (16, F32), "t1": (16, F32), "t2": (16, F32), "t3": (16, F32), "ti": (16, I32), "tj": (16, I32),
     "cA": (16, U16), "cS": (16, U16), "pK": (16, U16), "pA": (16, U16), "pKA": (16, U16), "pAK": (16, U16), "rep4": (4, U16),
     "L": (256, F32), "W": (256, F32), "ssl": (256, F32), "lp": (256, F32), "wp": (256, F32),
@@ -35,7 +36,7 @@ SB = {
     "key2": (M, F32), "run2": (M, F32), "u2": (M, F32), "e2": (M, F32), "sel2": (M, F32),
     "key5": (M, F32), "run5": (M, F32), "u5": (M, F32), "e5": (M, F32), "sel5": (M, F32),
     "bind": (M, BF), "cnt": (M, BF), "nocc": (16, F32), "nd": (16, F32), "need2": (16, F32), "P": (16, F32), "Pu": (16, U16),
-    "row": (M, F32), "eq": (M, BF), "dsc": (M, F32), "P2": (16, F32), "P2u": (32, U16), "T2u": (32, U16),
+    "row": (M3, F32), "eq": (M3, BF), "dsc": (M3, F32), "bo32": (128, F32), "P2": (16, F32), "P2u": (32, U16), "T2u": (32, U16),
     "ji": (16, I32), "jj": (16, I32), "jt": (16, F32), "jt2": (16, F32), "ju": (16, U16), "lju": (16, U16), "tlj": (M, F32), "dlt": (M, F32),
     "wi": (16, I32), "wj": (16, I32), "wf": (16, F32), "wu": (16, U16), "tc": (M, F32), "tcol": (M, F32),
     "ep": (16, F32), "eq1": (16, F32), "l12": (32, F32), "l12u": (32, U16), "ee": (16, F32), "tl": (M, F32), "tw": (M, F32),
@@ -67,10 +68,10 @@ SEMAPHORES = ["qV", "qS", "qP", "qG", "sent"] + ["dma%d" % i for i in range(NDMA
 IO = {"xs": [128, V], "sb": [128, V], "la": [128, M], "lw": [128, M], "z0": [128, M], "b0": [8, M], "th": [8, 1],
       "yx": [128, V], "yl": [128, M], "yw": [128, M], "yz": [128, M], "yb": [8, M]}
 ALL = slice(None)
-FIGURES = [(1.04, 1.56, 3.8, 0.52, 1.0), (0.95, 1.2, 2.5, 0.5, 1.4), (1.15, 1.95, 5.0, 0.6, 0.9)]
-KEY_S = "1"
+FIGURES = [(1.04, 1.56, 3.8, 0.52, 1.3), (0.95, 1.3, 3.0, 0.5, 2.2), (1.15, 1.9, 5.0, 0.6, 1.8)]
+KEY_S = "15"
 TRIES = 600
-TILE_FIRST = False
+TILE_FIRST = True
 
 
 def a(name, lo=None, hi=None, st=None, part=ALL):
@@ -221,8 +222,8 @@ def build(CY, GA, SC, PE, LAT):
         return add("R", [], [dst], [], 0, lat * LAT, ("msg", "%s%d" % (msg, r)), after=[s])
 
     def scatter(win, lst, vals):
-        for b in range(NA - 1, -1, -1):
-            cp(ind(win, a(lst, 2 * b, 2 * b + 1)), a(vals, 16 * b, 16 * b + 16))
+        for b in range(NA // 2 - 1, -1, -1):
+            cp(ind(win, a(lst, 2 * b, 2 * b + 2)), a(vals, 32 * b, 32 * b + 32))
 
     def c1(name):
         return a(name, 0, NA)
@@ -279,11 +280,12 @@ def build(CY, GA, SC, PE, LAT):
         ts(c1(tj), c1(ti), 15, AL.bitwise_and)
 
     def lowest(pw, p14, pu, outu):
-        tt(a("row"), ind(a("iot"), pu), a("poison"), AL.add)
-        tt(a("eq"), ind(pw, c1("cA")), a("row"), AL.is_equal)
+        cp(a("pu3"), ind(pw, a("rep3", 0, 2)))
+        tt(a("row"), ind(a("iot"), a("pu3", 0, 21)), a("poison"), AL.add)
+        tt(a("eq"), ind(pw, a("cA3", 0, 21)), a("row"), AL.is_equal)
         scan(a("dsc"), a("dd0"), a("eq"), AL.mult, AL.max)
-        tt(c1("P2"), ends("dsc"), p14, AL.max)
-        cp(a(outu, 0, 2 * NA, 2), c1("P2"))
+        tt(a("P2"), ind(a("dsc"), a("end3", 0, 1)), pw, AL.max)
+        cp(c1(outu), c1("P2"))
 
     X = a("x")
     P8 = slice(0, 8)
@@ -304,7 +306,7 @@ def build(CY, GA, SC, PE, LAT):
     iota(a("kidx"), [[0, NA], [1, 16]], 0, 0)
     for i in range(4):
         iota(a("iot", VW // 4 * i, VW // 4 * (i + 1)), [[1, VW // 4]], VW // 4 * i, 0)
-    cols = ["q", "p", "g16", "g16e", "q16", "q16e", "p14", "e", "fl", "ms"]
+    cols = ["q", "p", "g16", "g16e", "q16", "q16e", "p14", "e", "fl", "ms", "pq"]
     C = {n: a("col", i, i + 1) for i, n in enumerate(cols)}
     c14 = a("i144", 0, NA)
     cp(C["q"], a("qi", 0, 1))
@@ -321,6 +323,8 @@ def build(CY, GA, SC, PE, LAT):
     ts(a("qj", 2, 3), a("qi", 1, 2), 1, AL.bitwise_and)
     ts(C["fl"], a("qj", 2, 3), 240.0, AL.mult)
     ts(C["ms"], C["p"], float(NV2), AL.is_ge)
+    act(C["pq"], C["p"], AF.Identity, bias=0.25)
+    act(c1("frac"), c14, AF.Identity, scale=1.0 / NA)
     ts(c1("cidx"), c14, 16.0, AL.mult, C["p"], AL.add)
     ts(c1("dummy"), c1("cidx"), float(V), AL.add)
     cp(c1("cA"), c14)
@@ -351,10 +355,25 @@ def build(CY, GA, SC, PE, LAT):
     ts(a("kcb"), a("kidx"), -4096.0, AL.mult)
     ts(a("rst"), a("kidx"), 0.0, AL.is_equal, -2.0 ** 30, AL.mult)
     ts(a("cmask"), a("kidx"), 0.0, AL.is_gt)
-    ts(a("poison"), a("kidx"), C["p"], AL.is_ge, 8192.0, AL.mult)
-    cp(a("dd0"), a("cmask"))
-    cp(ends("dd0"), c1("dummy"))
-    ts(a("id16"), a("kidx", 0, 16), C["p"], AL.is_equal)
+    iota(a("row"), [[0, 21], [1, 16]], 0, 0)
+    ts(a("poison"), a("row"), C["p"], AL.is_ge, 8192.0, AL.mult)
+    for b in range(NA // 2):
+        iota(a("poison", 48 * b + 16, 48 * b + 32), [[0, 16]], 0, 0)
+    iota(a("dd0"), [[0, M3]], 1, 0)
+    iota(a("dd0", 0, M3, 48), [[0, 7]], 0, 0)
+    iota(a("dd0", 16, M3, 48), [[0, 7]], 0, 0)
+    act(a("dd0", 15, M3, 48), a("dummy", 0, NA, 2))
+    act(a("dd0", 47, M3, 48), a("dummy", 1, NA, 2))
+    ts(a("wi", 0, 2), a("cidx", 0, 2), 2.0 / 3, AL.mult, -1.0 / 3, AL.add)
+    ts(a("rep3", 0, 2), a("wi", 0, 2), 15.0, AL.min)
+    ts(a("l12i", 0, 21), a("i144", 0, 21), 2.0 / 3, AL.mult)
+    cp(a("cA3", 0, 21), a("l12i", 0, 21))
+    ts(a("qj", 3, 4), a("qi", 0, 1), 1, AL.bitwise_and)
+    ts(a("nf", 1, 2), a("qj", 3, 4), 8.0, AL.mult, 15.0, AL.add)
+    ts(a("nf", 2, 3), C["p"], 24.0, AL.mult, a("nf", 1, 2), AL.add)
+    ts(a("end3", 0, 1), a("nf", 2, 3), M3 - 1.0, AL.min)
+    ts(a("id16"), a("i144", 0, 32), C["p"], AL.is_equal)
+    act(a("bo32"), a("bo"))
     ms(a("mh"), -0.5)
     ms(a("x", V, VW), 0.0)
     ms(a("tile", V, VW), 0)
@@ -471,10 +490,14 @@ def build(CY, GA, SC, PE, LAT):
         mm([(bank3("pka"), a("i32"), a("thr16"), True, False)])
         for k0, k1 in [(0, NV4)] + chunks(NV4, 16, 5):
             reduce("pka", "zn", "m2", k0, k1, False, k1 == 16)
-        act(a("bind"), bank3("pka"), AF.Sign, bias=0.5)
+        if BIND_V:
+            act(c1("need3"), c1("need2"), AF.Identity, scale=0.5)
+            ts(a("bind"), bank3("pka"), 0.0, AL.is_ge, -0.5, AL.add)
+        else:
+            act(a("bind"), bank3("pka"), AF.Sign, bias=0.5)
         scan(a("cnt"), a("cmask"), a("bind"), AL.mult, AL.add)
         x0, y0 = XW * r, (M + XW) * r
-        tt(a("xks", x0 + M, x0 + M + NA), ends("cnt"), c1("need2"), AL.is_ge)
+        tt(a("xks", x0 + M, x0 + M + NA), ends("cnt"), c1("need3" if BIND_V else "need2"), AL.is_ge)
         act(a("xks", x0, x0 + M), ind(X, c1("Pu")))
         send("k", r, a("xks", x0, x0 + XW), a("yx2", y0 + M, y0 + M + XW), 3000)
         running("1", "pkb")
@@ -484,9 +507,8 @@ def build(CY, GA, SC, PE, LAT):
         cp(a("base4", 16, 16 + NA), c1("jj"))
         tt(a("delta4", 0, NA), LB, ends("sel1"), AL.subtract)
         tt(a("delta4", 16, 16 + NA), B, a("base4", 16, 16 + NA), AL.subtract)
-        ts(c1("jt"), c1("jj"), float(M), AL.mult)
-        tt(c1("jt2"), c1("jt"), c1("cidx"), AL.add)
-        cp(c1("ju"), c1("jt2"))
+        tt(c1("jt"), c1("jj"), c1("frac"), AL.add)
+        ts(c1("ju"), c1("jt"), float(M), AL.mult, C["pq"], AL.add)
         act(a("yx2", y0, y0 + M), ind(a("rawy"), c1("ju")))
         if not last:
             act(a("base4", 32, 32 + NA), ends("sel1"))
@@ -495,18 +517,15 @@ def build(CY, GA, SC, PE, LAT):
             cp(a("tlj"), ind(a("tile"), c1("lju")))
             mm([(a("pm", 0, M), a("i32"), a("ssl", 16, 240), True, False), (a("pm", 0, M), a("ni32"), a("tlj"), False, True)])
             act(a("dlt"), a("pm", 0, M))
-            ts(c1("t1"), B, float(M), AL.mult)
-            tt(c1("t2"), c1("t1"), c1("cidx"), AL.add)
-            cp(c1("plu"), c1("t2"))
+            tt(c1("t1"), B, c1("frac"), AL.add)
+            ts(c1("plu"), c1("t1"), float(M), AL.mult, C["pq"], AL.add)
             gather_y()
         else:
             turn16("L", "t12a")
             act(a("lsl"), ind(a("t12a"), c1("pA")))
             turn16("W", "t12b")
             act(a("wsl"), ind(a("t12b"), c1("pA")))
-            act(a("mb"), ind(a("id16"), a("n4u", n0 + 16, n0 + 16 + NA)))
-            act(a("tl"), a("mb"), AF.Identity, scale=-1.0, bias=1.0)
-            tt(a("l0"), a("lsl"), a("tl"), AL.mult)
+            tt(a("tw"), ind(a("iot"), LBu), a("wsl"), AL.subtract)
         fr = kb("fr", r)
         for ks in pairs(NV5, 16):
             act(kb("raws", ks[0], len(ks)), ind(X, sl("Wu", ks[0], len(ks))))
@@ -535,7 +554,7 @@ def build(CY, GA, SC, PE, LAT):
         cp(a("n4u", n1, n1 + 64), a("n4", n1, n1 + 64))
         if not last:
             mm([(a("pm", 0, NA), a("bo"), kr14, True, True)])
-            add("V", [("tensor_reduce", (a("nf", 0, 1), a("pm", 0, NA), AxisListType.X, AL.add), {})], [a("nf", 0, 1)], [a("pm", 0, NA)], 100)
+            add("S", [("activation", (c1("junk"), a("pm", 0, NA), AF.Identity), {"accum_out": a("nf", 0, 1)})], [c1("junk"), a("nf", 0, 1)], [a("pm", 0, NA)], 150)
             cp(a("ni", 0, 1), a("nf", 0, 1))
             ts(a("nj", 0, 1), a("ni", 0, 1), 1, AL.bitwise_and)
             ts(a("ys", YW * (r + 1) + M, YW * (r + 1) + M + 1), a("nj", 0, 1), 2.0, AL.mult, -8.0, AL.add)
@@ -546,16 +565,20 @@ def build(CY, GA, SC, PE, LAT):
         act(a("z"), a("zt"), AF.Identity, scale=0.5, bias=-1.5 * 2.0 ** 23)
         running("5", "pkb")
         slot("5", "wi", "wj")
-        cp(c1("wu"), c1("wj"))
         if not last:
+            cp(c1("wu"), c1("wj"))
             tt(a("tc"), ind(a("id16"), c1("wu")), a("dlt"), AL.mult)
             mm([(a("pm", 0, M), a("i32"), a("tlj"), True, True)])
             tt(a("tcol"), a("tc"), a("pm", 0, M), AL.add)
             scatter(a("tile"), "T2u", "tcol")
-        choose("5", "pkb", a("W", 16, 240))
-        tt(c1("eq1"), LB, ends("sel5"), AL.subtract)
-        tt(c1("ep"), c1("eq1"), kr14, AL.mult)
         if not last:
+            cp(c1("wf"), c1("wj"))
+            tt(a("ohw"), ind(a("wf"), c1("cA")), a("kidx"), AL.is_equal)
+            mm([(a("pf", 0, M), a("i32"), a("W", 16, 240), True, True)])
+            tt(a("e5"), a("pf", 0, M), a("ohw"), AL.mult)
+            scan(a("sel5"), a("cmask"), a("e5"), AL.mult, AL.add)
+            tt(c1("eq1"), LB, ends("sel5"), AL.subtract)
+            tt(c1("ep"), c1("eq1"), kr14, AL.mult)
             tt(c1("ee"), c1("ep"), c1("eq1"), AL.subtract)
             tt(a("l12", 0, NA), ends("sel5"), c1("ep"), AL.add)
             cp(a("l12u", 0, NA), a("l12", 0, NA))
@@ -566,22 +589,26 @@ def build(CY, GA, SC, PE, LAT):
             act(a("L", 16, 240), a("pm", 0, M))
             if r < RO - 2:
                 cp(a("Lu"), ind(a("L", 16, 240), c1("pAK")))
-            cp(c1("wf"), c1("wj"))
-            tt(a("ohw"), ind(a("wf"), c1("cA")), a("kidx"), AL.is_equal)
             tt(a("tw"), ind(a("ee"), c1("cA")), a("ohw"), AL.mult)
             mm([(a("pm", 0, M), a("i32"), a("W", 16, 240), True, False), (a("pm", 0, M), a("ni32"), a("tw"), False, True)])
             act(a("W", 16, 240), a("pm", 0, M))
             cp(a("Wu"), ind(a("W", 16, 240), c1("pAK")))
             tt(a("oh"), ind(a("n4", n1 + 16, n1 + 32), c1("cA")), a("kidx"), AL.is_equal)
         else:
-            tt(a("l12", 0, NA), ends("sel5"), c1("ep"), AL.add)
-            tt(a("l12", 16, 16 + NA), LB, c1("ep"), AL.subtract)
-            cp(a("l12u", 0, NA), a("l12", 0, NA))
-            cp(a("l12u", 16, 16 + NA), a("l12", 16, 16 + NA))
-            tt(a("tw"), ind(a("iot"), a("l12u", 16, 16 + NA)), a("wsl"), AL.subtract)
+            ts(c1("k16"), kr14, 16.0, AL.mult)
+            tt(c1("bk"), B, c1("k16"), AL.max)
+            cp(c1("bku"), c1("bk"))
+            act(a("mb"), ind(a("id16"), c1("bku")))
+            act(a("tl"), a("mb"), AF.Identity, scale=-1.0, bias=1.0)
+            tt(a("l0"), a("lsl"), a("tl"), AL.mult)
+            tt(c1("wf"), c1("wj"), c1("k16"), AL.max)
+            cp(c1("wu"), c1("wf"))
+            tt(a("e5"), ind(a("id16"), c1("wu")), a("wsl"), AL.mult)
+            mm([(a("pf", 0, M), a("bo32"), a("e5"), True, True)])
             tt(a("tc"), ind(a("id16"), c1("wu")), a("tw"), AL.mult)
-            tt(a("ow"), a("tc"), a("wsl"), AL.add)
-            tt(a("tl"), ind(a("iot"), a("l12u", 0, NA)), a("mb"), AL.mult)
+            mm([(a("pm", 0, M), a("i32"), a("tc"), True, False), (a("pm", 0, M), a("i32"), a("wsl"), False, True)])
+            act(a("ow"), a("pm", 0, M))
+            tt(a("tl"), a("pf", 0, M), a("mb"), AL.mult)
             tt(a("ol"), a("tl"), a("l0"), AL.add)
             act(a("ob"), ind(a("iot"), a("n4u", n1 + 16, n1 + 16 + NA)))
             dma("Y", whole("yb"), a("ob", part=slice(0, 128, 16)), 2000)
@@ -715,7 +742,7 @@ def arrange(plans):
     return order, [span(seq, k)[0] for k in range(len(plans))]
 
 
-HOLD, SAME, CROSS = 0.5, 60, 120
+HOLD, SAME, CROSS = 0.5, 110, 200
 PLAN = {}
 NE = 8
 

@@ -35,8 +35,8 @@ SB = {
     "key1": (M, F32), "run1": (M, F32), "u1": (M, F32), "e1": (M, F32), "sel1": (M, F32),
     "key2": (M, F32), "run2": (M, F32), "u2": (M, F32), "e2": (M, F32), "sel2": (M, F32),
     "key5": (M, F32), "run5": (M, F32), "u5": (M, F32), "e5": (M, F32), "sel5": (M, F32),
-    "bind": (M, BF), "cnt": (M, BF), "nocc": (16, F32), "nd": (16, F32), "need2": (16, F32), "P": (16, F32), "Pu": (16, U16),
-    "row": (M3, F32), "eq": (M3, BF), "dsc": (M3, F32), "bo32": (128, F32), "P2": (16, F32), "P2u": (32, U16), "T2u": (32, U16),
+    "bind": (M, BF), "cnt": (M, BF), "nocc": (16, F32), "nd": (16, F32), "need2": (16, F32), "P": (32, F32), "Pu": (16, U16),
+    "row": (M3, F32), "eq": (M3, BF), "dsc": (384, F32), "bo32": (128, F32), "P2": (32, F32), "P2u": (32, U16), "T2u": (32, U16),
     "ji": (16, I32), "jj": (16, I32), "jt": (16, F32), "jt2": (16, F32), "ju": (16, U16), "lju": (16, U16), "tlj": (M, F32), "dlt": (M, F32),
     "wi": (16, I32), "wj": (16, I32), "wf": (16, F32), "wu": (16, U16), "tc": (M, F32), "tcol": (M, F32),
     "ep": (16, F32), "eq1": (16, F32), "l12": (32, F32), "l12u": (32, U16), "ee": (16, F32), "tl": (M, F32), "tw": (M, F32),
@@ -68,9 +68,11 @@ SEMAPHORES = ["qV", "qS", "qP", "qG", "sent"] + ["dma%d" % i for i in range(NDMA
 IO = {"xs": [128, V], "sb": [128, V], "la": [128, M], "lw": [128, M], "z0": [128, M], "b0": [8, M], "th": [8, 1],
       "yx": [128, V], "yl": [128, M], "yw": [128, M], "yz": [128, M], "yb": [8, M]}
 ALL = slice(None)
-FIGURES = [(1.04, 1.56, 3.8, 0.52, 1.3), (0.95, 1.3, 3.0, 0.5, 2.2), (1.15, 1.9, 5.0, 0.6, 1.8)]
+FIGURES = [(0.9, 1.56, 3.8, 0.45, 1.2), (0.85, 1.3, 3.0, 0.43, 1.5), (1.15, 1.8, 4.5, 0.58, 1.8)]
+HALVES = [(8, NA), (0, 8)]
+SPLIT = "25cx"
 KEY_S = "15"
-TRIES = 600
+TRIES = 900
 TILE_FIRST = True
 
 
@@ -266,26 +268,44 @@ def build(CY, GA, SC, PE, LAT):
             (cp if k0 < NV1 else act)(a("rawy", M * k0, M * k1), ind(a("x"), a("Lu", NA * k0, NA * k1)))
 
     def running(n, bank):
-        (act if n in KEY_S else cp)(a("key" + n), bank3(bank))
-        scan(a("run" + n), a("rst"), a("key" + n), AL.add, AL.max)
+        for h in parts(n):
+            (act if n in KEY_S else cp)(w16("key" + n, h), a3(bank, slice(*h), ALL))
+        for h in parts(n):
+            scan(w16("run" + n, h), w16("rst", h), w16("key" + n, h), AL.add, AL.max)
+
+    def parts(n):
+        return HALVES if n in SPLIT else [(0, NA)]
+
+    def w16(name, h):
+        return a(name, 16 * h[0], 16 * h[1])
+
+    def e16(name, h):
+        return a(name, 16 * h[0] + 15, 16 * h[1], 16)
 
     def choose(n, bank, val):
         mm([(a("pf", 0, M), a("i32"), val, True, True)])
-        tt(a("u" + n), a("run" + n), bank3(bank), AL.subtract)
-        tt(a("e" + n), a("pf", 0, M), a("u" + n), AL.subtract)
-        scan(a("sel" + n), a("u" + n), a("e" + n), AL.min, AL.max)
+        for h in parts(n):
+            tt(w16("u" + n, h), w16("run" + n, h), a3(bank, slice(*h), ALL), AL.subtract)
+        for h in parts(n):
+            tt(w16("e" + n, h), w16("pf", h), w16("u" + n, h), AL.subtract)
+        for h in parts(n):
+            scan(w16("sel" + n, h), w16("u" + n, h), w16("e" + n, h), AL.min, AL.max)
 
     def slot(n, ti, tj):
-        ts(c1(ti), ends("run" + n), -1.0 / 4096, AL.mult, 131072.0, AL.add)
-        ts(c1(tj), c1(ti), 15, AL.bitwise_and)
+        for h in parts(n):
+            ts(a(ti, *h), e16("run" + n, h), -1.0 / 4096, AL.mult, 131072.0, AL.add)
+            ts(a(tj, *h), a(ti, *h), 15, AL.bitwise_and)
 
     def lowest(pw, p14, pu, outu):
-        cp(a("pu3"), ind(pw, a("rep3", 0, 2)))
-        tt(a("row"), ind(a("iot"), a("pu3", 0, 21)), a("poison"), AL.add)
-        tt(a("eq"), ind(pw, a("cA3", 0, 21)), a("row"), AL.is_equal)
-        scan(a("dsc"), a("dd0"), a("eq"), AL.mult, AL.max)
-        tt(a("P2"), ind(a("dsc"), a("end3", 0, 1)), pw, AL.max)
-        cp(c1(outu), c1("P2"))
+        for a0, a1 in HALVES:
+            n3, c0, c2 = 3 * (a1 - a0) // 2, 24 * a0, 24 * a1
+            win = a(pw, p14 + a0, p14 + a0 + 8)
+            cp(a("pu3", 2 * a0, 2 * a0 + 16), ind(win, a("rep3", 0, 1)))
+            tt(a("row", c0, c2), ind(a("iot"), a("pu3", 2 * a0, 2 * a0 + n3)), a("poison", c0, c2), AL.add)
+            tt(a("eq", c0, c2), ind(win, a("cA3", 0, n3)), a("row", c0, c2), AL.is_equal)
+            scan(a("dsc", c0, c2), a("dd0", c0, c2), a("eq", c0, c2), AL.mult, AL.max)
+            tt(a("P2", 2 * a0, 2 * a0 + 16), ind(a("dsc", c0, c0 + 192), a("end3", 0, 1)), a(pw, p14 + a0, p14 + a0 + 16), AL.max)
+            cp(a(outu, a0, a1), a("P2", 2 * a0, a0 + a1))
 
     X = a("x")
     P8 = slice(0, 8)
@@ -364,14 +384,15 @@ def build(CY, GA, SC, PE, LAT):
     iota(a("dd0", 16, M3, 48), [[0, 7]], 0, 0)
     act(a("dd0", 15, M3, 48), a("dummy", 0, NA, 2))
     act(a("dd0", 47, M3, 48), a("dummy", 1, NA, 2))
-    ts(a("wi", 0, 2), a("cidx", 0, 2), 2.0 / 3, AL.mult, -1.0 / 3, AL.add)
-    ts(a("rep3", 0, 2), a("wi", 0, 2), 15.0, AL.min)
+    ts(a("wi", 0, 1), C["p"], 2.0 / 3, AL.mult, -1.0 / 3, AL.add)
+    ts(a("rep3", 0, 1), a("wi", 0, 1), 7.0, AL.min)
+    iota(a("dsc", M3, 384), [[0, 384 - M3]], 0, 0)
     ts(a("l12i", 0, 21), a("i144", 0, 21), 2.0 / 3, AL.mult)
     cp(a("cA3", 0, 21), a("l12i", 0, 21))
     ts(a("qj", 3, 4), a("qi", 0, 1), 1, AL.bitwise_and)
     ts(a("nf", 1, 2), a("qj", 3, 4), 8.0, AL.mult, 15.0, AL.add)
     ts(a("nf", 2, 3), C["p"], 24.0, AL.mult, a("nf", 1, 2), AL.add)
-    ts(a("end3", 0, 1), a("nf", 2, 3), M3 - 1.0, AL.min)
+    ts(a("end3", 0, 1), a("nf", 2, 3), 191.0, AL.min)
     ts(a("id16"), a("i144", 0, 32), C["p"], AL.is_equal)
     act(a("bo32"), a("bo"))
     ms(a("mh"), -0.5)
@@ -458,18 +479,21 @@ def build(CY, GA, SC, PE, LAT):
         cp(a("sf"), kb("sr", r))
         act(a("sa"), ind(a("sf"), c1("pKA")))
         running("2", "pka")
-        act(a("bind"), a("key2"), AF.Sign, bias=61440.5)
         choose("2", "pka", a("sa"))
-        scan(a("cnt"), a("cmask"), a("bind"), AL.mult, AL.add)
-        ts(c1("nocc"), ends("cnt"), need, AL.is_lt)
-        tt(c1("nd"), c1("nocc"), c1("dummy"), AL.mult)
-        tt(c1("P"), ends("sel2"), c1("nd"), AL.max)
-        cp(c1("Pu"), c1("P"))
+        for h in parts("c"):
+            act(w16("bind", h), w16("key2", h), AF.Sign, bias=61440.5)
+            scan(w16("cnt", h), w16("cmask", h), w16("bind", h), AL.mult, AL.add)
+            ts(a("nocc", *h), e16("cnt", h), need, AL.is_lt)
+            tt(a("nd", *h), a("nocc", *h), a("dummy", *h), AL.mult)
+        for h in parts("2"):
+            tt(a("P", *h), e16("sel2", h), a("nd", *h), AL.max)
         ts(c1("need2"), c1("nocc"), 99.0, AL.mult, need, AL.add)
-        act(a("xsel"), ind(X, c1("Pu")))
-        mm([(a("pm", 0, M), a("ib"), a("xsel"), True, False), (a("pm", 0, M), a("nib"), a("qq"), False, True)])
-        act(a("new"), a("pm", 0, M), AF.Relu, bias=160.0)
-        lowest(a("P"), c1("P"), c1("Pu"), "P2u")
+        for h, bank in zip(parts("x"), ("pm", "pf")):
+            cp(a("Pu", *h), a("P", *h))
+            act(w16("xsel", h), ind(X, a("Pu", *h)))
+            mm([(w16(bank, h), a("ib"), w16("xsel", h), True, False), (w16(bank, h), a("nib"), w16("qq", h), False, True)])
+            act(w16("new", h), w16(bank, h), AF.Relu, bias=160.0)
+        lowest("P", 0, None, "P2u")
         scatter(X, "P2u", "new")
         if last:
             dma("Y", whole("yx"), a("x", 0, V), 4500)
@@ -531,8 +555,16 @@ def build(CY, GA, SC, PE, LAT):
             act(kb("raws", ks[0], len(ks)), ind(X, sl("Wu", ks[0], len(ks))))
         for k in range(NV5):
             tt(a3("rawv", ALL, k), ind(X, sl("Wu", k)), fr, AL.subtract)
-        for n, ks in enumerate(pairs(NV5, 16)):
-            diff(ks, lambda k: kb("raws", k), lambda k: fr, AF.Abs, "m5", 2 * (n // 2 % 2))
+        held = list(zip(["pd2", "pd3", "pd0", "pd1"] * 2, pairs(NV5, 16)))
+        pre = lambda bank, ks: mm([(a(bank, 0, len(ks) * M), a("ib"), kb("raws", ks[0], len(ks)), True, False)])
+        for bank, ks in held[:4]:
+            pre(bank, ks)
+        for n, (bank, ks) in enumerate(held):
+            if n >= 4:
+                pre(bank, ks)
+            mm([(a(bank, i * M, (i + 1) * M), a("nib"), fr, False, i == len(ks) - 1) for i in range(len(ks))])
+            for i, k in enumerate(ks):
+                act(a3("m5", ALL, k), a(bank, i * M, (i + 1) * M), AF.Abs)
         mm([(bank3("pkb"), a("ib"), a("kcb"), True, False)])
         cv, cs = chunks(0, NV5, CH5), chunks(NV5, 16, 5)
         for n, (k0, k1) in enumerate(cv):
@@ -558,7 +590,7 @@ def build(CY, GA, SC, PE, LAT):
             cp(a("ni", 0, 1), a("nf", 0, 1))
             ts(a("nj", 0, 1), a("ni", 0, 1), 1, AL.bitwise_and)
             ts(a("ys", YW * (r + 1) + M, YW * (r + 1) + M + 1), a("nj", 0, 1), 2.0, AL.mult, -8.0, AL.add)
-            lowest(a("n4", n1 + 32, n1 + 48), a("n4", n1 + 32, n1 + 32 + NA), a("n4u", n1 + 32, n1 + 32 + NA), "T2u")
+            lowest("n4", n1 + 32, None, "T2u")
         act(a("zsel"), ind(a("yx2", y0, y0 + 2 * M), a("n4u", n1 + 48, n1 + 48 + NA)))
         mm([(a("pm", 0, M), a("ib"), i, n == 0, n == 2) for n, i in enumerate((a("mh"), a("z"), a("zsel")))])
         act(a("zt"), a("pm", 0, M), AF.Identity, bias=1.5 * 2.0 ** 24)
@@ -566,10 +598,11 @@ def build(CY, GA, SC, PE, LAT):
         running("5", "pkb")
         slot("5", "wi", "wj")
         if not last:
-            cp(c1("wu"), c1("wj"))
-            tt(a("tc"), ind(a("id16"), c1("wu")), a("dlt"), AL.mult)
             mm([(a("pm", 0, M), a("i32"), a("tlj"), True, True)])
-            tt(a("tcol"), a("tc"), a("pm", 0, M), AL.add)
+            for h in parts("5"):
+                cp(a("wu", *h), a("wj", *h))
+                tt(w16("tc", h), ind(a("id16"), a("wu", *h)), w16("dlt", h), AL.mult)
+                tt(w16("tcol", h), w16("tc", h), w16("pm", h), AL.add)
             scatter(a("tile"), "T2u", "tcol")
         if not last:
             cp(c1("wf"), c1("wj"))
@@ -601,15 +634,16 @@ def build(CY, GA, SC, PE, LAT):
             act(a("mb"), ind(a("id16"), c1("bku")))
             act(a("tl"), a("mb"), AF.Identity, scale=-1.0, bias=1.0)
             tt(a("l0"), a("lsl"), a("tl"), AL.mult)
-            tt(c1("wf"), c1("wj"), c1("k16"), AL.max)
-            cp(c1("wu"), c1("wf"))
+            mm([(a("pd0", 0, M), a("i32"), a("l0"), True, True)])
+            mm([(a("pd1", 0, M), a("bo32"), a("mb"), True, True), (a("pd1", M, 2 * M), a("i32"), a("wsl"), True, True)])
+            tt(a("dlt"), a("pd1", 0, M), a("tw"), AL.mult)
+            cp(c1("wu"), c1("wj"))
             tt(a("e5"), ind(a("id16"), c1("wu")), a("wsl"), AL.mult)
             mm([(a("pf", 0, M), a("bo32"), a("e5"), True, True)])
-            tt(a("tc"), ind(a("id16"), c1("wu")), a("tw"), AL.mult)
-            mm([(a("pm", 0, M), a("i32"), a("tc"), True, False), (a("pm", 0, M), a("i32"), a("wsl"), False, True)])
-            act(a("ow"), a("pm", 0, M))
+            tt(a("tc"), ind(a("id16"), c1("wu")), a("dlt"), AL.mult)
             tt(a("tl"), a("pf", 0, M), a("mb"), AL.mult)
-            tt(a("ol"), a("tl"), a("l0"), AL.add)
+            tt(a("ow"), a("tc"), a("pd1", M, 2 * M), AL.add)
+            tt(a("ol"), a("tl"), a("pd0", 0, M), AL.add)
             act(a("ob"), ind(a("iot"), a("n4u", n1 + 16, n1 + 16 + NA)))
             dma("Y", whole("yb"), a("ob", part=slice(0, 128, 16)), 2000)
             dma("Y", whole("yz"), a("z"), 2200)
@@ -742,7 +776,7 @@ def arrange(plans):
     return order, [span(seq, k)[0] for k in range(len(plans))]
 
 
-HOLD, SAME, CROSS = 0.5, 110, 200
+HOLD, SAME, CROSS = 0.5, 170, 220
 PLAN = {}
 NE = 8
 

@@ -4,44 +4,47 @@ from concourse.mybir import dt, AluOpType, AxisListType, ActivationFunctionType
 
 AL = AluOpType
 AF = ActivationFunctionType
-s_ = np.s_
 V, M, RO, NA = 3072, 224, 3, 14
 HOPS = [1, 3, 6]
-VW = V + M
+VW = V + 16 + M
+VX = VW + M
+M7 = 17 * NA
 W1 = 65536.0
-NV2, NV4, NV5, NV1 = 11, 8, 7, 0
-CH5, ABS5, REL4, FS_S, BIND_V = 4, 1, 0, 0, 0
-YW, XW, M3 = 232, 240, 336
+NV2, NV4, NV5, NV1 = 12, 7, 8, 0
+ABS5, REL4 = 1, 0
+RC, RC1 = 5, 9
+NS, CH1 = 7, 4
+DLT_V = False
+EW, M3 = 240, 336
+XC = 2
 BF, F32, I32, U16 = "bfloat16", "float32", "int32", "uint16"
 
 SB = {
-    "x": (VW, BF), "tile": (VW, I32), "iot": (VW, F32),
-    "lai": (M, I32), "lwi": (M, I32), "bi": (M, I32), "thi": (4, I32), "z": (M, BF),
-    "bb": (M, BF), "thf": (4, F32), "thw": (4, F32),
-    "qi": (4, I32), "qj": (4, I32), "col": (16, F32), "i144": (144, F32), "gm16": (128, F32), "kidx": (M, F32), "c14": (16, F32),
-    "zp": (144, BF), "zn": (144, BF), "z2p": (144, BF), "z2n": (144, BF), "z8": (144, BF), "bo8": (128, F32), "bo": (128, BF),
-    "i32": (128, F32), "ib": (128, BF), "nib": (128, BF), "nbi": (128, BF), "mh": (M, BF),
-    "kcb": (M, BF), "kcth": (M, F32), "rst": (M, F32), "cmask": (M, BF), "poison": (M3, F32), "dd0": (M3, F32), "id16": (32, F32),
-    "pu3": (32, U16), "rep3": (2, U16), "cA3": (32, U16), "end3": (2, U16), "l12i": (32, I32), "k16": (16, F32), "need3": (16, F32), "frac": (16, F32), "junk": (16, F32), "bk": (16, F32), "bku": (16, U16),
-    "cidx": (16, F32), "dummy": (16, F32), "t1": (16, F32), "t2": (16, F32), "t3": (16, F32), "ti": (16, I32), "tj": (16, I32),
-    "cA": (16, U16), "cS": (16, U16), "pK": (16, U16), "pA": (16, U16), "pKA": (16, U16), "pAK": (16, U16), "rep4": (4, U16),
+    "x": (VW, BF), "xp0": (VX, BF), "xp1": (VX, BF), "xp2": (VX, BF), "tile": (VW, I32), "iot": (VW, F32),
+    "lai": (M, I32), "lwi": (M, I32), "bi": (M, I32), "z": (M, BF), "bb": (M, BF), "thf": (4, F32),
+    "qi": (4, I32), "qj": (4, I32), "col": (16, F32), "i144": (144, F32), "gm16": (128, F32), "kidx": (M, F32), "k17": (M7, F32),
+    "zp": (144, BF), "zn": (144, BF), "z2n": (144, BF), "z8": (144, BF), "bo8": (128, F32), "bo2": (128, BF), "bo32": (128, F32),
+    "i32": (128, F32), "ni32": (128, F32), "ib32": (128, F32), "ib": (128, BF), "nib": (128, BF), "nbi": (128, BF), "nq": (128, BF), "mh": (M, BF),
+    "kcb": (M, BF), "kc7": (M7, BF), "rst": (M, F32), "rs7": (M7, F32), "cmask": (M, BF), "poison": (M3, F32), "dd0": (M3, F32), "id16": (32, F32),
+    "pu3": (32, U16), "rep3": (2, U16), "cA3": (32, U16), "end3": (2, U16), "end7": (4, U16), "l12i": (32, I32), "k16": (16, F32), "bk": (16, F32), "bku": (16, U16),
+    "cidx": (16, F32), "t1": (16, F32), "t2": (16, F32), "t3": (16, F32), "ti": (16, I32), "tj": (16, I32),
+    "cA": (16, U16), "cS": (16, U16), "pK": (16, U16), "pA": (16, U16), "pAK": (16, U16), "rep4": (4, U16),
     "L": (256, F32), "W": (256, F32), "ssl": (256, F32), "lp": (256, F32), "wp": (256, F32),
-    "t12a": (480, F32), "t12b": (480, F32), "t12c": (480, F32), "Lu": (M, U16), "Wu": (M, U16), "oh": (M, BF), "ohw": (M, BF),
-    "n4": (64 * (RO + 1), F32), "n4u": (64 * (RO + 1), U16), "n4t": (64, F32), "base4": (64, F32), "delta4": (64, F32),
-    "ys": (YW * RO, BF), "yr": (YW * RO, BF), "ss": (M * RO, U16), "sr": (M * RO, U16), "xks": (XW * RO, BF), "yx2": ((M + XW) * RO, BF),
-    "fs": (M * RO, BF), "fr": (M * RO, BF),
+    "t12a": (480, F32), "t12b": (480, F32), "t12c": (480, F32), "Lu": (M, U16), "Wu": (M, U16), "oh": (M * RO, BF), "ohw": (M, BF),
+    "n4": (64 * (RO + 1), F32), "n4u": (64 * (RO + 1), U16), "n4t": (64, F32), "base4": (64, I32), "delta4": (64, F32), "DP": (48, F32),
+    "kp": (16 * (RO + 1), BF), "su": (M, U16), "ed": (EW * RO, U16), "eo": (EW * RO, U16), "xq": (V, BF),
     "rawy": (16 * M, BF), "raws": (16 * M, BF), "D": (16 * M, BF), "D0": (16 * M, BF), "Do": (16 * M, BF),
-    "sf": (M, F32), "sa": (M, F32), "ywin": (16, F32), "add2": (M, F32), "thr16": (M, F32), "qq": (M, BF), "xsel": (M, BF), "new": (M, BF),
-    "key1": (M, F32), "run1": (M, F32), "u1": (M, F32), "e1": (M, F32), "sel1": (M, F32),
+    "sa": (M, F32), "ywin": (16, F32), "thr16": (M, F32), "xsel": (M, BF),
+    "key1": (M7, F32), "run1": (M7, F32), "u1": (M7, F32), "e1": (M7, F32), "sel1": (M7 + 2, F32),
     "key2": (M, F32), "run2": (M, F32), "u2": (M, F32), "e2": (M, F32), "sel2": (M, F32),
-    "key5": (M, F32), "run5": (M, F32), "u5": (M, F32), "e5": (M, F32), "sel5": (M, F32),
-    "bind": (M, BF), "cnt": (M, BF), "nocc": (16, F32), "nd": (16, F32), "need2": (16, F32), "P": (32, F32), "Pu": (16, U16),
-    "row": (M3, F32), "eq": (M3, BF), "dsc": (384, F32), "bo32": (128, F32), "P2": (32, F32), "P2u": (32, U16), "T2u": (32, U16),
-    "ji": (16, I32), "jj": (16, I32), "jt": (16, F32), "jt2": (16, F32), "ju": (16, U16), "lju": (16, U16), "tlj": (M, F32), "dlt": (M, F32),
-    "wi": (16, I32), "wj": (16, I32), "wf": (16, F32), "wu": (16, U16), "tc": (M, F32), "tcol": (M, F32),
-    "ep": (16, F32), "eq1": (16, F32), "l12": (32, F32), "l12u": (32, U16), "ee": (16, F32), "tl": (M, F32), "tw": (M, F32),
-    "nf": (4, F32), "ni": (4, I32), "nj": (4, I32), "zsel": (M, BF), "zt": (M, F32),
-    "ni32": (128, F32), "ynew": (M, BF), "plu": (16, U16), "mb": (M, F32), "l0": (M, F32), "wsl": (M, F32), "lsl": (M, F32), "ol": (M, F32), "ow": (M, F32), "ob": (M, F32),
+    "key5": (M, F32), "run5": (M, F32), "e5": (M, F32), "sel5": (M, F32),
+    "bind": (M, BF), "cnt": (M, BF), "nocc": (16, F32), "nd": (16, F32), "need": (4, F32), "need2": (16, F32), "Pu": (16, U16),
+    "row": (M3, F32), "eq": (M3, BF), "dsc": (384, F32), "P2": (32, F32), "T2u": (32, U16),
+    "ji": (16, I32), "jt": (16, F32), "jt2": (16, F32), "lju": (16, U16), "tlj": (M, F32), "dlt": (M, F32),
+    "wi": (16, I32), "wj": (16, I32), "wf": (16, F32), "wu": (16, U16), "wwu": (16, U16), "tc": (M, F32), "tcol": (M, F32),
+    "ex": (16, F32), "eq1": (16, F32), "ee": (16, F32), "tl": (M, F32), "tw": (M, F32),
+    "nf": (4, F32), "ni": (4, I32), "zsel": (M, BF), "zt": (M, F32),
+    "ynew": (M, BF), "mb": (M, F32), "l0": (M, F32), "wsl": (M, F32), "lsl": (M, F32), "ol": (M, F32), "ow": (M, F32), "ob": (M, F32),
 }
 SHARED = {}
 SCRATCH = {}
@@ -56,24 +59,32 @@ for _n, (_w, _d) in SB.items():
 for _d, _o in _fill.items():
     SCRATCH["small_" + _d] = ("sbuf", [128, _o], _d)
 SCRATCH["thi2"] = ("sbuf", [128, 4], I32)
-for _n in ("m1", "m2", "m5", "rawv"):
+SCRATCH["thb"] = ("sbuf", [128, 4], F32)
+SCRATCH["thr"] = ("sbuf", [128, 4 * RO], F32)
+for _n in ("m2", "m5", "rawv"):
     SCRATCH[_n] = ("sbuf", [128, M, 16], BF)
-for _n in ("pka", "pkb"):
-    SCRATCH[_n] = ("psum", [128, 32, 16], F32)
-for _n in ("pd0", "pd1", "pd2", "pd3", "pm", "pf"):
+SCRATCH["m1"] = ("sbuf", [128, M, 17], BF)
+for _n in ("pkb", "pf"):
+    SCRATCH[_n] = ("psum", [128, 30, 17], F32)
+for _n in ("pd0", "pd1", "pd2", "pd3", "pm", "pka"):
     SCRATCH[_n] = ("psum", [128, 512], F32)
-MSG = ["y", "s", "f", "k"]
 NDMA = 16
-SEMAPHORES = ["qV", "qS", "qP", "qG", "sent"] + ["dma%d" % i for i in range(NDMA)] + ["%s%d" % (m, r) for m in MSG for r in range(RO)]
+RELAYED = ["xc%d" % r for r in range(RO - 1)]
+ARRIVE = ["th"] + ["xa%d" % i for i in range(XC)] + ["eo%d" % r for r in range(RO)] + ["xb%d" % r for r in range(RO - 1)] + RELAYED
+LEAVE = ["out_xa%d" % i for i in range(XC)]
+SEMAPHORES = ["qV", "qS", "qP", "qG", "sent"] + ["dma%d" % i for i in range(NDMA)] + ARRIVE + LEAVE + ["held_" + k for k in RELAYED]
 IO = {"xs": [128, V], "sb": [128, V], "la": [128, M], "lw": [128, M], "z0": [128, M], "b0": [8, M], "th": [8, 1],
       "yx": [128, V], "yl": [128, M], "yw": [128, M], "yz": [128, M], "yb": [8, M]}
 ALL = slice(None)
 FIGURES = [(0.9, 1.56, 3.8, 0.45, 1.2), (0.85, 1.3, 3.0, 0.43, 1.5), (1.15, 1.8, 4.5, 0.58, 1.8)]
 HALVES = [(8, NA), (0, 8)]
-SPLIT = "25cx"
-KEY_S = "15"
-TRIES = 900
-TILE_FIRST = True
+SPLIT = ""
+SETS = {6: ([(0, 4), (1, 8)], [(5, 8), (2, 4), (3, 4)]), 8: ([(0, 4), (1, 4)], [(2, 4), (3, 4)]), 10: ([(0, 4), (1, 4), (2, 8)], [(6, 8), (3, 4)]),
+        12: ([(0, 4), (1, 4), (2, 4)], [(3, 4)]), 16: ([(0, 4), (1, 4), (2, 4), (3, 4)], [])}
+KEY_S, KEY_P = "1", "25"
+THR_PE = False
+B4 = "pkb"
+TRIES, MOVES, HEAT, ANY, EARLY = 300, 50000, 40.0, 0.2, 1.0
 
 
 def a(name, lo=None, hi=None, st=None, part=ALL):
@@ -91,21 +102,27 @@ def ind(win, off):
     return ("*", win, off)
 
 
+CELLS = {}
+
+
+def cells(name):
+    if name not in CELLS:
+        shape = IO[name][1:] if name in IO else SCRATCH[name][1][1:]
+        CELLS[name] = np.arange(int(np.prod(shape))).reshape(shape)
+    return CELLS[name]
+
+
 def foot(ap):
     name, idx = ap
-    shape = IO[name][1:] if name in IO else SCRATCH[name][1][1:]
-    n = int(np.prod(shape))
     if name not in IO and SCRATCH[name][0] == "psum":
-        return np.arange(n)
-    return np.arange(n).reshape(shape)[idx[1:]].reshape(-1)
+        return cells(name).reshape(-1)
+    return cells(name)[idx[1:]].reshape(-1)
 
 
 def count(ap):
     if ap[0] == "*":
         return 16 * count(ap[2])
-    name, idx = ap
-    shape = IO[name][1:] if name in IO else SCRATCH[name][1][1:]
-    return int(np.empty(shape, np.int8)[idx[1:]].size)
+    return int(cells(ap[0])[ap[1][1:]].size)
 
 
 def is_ap(v):
@@ -122,9 +139,9 @@ def narrow(ap):
 
 def build(CY, GA, SC, PE, LAT):
     ops = []
-    lastw, readers = {}, {}
+    lastw, readers, banks = {}, {}, {}
 
-    def add(eng, calls, outs, ins, cost, lat=0.0, tag=None, after=()):
+    def add(eng, calls, outs, ins, cost, lat=0.0, tag=None, after=(), adds=False):
         me = len(ops)
         deps = {d: True for d in after}
         rd, wr = [], []
@@ -136,8 +153,15 @@ def build(CY, GA, SC, PE, LAT):
                 wr.append(p[1]); rd.append(p[2])
             else:
                 wr.append(p)
-        excl = [p for p in rd if psum(p)]
+        group = None
+        for b in {p[0] for p in rd + wr if psum(p)}:
+            base, more = banks.get(b, ([], []))
+            for d in base + ([] if adds else more):
+                deps.setdefault(d, False)
+            banks[b] = (base, more + [me]) if adds else ([me], [])
+            group = base[0] if adds else None
         rd = [p for p in rd if not psum(p)]
+        wr = [p for p in wr if not psum(p)]
         for p in rd:
             f = foot(p)
             lw = lastw.get(p[0])
@@ -145,13 +169,13 @@ def build(CY, GA, SC, PE, LAT):
                 for d in np.unique(lw[f]):
                     if d >= 0:
                         deps[int(d)] = True
-        for p in wr + excl:
+        for p in wr:
             f = foot(p)
-            n = foot((p[0], (ALL,))).size
+            n = cells(p[0]).size
             lw = lastw.setdefault(p[0], np.full(n, -1))
             for d in np.unique(lw[f]):
                 if d >= 0:
-                    deps.setdefault(int(d), not psum(p))
+                    deps[int(d)] = True
             mark = np.zeros(n, bool); mark[f] = True
             left = []
             for (d, rf) in readers.get(p[0], []):
@@ -165,7 +189,7 @@ def build(CY, GA, SC, PE, LAT):
         for p in rd:
             readers.setdefault(p[0], []).append((me, foot(p)))
         deps.pop(me, None)
-        ops.append({"eng": eng, "calls": calls, "deps": deps, "cost": cost, "lat": lat, "tag": tag})
+        ops.append({"eng": eng, "calls": calls, "deps": deps, "cost": cost, "lat": lat, "tag": tag, "group": group})
         return me
 
     def vcost(out, ins, plain):
@@ -202,9 +226,9 @@ def build(CY, GA, SC, PE, LAT):
         cost = 65 + count(out) * GA * CY if in_[0] == "*" else 65 + max(64, count(out)) * CY
         return add("S", [("activation", (out, in_, func), kw)], [out], [in_] + list(kw.values()), cost)
 
-    def mm(items):
+    def mm(items, adds=False):
         cost = sum(max(64, count(i[2])) * PE * (1 if narrow(i[2]) else 4) for i in items) + 60
-        return add("P", [("matmul", i, {}) for i in items], [i[0] for i in items], [i[1] for i in items] + [i[2] for i in items], cost)
+        return add("P", [("matmul", i, {}) for i in items], [i[0] for i in items], [i[1] for i in items] + [i[2] for i in items], cost, adds=adds)
 
     def iota(out, pat, base, cm):
         kw = {} if SCRATCH[out[0]][2] == I32 else {"allow_small_or_imprecise_dtypes": True}
@@ -212,20 +236,27 @@ def build(CY, GA, SC, PE, LAT):
 
     ndma = [0]
 
-    def dma(eng, out, in_, lat, behind=False):
+    def dma(eng, out, in_, lat, behind=False, after=()):
         ndma[0] += 1
-        me = add(eng, [("dma_start", (out, in_), {})], [out], [in_], 60, lat, ("dma", ndma[0] - 1))
+        me = add(eng, [("dma_start", (out, in_), {})], [out], [in_], 60, lat, ("dma", ndma[0] - 1), after)
         if behind:
             ops[me]["behind"] = max(i for i in range(me) if ops[i]["eng"] == eng)
         return me
 
-    def send(msg, r, src, dst, lat):
-        s = add("G", [("send", (msg, r, src, dst), {})], [], [src], 500)
-        return add("R", [], [dst], [], 0, lat * LAT, ("msg", "%s%d" % (msg, r)), after=[s])
+    def send(key, src, ways, lat, left=0.0, relay=False):
+        s = add("G", [("send", (key, src, ways, relay), {})], [], [src], 500)
+        if left:
+            add("R", [], [], [src], 0, left, ("msg", "out_" + key, 1), after=[s])
+        me = add("R", [], [d for _, d in ways], [], 0, lat, ("msg", key, len(ways)), after=[s])
+        ops[me]["from"] = key
+        return me
 
     def scatter(win, lst, vals):
         for b in range(NA // 2 - 1, -1, -1):
-            cp(ind(win, a(lst, 2 * b, 2 * b + 2)), a(vals, 32 * b, 32 * b + 32))
+            cp(ind(win, lst(2 * b, 2 * b + 2)), vals(32 * b, 32 * b + 32))
+
+    def edit(table, msg, r):
+        scatter(a(table, 0, VW), lambda i, j: a(msg, EW * r + M + i, EW * r + M + j), lambda i, j: a(msg, EW * r + i, EW * r + j))
 
     def c1(name):
         return a(name, 0, NA)
@@ -233,11 +264,13 @@ def build(CY, GA, SC, PE, LAT):
     def ends(name):
         return a(name, 15, M, 16)
 
-    def bank3(name, k0=0, k1=16):
-        return a3(name, slice(0, NA), slice(k0, k1))
+    def bank3(name, k0=0, k1=16, h=(0, NA)):
+        if name == "pka":
+            return a(name, 16 * h[0], 16 * h[1])
+        return a3(name, slice(*h), slice(k0, k1) if k1 > k0 + 1 else k0)
 
-    def reduce(bank, zw, m, k0, k1, first, last):
-        mm([(bank3(bank, k0, k1), a(zw, 15 - p, 143 - p), a3(m, slice(p, None, 16), slice(k0, k1)), first and p == 0, last and p == 15) for p in range(16)])
+    def reduce(bank, zw, m, k0, k1):
+        mm([(bank3(bank, k0, k1), a(zw, 15 - p, 143 - p), a3(m, slice(p, None, 16), slice(k0, k1) if k1 > k0 + 1 else k0), False, False) for p in range(16)], True)
 
     turn = [0]
 
@@ -249,14 +282,34 @@ def build(CY, GA, SC, PE, LAT):
             o = a(bank, i, n * M, n)
             it += [(o, a("ib"), plus(k), True, False), (o, a("nib"), minus(k), False, True)]
         mm(it)
-        act(a3(m, ALL, slice(ks[0], ks[0] + n)), a(bank, 0, n * M), func)
+        act(a3(m, ALL, both(ks)), a(bank, 0, n * M), func)
+
+    def both(ks):
+        return slice(ks[0], ks[-1] + 1, max(1, ks[-1] - ks[0]))
 
     def pairs(k0, k1):
         return [list(range(k, min(k + 2, k1))) for k in range(k0, k1, 2)]
 
+    def slots(sets):
+        return [k for k0, st in sets for k in range(k0, 16, st)]
+
+    def twos(sets):
+        ks = sorted(slots(sets))
+        near = [[k, k + 1] for k in ks if k % 2 == 0 and k + 1 in ks]
+        far = [k for k in ks if k ^ 1 not in ks]
+        return near + [far[i:i + 2] for i in range(0, len(far), 2)]
+
+    def raw(win, lst, sets):
+        for ks in twos(sets):
+            for k0, n in ([(ks[0], 2)] if ks[-1] == ks[0] + 1 else [(k, 1) for k in ks]):
+                act(a("raws", M * k0, M * (k0 + n)), ind(win, a(lst, NA * k0, NA * (k0 + n))))
+
+    def reduce2(zw, m, k0, st):
+        mm([(a("pka", k0, M, st), a(zw, 15 - p, 143 - p), a3(m, slice(p, None, 16), slice(k0, 16, st)), False, False) for p in range(16)], True)
+
     def chunks(k0, k1, n):
         c = -(-(k1 - k0) // n)
-        e = [k0 + (k1 - k0) * i // c for i in range(c + 1)]
+        e = [k0 + (k1 - k0) * i // c for i in range(c + 1)] if c else []
         return list(zip(e[:-1], e[1:]))
 
     def turn16(src, t12):
@@ -264,71 +317,86 @@ def build(CY, GA, SC, PE, LAT):
         tr(a(t12, M, 480), a(src, 0, 256))
 
     def gather_y():
-        for k0, k1 in chunks(0, 16, 2):
-            (cp if k0 < NV1 else act)(a("rawy", M * k0, M * k1), ind(a("x"), a("Lu", NA * k0, NA * k1)))
+        for k0, k1 in chunks(NV1, 16, 2):
+            act(a("rawy", M * k0, M * k1), ind(X, a("Lu", NA * k0, NA * k1)))
 
-    def running(n, bank):
-        for h in parts(n):
-            (act if n in KEY_S else cp)(w16("key" + n, h), a3(bank, slice(*h), ALL))
-        for h in parts(n):
-            scan(w16("run" + n, h), w16("rst", h), w16("key" + n, h), AL.add, AL.max)
+    def ys(c0, c2, st=1):
+        return a("D0", NV4 + 16 * c0, 16 * c2, 16 * st)
+
+    def bound(r):
+        act(ys(0, M), ind(X, a("n4u", 64 * r, 64 * r + NA)))
+        mm([(a("pm", 0, NA), a("zp", 15 - p, 143 - p), ys(p, M, 16), p == 0, p == 15) for p in range(16)])
+        act(c1("ywin"), a("pm", 0, NA))
 
     def parts(n):
         return HALVES if n in SPLIT else [(0, NA)]
 
-    def w16(name, h):
-        return a(name, 16 * h[0], 16 * h[1])
+    def w16(name, h, n=16):
+        return a(name, n * h[0], n * h[1])
 
-    def e16(name, h):
-        return a(name, 16 * h[0] + 15, 16 * h[1], 16)
+    def e16(name, h, n=16):
+        return a(name, n * h[0] + n - 1, n * h[1], n)
 
-    def choose(n, bank, val):
-        mm([(a("pf", 0, M), a("i32"), val, True, True)])
+    def running(n, bank, w=16):
         for h in parts(n):
-            tt(w16("u" + n, h), w16("run" + n, h), a3(bank, slice(*h), ALL), AL.subtract)
+            if n not in KEY_P:
+                (act if n in KEY_S else cp)(w16("key" + n, h, w), bank3(bank, 0, w, h))
         for h in parts(n):
-            tt(w16("e" + n, h), w16("pf", h), w16("u" + n, h), AL.subtract)
-        for h in parts(n):
-            scan(w16("sel" + n, h), w16("u" + n, h), w16("e" + n, h), AL.min, AL.max)
+            scan(w16("run" + n, h, w), w16("rst" if w == 16 else "rs7", h, w), bank3(bank, 0, w, h) if n in KEY_P else w16("key" + n, h, w), AL.min, AL.max)
 
-    def slot(n, ti, tj):
+    def choose(n, bank, w=16, between=lambda: None):
         for h in parts(n):
-            ts(a(ti, *h), e16("run" + n, h), -1.0 / 4096, AL.mult, 131072.0, AL.add)
-            ts(a(tj, *h), a(ti, *h), 15, AL.bitwise_and)
+            tt(w16("u" + n, h, w), w16("run" + n, h, w), bank3(bank, 0, w, h), AL.subtract)
+        between()
+        for h in parts(n):
+            tt(w16("e" + n, h, w), bank3("pf", 0, w, h), w16("u" + n, h, w), AL.subtract)
+        for h in parts(n):
+            scan(w16("sel" + n, h, w), w16("u" + n, h, w), w16("e" + n, h, w), AL.min, AL.max)
 
-    def lowest(pw, p14, pu, outu):
-        for a0, a1 in HALVES:
+    def slot(n, ti, tj, w=16):
+        for h in parts(n):
+            ts(a(ti, *h), e16("run" + n, h, w), -1.0 / 4096, AL.mult, 131072.0, AL.add)
+            ts(tj(*h), a(ti, *h), 15, AL.bitwise_and)
+
+    LW = 8 if "l" in SPLIT else 16
+
+    def lowest(pw, p14, out):
+        for a0, a1 in parts("l"):
             n3, c0, c2 = 3 * (a1 - a0) // 2, 24 * a0, 24 * a1
-            win = a(pw, p14 + a0, p14 + a0 + 8)
-            cp(a("pu3", 2 * a0, 2 * a0 + 16), ind(win, a("rep3", 0, 1)))
+            win = a(pw, p14 + a0, p14 + a0 + LW)
+            cp(a("pu3", 2 * a0, 2 * a0 + 2 * LW), ind(win, a("rep3", 0, LW // 8)))
             tt(a("row", c0, c2), ind(a("iot"), a("pu3", 2 * a0, 2 * a0 + n3)), a("poison", c0, c2), AL.add)
             tt(a("eq", c0, c2), ind(win, a("cA3", 0, n3)), a("row", c0, c2), AL.is_equal)
             scan(a("dsc", c0, c2), a("dd0", c0, c2), a("eq", c0, c2), AL.mult, AL.max)
-            tt(a("P2", 2 * a0, 2 * a0 + 16), ind(a("dsc", c0, c0 + 192), a("end3", 0, 1)), a(pw, p14 + a0, p14 + a0 + 16), AL.max)
-            cp(a(outu, a0, a1), a("P2", 2 * a0, a0 + a1))
+            tt(a("P2", 2 * a0, 2 * a0 + 16), ind(a("dsc", c0, c0 + 24 * LW), a("end3", 0, 1)), a(pw, p14 + a0, p14 + a0 + 16), AL.max)
+            cp(out(a0, a1), a("P2", 2 * a0, a0 + a1))
 
-    X = a("x")
+    X = a("x", 0, V)
     P8 = slice(0, 8)
     whole = lambda n: (n, (ALL, ALL))
-    dma("Y", a("lai"), whole("la"), 2200)
-    dma("S", a("bi", part=P8), whole("b0"), 2000)
-    big = [(a("tile", 0, V), whole("sb"), 4500), (a("x", 0, V), whole("xs"), 2300)]
-    t = 2200
-    for o, i, d in (big if TILE_FIRST else big[::-1]):
-        t += d
-        dma("Y", o, i, t, True)
+    piece = lambda n, i: a(n, V // XC * i, V // XC * (i + 1))
     dma("S", a("thi2", 0, 1, part=P8), whole("th"), 2000)
+    for i in range(XC):
+        dma("Y", piece("x", i), piece("xs", i), 2200 + 2300 * (i + 1) // XC, i > 0)
+    tile = dma("Y", a("tile", 0, V), whole("sb"), 11000, True)
+    dma("S", a("lai"), whole("la"), 2500)
+    dma("S", a("bi", part=P8), whole("b0"), 2000)
     dma("S", a("z"), whole("z0"), 2500)
     dma("S", a("lwi"), whole("lw"), 2500)
+    for i in range(XC):
+        send("xa%d" % i, piece("x", i), [(-HOPS[0], piece("xp0", i))], 7000, 6000)
+    dma("Y", a("xq"), X, 4500, after=[tile])
     iota(a("qi", 0, 1), [[0, 1]], 0, 1)
     iota(a("i144"), [[1, 144]], 0, 0)
     iota(a("gm16"), [[16, 8], [0, 16]], 0, 0)
     iota(a("kidx"), [[0, NA], [1, 16]], 0, 0)
-    for i in range(4):
-        iota(a("iot", VW // 4 * i, VW // 4 * (i + 1)), [[1, VW // 4]], VW // 4 * i, 0)
-    cols = ["q", "p", "g16", "g16e", "q16", "q16e", "p14", "e", "fl", "ms", "pq"]
+    iota(a("k17"), [[0, NA], [1, 17]], 0, 0)
+    for i in range(8):
+        iota(a("iot", VW // 8 * i, VW // 8 * (i + 1)), [[1, VW // 8]], VW // 8 * i, 0)
+    cols = ["q", "p", "g16", "g16e", "q16", "q16e", "e", "fl", "ms"]
     C = {n: a("col", i, i + 1) for i, n in enumerate(cols)}
     c14 = a("i144", 0, NA)
+    spare = a("DP", 0, NA)
     cp(C["q"], a("qi", 0, 1))
     ts(a("qj", 0, 1), a("qi", 0, 1), 15, AL.bitwise_and)
     cp(C["p"], a("qj", 0, 1))
@@ -336,19 +404,15 @@ def build(CY, GA, SC, PE, LAT):
     ts(C["g16e"], C["g16"], 15.0, AL.add)
     ts(C["q16"], C["q"], 16.0, AL.mult)
     ts(C["q16e"], C["q"], 16.0, AL.mult, 15.0, AL.add)
-    ts(C["p14"], C["p"], 14.0, AL.mult)
     ts(a("qj", 1, 2), a("qi", 0, 1), 4, AL.arith_shift_right, 1, AL.bitwise_and)
     cp(C["e"], a("qj", 1, 2))
     tt(a("qi", 1, 2), C["p"], C["e"], AL.add)
     ts(a("qj", 2, 3), a("qi", 1, 2), 1, AL.bitwise_and)
     ts(C["fl"], a("qj", 2, 3), 240.0, AL.mult)
-    ts(C["ms"], C["p"], float(NV2), AL.is_ge)
-    act(C["pq"], C["p"], AF.Identity, bias=0.25)
-    act(c1("frac"), c14, AF.Identity, scale=1.0 / NA)
     ts(c1("cidx"), c14, 16.0, AL.mult, C["p"], AL.add)
-    ts(c1("dummy"), c1("cidx"), float(V), AL.add)
+    iota(a("DP", NA, 48), [[0, 48 - NA]], 0, 0)
+    ts(spare, c1("cidx"), V + 16.0, AL.add)
     cp(c1("cA"), c14)
-    ts(c1("pKA"), c14, C["p14"], AL.add)
     ts(c1("ti"), c14, C["e"], AL.add)
     ts(c1("tj"), c1("ti"), 1, AL.bitwise_and)
     ts(c1("t1"), c1("tj"), 240.0, AL.mult)
@@ -360,21 +424,23 @@ def build(CY, GA, SC, PE, LAT):
     tt(c1("t3"), c1("jt"), c1("jt2"), AL.add)
     cp(c1("pAK"), c1("t3"))
     ts(c1("pK"), c1("t3"), C["fl"], AL.add)
-    ts(c1("wf"), c14, -14.0, AL.add, C["ms"], AL.mult)
-    ts(c1("cS"), c1("wf"), 14.0, AL.add)
     ts(a("rep4"), a("i144", 0, 4), 0.0, AL.mult, C["p"], AL.add)
-    for n, w in (("zp", W1), ("zn", -W1), ("z2p", 2 * W1), ("z2n", -2 * W1)):
-        ts(a(n), a("i144"), C["g16e"], AL.is_equal, w, AL.mult)
+    ts(a("zp"), a("i144"), C["g16e"], AL.is_equal, W1, AL.mult)
+    for n, w in (("zn", -1.0), ("z2n", -2.0)):
+        act(a(n), a("zp"), AF.Identity, scale=w)
     ts(a("z8"), a("i144"), C["q16e"], AL.is_equal)
     ts(a("bo8"), a("gm16"), C["q16"], AL.is_equal)
-    ts(a("bo"), a("gm16"), C["g16"], AL.is_equal)
+    ts(a("bo2"), a("gm16"), C["g16"], AL.is_equal, 2.0, AL.mult)
     ts(a("i32"), a("i144", 0, 128), C["q"], AL.is_equal)
-    cp(a("ib"), a("i32"))
-    ts(a("nib"), a("ib"), -1.0, AL.mult)
-    ts(a("nbi"), a("ib"), -2.0 ** 29, AL.mult)
-    ts(a("kcb"), a("kidx"), -4096.0, AL.mult)
-    ts(a("rst"), a("kidx"), 0.0, AL.is_equal, -2.0 ** 30, AL.mult)
-    ts(a("cmask"), a("kidx"), 0.0, AL.is_gt)
+    for n, w in (("ib", 1.0), ("nib", -1.0), ("nbi", -2.0 ** 29), ("nq", -0.25), ("ni32", -1.0), ("ib32", -4096.0)):
+        act(a(n), a("i32"), AF.Identity, scale=w)
+    act(a("bo32"), a("bo2"), AF.Identity, scale=0.5)
+    act(a("kcb"), a("kidx"), AF.Identity, scale=-4096.0)
+    act(a("kc7"), a("k17"), AF.Identity, scale=-4096.0)
+    iota(a("kc7", 16, M7, 17), [[0, NA]], 0, 0)
+    act(a("rst"), a("kidx"), AF.Identity, scale=2.0 ** 32, bias=-2.0 ** 31)
+    act(a("rs7"), a("k17"), AF.Identity, scale=2.0 ** 32, bias=-2.0 ** 31)
+    act(a("cmask"), a("kidx"), AF.Sign)
     iota(a("row"), [[0, 21], [1, 16]], 0, 0)
     ts(a("poison"), a("row"), C["p"], AL.is_ge, 8192.0, AL.mult)
     for b in range(NA // 2):
@@ -382,39 +448,41 @@ def build(CY, GA, SC, PE, LAT):
     iota(a("dd0"), [[0, M3]], 1, 0)
     iota(a("dd0", 0, M3, 48), [[0, 7]], 0, 0)
     iota(a("dd0", 16, M3, 48), [[0, 7]], 0, 0)
-    act(a("dd0", 15, M3, 48), a("dummy", 0, NA, 2))
-    act(a("dd0", 47, M3, 48), a("dummy", 1, NA, 2))
-    ts(a("wi", 0, 1), C["p"], 2.0 / 3, AL.mult, -1.0 / 3, AL.add)
-    ts(a("rep3", 0, 1), a("wi", 0, 1), 7.0, AL.min)
+    act(a("dd0", 15, M3, 48), a("DP", 0, NA, 2))
+    act(a("dd0", 47, M3, 48), a("DP", 1, NA, 2))
+    ts(a("nf", 0, 1), C["p"], 2.0 / 3, AL.mult, -1.0 / 3, AL.add)
+    ts(a("wi", 0, 2), a("i144", 0, 2), 32.0 / 3, AL.mult, a("nf", 0, 1), AL.add)
+    ts(a("rep3", 0, 2), a("wi", 0, 2), LW - 1.0, AL.min)
     iota(a("dsc", M3, 384), [[0, 384 - M3]], 0, 0)
     ts(a("l12i", 0, 21), a("i144", 0, 21), 2.0 / 3, AL.mult)
     cp(a("cA3", 0, 21), a("l12i", 0, 21))
     ts(a("qj", 3, 4), a("qi", 0, 1), 1, AL.bitwise_and)
     ts(a("nf", 1, 2), a("qj", 3, 4), 8.0, AL.mult, 15.0, AL.add)
     ts(a("nf", 2, 3), C["p"], 24.0, AL.mult, a("nf", 1, 2), AL.add)
-    ts(a("end3", 0, 1), a("nf", 2, 3), 191.0, AL.min)
+    ts(a("end3", 0, 1), a("nf", 2, 3), 24.0 * LW - 1, AL.min)
+    ts(a("nf", 3, 4), C["p"], 17.0, AL.mult, 16.0, AL.add)
+    ts(a("end7"), a("i144", 0, 4), a("nf", 3, 4), AL.max, M7 - 1.0, AL.min)
     ts(a("id16"), a("i144", 0, 32), C["p"], AL.is_equal)
-    act(a("bo32"), a("bo"))
-    ms(a("mh"), -0.5)
-    ms(a("x", V, VW), 0.0)
-    ms(a("tile", V, VW), 0)
+    fill = lambda p, c=0: iota(p, [[0, count(p)]], c, 0)
+    fill(a("mh"), 2)
+    for n in ["x", "tile"] + ["xp%d" % r for r in range(RO)]:
+        fill(a(n, V, VW))
+    for i in (NA, NA + 1):
+        ms(a("ed", M + i, EW * RO, EW), 0)
     for n in ("L", "W", "ssl", "lp", "wp"):
-        ms(a(n, 0, 256, 240), 0.0) if False else (ms(a(n, 0, 16), 0.0), ms(a(n, 240, 256), 0.0))
-    for r in range(RO):
-        ms(a("ys", YW * r + M, YW * (r + 1)), -8.0)
-    for r in range(RO):
-        ms(a("xks", XW * r + M + NA, XW * (r + 1)), 0.0)
-    ms(a("ywin"), 0.0)
-    ms(a("P"), 0.0)
-    ms(a("wf"), 0.0)
-    ms(a("ee"), 0.0)
-    ms(a("n4", 0, 64), 0.0)
-    ms(a("base4"), 0.0)
-    ms(a("delta4"), float(M))
-    cp(a("base4", 48, 48 + NA), c1("cidx"))
+        fill(a(n, 0, 16))
+        fill(a(n, 240, 256))
+    fill(a("kp"), 1)
+    for p in (a("ywin"), a("wj"), a("ee"), a("n4", 0, 64), a("base4", 48 + NA, 64)):
+        fill(p)
+    ts(a("base4", 48, 48 + NA), c1("cidx"), float(VW), AL.add)
     for i in range(4):
-        iota(a("D0", 4 * M * i, 4 * M * (i + 1)), [[0, 4 * M]], 0, 0)
+        ms(a("D0", 4 * M * i, 4 * M * (i + 1)), 0.0)
     ms(a("D0", 0, None, 16), -1024.0)
+    cp(a("thf", 0, 1, part=P8), a("thi2", 0, 1, part=P8))
+    mm([(a("pm", 0, 1), a("bo8", part=P8), a("thf", 0, 1, part=P8), True, True)])
+    ts(a("thb", 0, 1), a("pm", 0, 1), -W1, AL.mult, 63488.0, AL.add)
+    send("th", a("thb", 0, 1), [(-HOPS[r], a("thr", 4 * r, 4 * r + 1)) for r in range(RO)], 5000)
     cp(a("lp", 16, 240), a("lai"))
     turn16("lp", "t12a")
     cp(a("Lu"), ind(a("t12a"), c1("pK")))
@@ -422,211 +490,210 @@ def build(CY, GA, SC, PE, LAT):
     cp(a("bb", part=P8), a("bi", part=P8))
     mm([(a("pm", 0, NA), a("z8", 15 - p, 143 - p, part=P8), a("bb", p, M, 16, part=P8), p == 0, p == 15) for p in range(16)])
     cp(a("n4", 16, 16 + NA), a("pm", 0, NA))
-    tt(a("oh"), ind(a("n4", 16, 32), c1("cA")), a("kidx"), AL.is_equal)
-    tt(a("tl"), a("oh"), a("L", 16, 240), AL.mult)
+    tt(a("oh", 0, M), ind(a("n4", 16, 32), c1("cA")), a("kidx"), AL.is_equal)
+    tt(a("tl"), a("oh", 0, M), a("L", 16, 240), AL.mult)
     scan(a("tw"), a("cmask"), a("tl"), AL.mult, AL.add)
     cp(a("n4", 0, NA), ends("tw"))
     cp(a("n4u", 0, 64), a("n4", 0, 64))
-    cp(a("thf", 0, 1, part=P8), a("thi2", 0, 1, part=P8))
-    mm([(a("pm", 0, 1), a("bo8", part=P8), a("thf", 0, 1, part=P8), True, True)])
-    ts(a("thw", 0, 1), a("pm", 0, 1), -W1, AL.mult)
-    ts(a("kcth"), a("kidx"), -4096.0, AL.mult, a("thw", 0, 1), AL.add)
-    act(a("ni32"), a("i32"), AF.Identity, scale=-1.0)
     cp(a("wp", 16, 240), a("lwi"))
     turn16("wp", "t12b")
     cp(a("Wu"), ind(a("t12b"), c1("pK")))
     act(a("W", 16, 240), ind(a("t12b"), c1("pA")))
+    bound(0)
+    gather_y()
 
     for r in range(RO):
         last = r == RO - 1
         n0, n1 = 64 * r, 64 * (r + 1)
         LB, LBu, B = a("n4", n0, n0 + NA), a("n4u", n0, n0 + NA), a("n4", n0 + 16, n0 + 16 + NA)
-        yr, need = a("yr", YW * r, YW * r + M), a("yr", YW * r + M, YW * r + M + 1)
-        sl = lambda name, k, n=1, o=0: a(name, o + NA * k, o + NA * (k + n))
+        xp = "xp%d" % r
+        XP = a(xp, 0, V)
+        y, oh, thr = ys(0, M), a("oh", M * r, M * (r + 1)), a("thr", 4 * r, 4 * r + 1)
+        need = a("need", r, r + 1) if r else -8.0
+        sl = lambda name, k, n=1: a(name, NA * k, NA * (k + n))
         kb = lambda name, k, n=1: a(name, M * k, M * (k + n))
-        act(a("ys", YW * r, YW * r + M), ind(X, LBu))
-        send("y", r, a("ys", YW * r, YW * (r + 1)), a("yr", YW * r, YW * (r + 1)), 3000)
         cp(a("ssl", 16, 240), ind(a("tile"), LBu))
         turn16("ssl", "t12c")
-        cp(kb("ss", r), ind(a("t12c"), c1("pK")))
-        send("s", r, kb("ss", r), kb("sr", r), 3000)
-        if r == 0:
-            gather_y()
-        for ks in pairs(0, 16):
+        cp(a("su"), ind(a("t12c"), c1("pK")))
+        act(a("sa"), ind(a("t12c"), c1("pA")))
+        for ks in pairs(NV1, 16):
             diff(ks, lambda k: kb("rawy", k), lambda k: a("z"), AF.Abs, "m1", 2)
-        mm([(bank3("pkb"), a("ib"), a("kcb"), True, False), (bank3("pkb"), a("nbi"), a("oh"), False, False)])
-        for k0, k1 in chunks(0, 16, 8):
-            reduce("pkb", "zn", "m1", k0, k1, False, k1 == 16)
-        mm([(a("pm", 0, NA), a("zp", 15 - p, 143 - p), a("yr", YW * r + p, YW * r + M, 16), p == 0, p == 15) for p in range(16)])
-        act(c1("ywin"), a("pm", 0, NA))
-        act(a("add2"), ind(a("ywin"), c1("cS")))
-        act(a("thr16"), ind(a("ywin"), c1("cA")), AF.Identity, bias=a("thw", 0, 1))
-        act(a("qq"), yr, AF.Identity, scale=0.25, bias=159.625)
-        act(a("D0", NV4, None, 16), yr)
-        mm([(bank3("pka"), a("i32"), a("kcth"), True, False)])
-        for k in range(NV2):
-            tt(a3("m2", ALL, k), ind(X, sl("sr", k, 1, M * r)), yr, AL.min)
-        for ks in pairs(NV2, 16):
-            act(kb("raws", ks[0], len(ks)), ind(X, sl("sr", ks[0], len(ks), M * r)))
-        for ks in pairs(NV2, 16):
-            diff(ks, lambda k: yr, lambda k: kb("raws", k), AF.Relu, "m2")
-        cv = chunks(0, NV2, 5)
-        for k0, k1 in cv[:-1]:
-            reduce("pka", "zp", "m2", k0, k1, False, False)
-        mm([(bank3("pka"), a("i32"), a("add2"), False, False)])
-        reduce("pka", "zn", "m2", NV2, 16, False, False)
-        reduce("pka", "zp", "m2", cv[-1][0], cv[-1][1], False, True)
-        cp(a("sf"), kb("sr", r))
-        act(a("sa"), ind(a("sf"), c1("pKA")))
+        mm([(bank3("pkb", 0, 17), a("ib"), a("kc7"), True, False)])
+        for k in range(NV1):
+            tt(a3("rawv", ALL, k), ind(a("xq") if r else X, sl("Lu", k)), a("z"), AL.subtract)
+        if r == 1:
+            cp(a("Lu"), ind(a("L", 16, 240), c1("pAK")))
+        for k0, k1 in chunks(0, NV1, CH1):
+            ts(a3("m1", ALL, slice(k0, k1)), a3("rawv", ALL, slice(k0, k1)), 0.0, AL.max)
+        if NV1:
+            reduce("pkb", "zp", "rawv", 0, NV1)
+            reduce("pkb", "z2n", "m1", 0, NV1)
+        it = [(bank3("pkb"), a("nbi"), oh, False, False), (bank3("pkb", 16, 17), a("nbi"), a("kp", 16 * r, 16 * r + NA), False, False)]
+        if r:
+            it += [(bank3("pkb"), a("nbi"), kb("oh", r - 1), False, False), (bank3("pkb", 16, 17), a("ib32"), a("n4", n0 - 48, n0 - 48 + NA), False, False)]
+        mm(it, True)
+        if r:
+            diff([16], lambda k: a("ynew"), lambda k: a("z"), AF.Abs, "m1", 2)
+        for k0, k1 in chunks(NV1, 17 if r else 16, RC1):
+            reduce("pkb", "zn", "m1", k0, k1)
+        if not THR_PE:
+            act(a("thr16"), ind(a("ywin"), c1("cA")))
+        mm([(a("pka", 0, M), a("ib"), a("kcb"), True, False)])
+        cv, cs = SETS[NV2]
+        for k in slots(cv):
+            tt(a3("m2", ALL, k), ind(XP, sl("su", k)), y, AL.min)
+        raw(XP, "su", cs)
+        for ks in twos(cs):
+            diff(ks, lambda k: y, lambda k: kb("raws", k), AF.Relu, "m2")
+        for c in cv:
+            reduce2("zp", "m2", *c)
+        if cs:
+            mm([(a("pka", k, M, 16), a("i32"), c1("ywin"), False, False) for k in slots(cs)], True)
+        for c in cs:
+            reduce2("zn", "m2", *c)
         running("2", "pka")
-        choose("2", "pka", a("sa"))
+        mm([(bank3("pf"), a("i32"), a("sa"), True, True)])
+        choose("2", "pka", 16, lambda: [act(w16("bind", h), w16("pka" if "2" in KEY_P else "key2", h), AF.Sign, bias=thr) for h in parts("c")])
         for h in parts("c"):
-            act(w16("bind", h), w16("key2", h), AF.Sign, bias=61440.5)
             scan(w16("cnt", h), w16("cmask", h), w16("bind", h), AL.mult, AL.add)
-            ts(a("nocc", *h), e16("cnt", h), need, AL.is_lt)
-            tt(a("nd", *h), a("nocc", *h), a("dummy", *h), AL.mult)
+            ts(a("nd", *h), e16("cnt", h), need, AL.is_lt, float(V), AL.mult)
         for h in parts("2"):
-            tt(a("P", *h), e16("sel2", h), a("nd", *h), AL.max)
-        ts(c1("need2"), c1("nocc"), 99.0, AL.mult, need, AL.add)
-        for h, bank in zip(parts("x"), ("pm", "pf")):
-            cp(a("Pu", *h), a("P", *h))
-            act(w16("xsel", h), ind(X, a("Pu", *h)))
-            mm([(w16(bank, h), a("ib"), w16("xsel", h), True, False), (w16(bank, h), a("nib"), w16("qq", h), False, True)])
-            act(w16("new", h), w16(bank, h), AF.Relu, bias=160.0)
-        lowest("P", 0, None, "P2u")
-        scatter(X, "P2u", "new")
-        if last:
-            dma("Y", whole("yx"), a("x", 0, V), 4500)
-        for k in range(NV4):
-            tt(a("D", k, None, 16), ind(X, sl("sr", k, 1, M * r)), yr, AL.subtract)
-        for k in range(NV4, 16):
-            act(a("D", k, None, 16), ind(X, sl("sr", k, 1, M * r)))
-        for k in range(NV4):
-            if k < REL4:
-                act(a3("m2", ALL, k), a("D", k, None, 16), AF.Relu, scale=-1.0)
-            else:
-                ts(a3("m2", ALL, k), a("D", k, None, 16), -1.0, AL.mult, 0.0, AL.max)
-        for ks in pairs(NV4, 16):
-            diff(ks, lambda k: yr, lambda k: a("D", k, None, 16), AF.Relu, "m2")
-        scan(a("Do"), a("D0"), a("D"), AL.add, AL.max)
-        (act if FS_S else cp)(kb("fs", r), a("Do", 15, None, 16))
-        send("f", r, kb("fs", r), kb("fr", r), 3000)
-        mm([(bank3("pka"), a("i32"), a("thr16"), True, False)])
-        for k0, k1 in [(0, NV4)] + chunks(NV4, 16, 5):
-            reduce("pka", "zn", "m2", k0, k1, False, k1 == 16)
-        if BIND_V:
-            act(c1("need3"), c1("need2"), AF.Identity, scale=0.5)
-            ts(a("bind"), bank3("pka"), 0.0, AL.is_ge, -0.5, AL.add)
-        else:
-            act(a("bind"), bank3("pka"), AF.Sign, bias=0.5)
-        scan(a("cnt"), a("cmask"), a("bind"), AL.mult, AL.add)
-        x0, y0 = XW * r, (M + XW) * r
-        tt(a("xks", x0 + M, x0 + M + NA), ends("cnt"), c1("need3" if BIND_V else "need2"), AL.is_ge)
-        act(a("xks", x0, x0 + M), ind(X, c1("Pu")))
-        send("k", r, a("xks", x0, x0 + XW), a("yx2", y0 + M, y0 + M + XW), 3000)
-        running("1", "pkb")
-        choose("1", "pkb", a("L", 16, 240))
-        slot("1", "ji", "jj")
-        act(a("base4", 0, NA), ends("sel1"))
-        cp(a("base4", 16, 16 + NA), c1("jj"))
-        tt(a("delta4", 0, NA), LB, ends("sel1"), AL.subtract)
-        tt(a("delta4", 16, 16 + NA), B, a("base4", 16, 16 + NA), AL.subtract)
-        tt(c1("jt"), c1("jj"), c1("frac"), AL.add)
-        ts(c1("ju"), c1("jt"), float(M), AL.mult, C["pq"], AL.add)
-        act(a("yx2", y0, y0 + M), ind(a("rawy"), c1("ju")))
+            tt(a("DP", 16 + h[0], 16 + h[1]), e16("sel2", h), a("nd", *h), AL.max)
+        ts(c1("need2"), c1("nd"), need, AL.add)
+        e0 = EW * r
+        for h, bank in zip(parts("x"), (lambda h: w16("pd0", h), lambda h: w16("pd1", h))):
+            cp(a("Pu", *h), e16("sel2", h))
+            act(w16("xsel", h), ind(XP, a("Pu", *h)))
+            mm([(bank(h), a("ib"), w16("xsel", h), True, False), (bank(h), a("nq"), ys(16 * h[0], 16 * h[1]), False, True)])
+            ts(a("ed", e0 + 16 * h[0], e0 + 16 * h[1]), bank(h), 0.375, AL.add)
+        lowest("DP", 16, lambda i, j: a("ed", e0 + M + i, e0 + M + j))
+        ed = a("ed", e0, e0 + EW)
+        send("eo%d" % r, ed, [(HOPS[r], a("eo", e0, e0 + EW))], 3000 * LAT)
+        edit(xp, "ed", r)
         if not last:
-            act(a("base4", 32, 32 + NA), ends("sel1"))
-            tt(a("delta4", 32, 32 + NA), c1("dummy"), ends("sel1"), AL.subtract)
-            cp(c1("lju"), ends("sel1"))
+            for key, i in (("xb", 0), ("xc", 1)):
+                cut = lambda n: a(n, V // 2 * i, V // 2 * (i + 1))
+                send(key + str(r), cut(xp), [(HOPS[r] - HOPS[r + 1], cut("xp%d" % (r + 1)))], 9000 + 4000 * i, 0, i == 1)
+        running("1", "pkb", 17)
+        mm([(bank3("pf"), a("i32"), a("L", 16, 240), True, False), (bank3("pf", 16, 17), a("i32"), ends("sel5") if r else spare, False, True)])
+        choose("1", "pkb", 17)
+        cp(a("base4", 0, 48), ind(a("sel1", 0, M7), a("end7", 0, 3)))
+        slot("1", "ji", lambda i, j: a("base4", 16 + i, 16 + j), 17)
+        tt(a("delta4", 0, 32), a("n4", n0, n0 + 32), a("base4", 0, 32), AL.subtract)
+        tt(a("delta4", 32, 64), a("DP", 0, 32), a("base4", 32, 64), AL.subtract)
+        cp(c1("lju"), e16("sel1", (0, NA), 17))
+        act(a(xp, VW, VX), ind(a("xq"), c1("lju")))
+        if not last:
             cp(a("tlj"), ind(a("tile"), c1("lju")))
-            mm([(a("pm", 0, M), a("i32"), a("ssl", 16, 240), True, False), (a("pm", 0, M), a("ni32"), a("tlj"), False, True)])
-            act(a("dlt"), a("pm", 0, M))
-            tt(c1("t1"), B, c1("frac"), AL.add)
-            ts(c1("plu"), c1("t1"), float(M), AL.mult, C["pq"], AL.add)
-            gather_y()
+            if DLT_V:
+                tt(a("dlt"), a("ssl", 16, 240), a("tlj"), AL.subtract)
+            else:
+                mm([(a("pm", 0, M), a("i32"), a("ssl", 16, 240), True, False), (a("pm", 0, M), a("ni32"), a("tlj"), False, True)])
+                act(a("dlt"), a("pm", 0, M))
         else:
             turn16("L", "t12a")
             act(a("lsl"), ind(a("t12a"), c1("pA")))
             turn16("W", "t12b")
             act(a("wsl"), ind(a("t12b"), c1("pA")))
             tt(a("tw"), ind(a("iot"), LBu), a("wsl"), AL.subtract)
-        fr = kb("fr", r)
-        for ks in pairs(NV5, 16):
-            act(kb("raws", ks[0], len(ks)), ind(X, sl("Wu", ks[0], len(ks))))
-        for k in range(NV5):
+        edit("x", "eo", r)
+        if last:
+            dma("Y", whole("yx"), X, 4500)
+        else:
+            dma("Y", a("xq"), X, 4500)
+        for k in range(NV4):
+            tt(a("D", k, None, 16), ind(XP, sl("su", k)), y, AL.subtract)
+        for k in range(NV4, 16):
+            act(a("D", k, None, 16), ind(XP, sl("su", k)))
+        for k in range(NV4):
+            if k < REL4:
+                act(a3("m2", ALL, k), a("D", k, None, 16), AF.Relu, scale=-1.0)
+            else:
+                ts(a3("m2", ALL, k), a("D", k, None, 16), -1.0, AL.mult, 0.0, AL.max)
+        for ks in pairs(NV4, 16):
+            diff(ks, lambda k: y, lambda k: a("D", k, None, 16), AF.Relu, "m2")
+        for c0, c2 in chunks(0, M, M // NS):
+            scan(a("Do", 16 * c0, 16 * c2), a("D0", 16 * c0, 16 * c2), a("D", 16 * c0, 16 * c2), AL.add, AL.max)
+        if THR_PE:
+            mm([(a(B4, k, M, 16) if B4 == "pka" else bank3(B4, k, k + 1), a("i32"), c1("ywin"), k == 0, False) for k in range(16)])
+        else:
+            mm([(bank3(B4), a("i32"), a("thr16"), True, False)])
+        if B4 == "pka":
+            for j in range(4):
+                mm([(a(B4, j, M, 4), a("zn", 15 - p, 143 - p), a3("m2", slice(p, None, 16), slice(4 * j, 4 * j + 4)), False, False) for p in range(16)], True)
+        else:
+            for k0, k1 in [(0, NV4)] + chunks(NV4, 16, RC):
+                reduce(B4, "zn", "m2", k0, k1)
+        act(a("bind"), bank3(B4), AF.Sign, bias=thr)
+        scan(a("cnt"), a("cmask"), a("bind"), AL.mult, AL.add)
+        kr, kr14 = a("kp", 16 * r + 16, 16 * r + 32), a("kp", 16 * r + 16, 16 * r + 16 + NA)
+        tt(kr14, ends("cnt"), c1("need2"), AL.is_ge)
+        fr = a("Do", 15, None, 16)
+        cv, cs = SETS[NV5]
+        raw(X, "Wu", cs)
+        for k in slots(cv):
             tt(a3("rawv", ALL, k), ind(X, sl("Wu", k)), fr, AL.subtract)
-        held = list(zip(["pd2", "pd3", "pd0", "pd1"] * 2, pairs(NV5, 16)))
-        pre = lambda bank, ks: mm([(a(bank, 0, len(ks) * M), a("ib"), kb("raws", ks[0], len(ks)), True, False)])
+        held = list(zip(["pd2", "pd3", "pd0", "pd1"] * 2, twos(cs)))
+        pre = lambda bank, ks: mm([(a(bank, i, len(ks) * M, len(ks)), a("ib"), kb("raws", k), i == 0, False) for i, k in enumerate(ks)])
         for bank, ks in held[:4]:
             pre(bank, ks)
         for n, (bank, ks) in enumerate(held):
             if n >= 4:
                 pre(bank, ks)
-            mm([(a(bank, i * M, (i + 1) * M), a("nib"), fr, False, i == len(ks) - 1) for i in range(len(ks))])
-            for i, k in enumerate(ks):
-                act(a3("m5", ALL, k), a(bank, i * M, (i + 1) * M), AF.Abs)
-        mm([(bank3("pkb"), a("ib"), a("kcb"), True, False)])
-        cv, cs = chunks(0, NV5, CH5), chunks(NV5, 16, 5)
-        for n, (k0, k1) in enumerate(cv):
+            mm([(a(bank, i, len(ks) * M, len(ks)), a("nib"), fr, False, i == len(ks) - 1) for i in range(len(ks))])
+            act(a3("m5", ALL, both(ks)), a(bank, 0, len(ks) * M), AF.Abs)
+        mm([(a("pka", 0, M), a("ib"), a("kcb"), True, False)])
+        for n, (k0, st) in enumerate(cv):
             if n < ABS5:
-                act(a3("m5", ALL, slice(k0, k1)), a3("rawv", ALL, slice(k0, k1)), AF.Abs)
+                act(a3("m5", ALL, slice(k0, 16, st)), a3("rawv", ALL, slice(k0, 16, st)), AF.Abs)
             else:
-                ts(a3("m5", ALL, slice(k0, k1)), a3("rawv", ALL, slice(k0, k1)), 0.0, AL.max)
-        for k0, k1 in cs[:-1]:
-            reduce("pkb", "zn", "m5", k0, k1, False, False)
-        for n, (k0, k1) in enumerate(cv):
+                ts(a3("m5", ALL, slice(k0, 16, st)), a3("rawv", ALL, slice(k0, 16, st)), 0.0, AL.max)
+        for c in cs:
+            reduce2("zn", "m5", *c)
+        for n, c in enumerate(cv):
             if n >= ABS5:
-                reduce("pkb", "zp", "rawv", k0, k1, False, False)
-            if k1 == NV5:
-                reduce("pkb", "zn", "m5", cs[-1][0], 16, False, False)
-            reduce("pkb", "zn" if n < ABS5 else "z2n", "m5", k0, k1, False, k1 == NV5)
-        kr, kr14 = a("yx2", y0 + 2 * M, y0 + 2 * M + 16), a("yx2", y0 + 2 * M, y0 + 2 * M + NA)
+                reduce2("zp", "rawv", *c)
+            reduce2("zn" if n < ABS5 else "z2n", "m5", *c)
         tt(a("n4t"), ind(kr, a("rep4")), a("delta4"), AL.mult)
         tt(a("n4", n1, n1 + 64), a("n4t"), a("base4"), AL.add)
         cp(a("n4u", n1, n1 + 64), a("n4", n1, n1 + 64))
         if not last:
-            mm([(a("pm", 0, NA), a("bo"), kr14, True, True)])
-            add("S", [("activation", (c1("junk"), a("pm", 0, NA), AF.Identity), {"accum_out": a("nf", 0, 1)})], [c1("junk"), a("nf", 0, 1)], [a("pm", 0, NA)], 150)
-            cp(a("ni", 0, 1), a("nf", 0, 1))
-            ts(a("nj", 0, 1), a("ni", 0, 1), 1, AL.bitwise_and)
-            ts(a("ys", YW * (r + 1) + M, YW * (r + 1) + M + 1), a("nj", 0, 1), 2.0, AL.mult, -8.0, AL.add)
-            lowest("n4", n1 + 32, None, "T2u")
-        act(a("zsel"), ind(a("yx2", y0, y0 + 2 * M), a("n4u", n1 + 48, n1 + 48 + NA)))
-        mm([(a("pm", 0, M), a("ib"), i, n == 0, n == 2) for n, i in enumerate((a("mh"), a("z"), a("zsel")))])
+            mm([(a("pm", 0, 1), a("bo2"), a("kp", 16 * r + 16 + i, 16 * r + 17 + i), i == 0, i == NA - 1) for i in range(NA)])
+            ts(a("ni", 0, 1), a("pm", 0, 1), 0.25, AL.mult, 1.75, AL.add)
+            ts(a("need", r + 1, r + 2), a("ni", 0, 1), -4.0, AL.mult, a("pm", 0, 1), AL.add)
+            lowest("n4", n1 + 32, lambda i, j: a("T2u", i, j))
+            bound(r + 1)
+            gather_y()
+        act(a("zsel"), ind(a(xp), a("n4u", n1 + 48, n1 + 48 + NA)))
+        mm([(a("pm", 0, M), a("ib" if n else "nq"), i, n == 0, n == 2) for n, i in enumerate((a("mh"), a("z"), a("zsel")))])
         act(a("zt"), a("pm", 0, M), AF.Identity, bias=1.5 * 2.0 ** 24)
         act(a("z"), a("zt"), AF.Identity, scale=0.5, bias=-1.5 * 2.0 ** 23)
-        running("5", "pkb")
-        slot("5", "wi", "wj")
+        running("5", "pka")
+        slot("5", "wi", lambda i, j: a("wj", i, j))
         if not last:
-            mm([(a("pm", 0, M), a("i32"), a("tlj"), True, True)])
+            mm([(a("pd1", 0, M), a("i32"), a("tlj"), True, True)])
             for h in parts("5"):
                 cp(a("wu", *h), a("wj", *h))
                 tt(w16("tc", h), ind(a("id16"), a("wu", *h)), w16("dlt", h), AL.mult)
-                tt(w16("tcol", h), w16("tc", h), w16("pm", h), AL.add)
-            scatter(a("tile"), "T2u", "tcol")
-        if not last:
-            cp(c1("wf"), c1("wj"))
-            tt(a("ohw"), ind(a("wf"), c1("cA")), a("kidx"), AL.is_equal)
-            mm([(a("pf", 0, M), a("i32"), a("W", 16, 240), True, True)])
-            tt(a("e5"), a("pf", 0, M), a("ohw"), AL.mult)
+                tt(w16("tcol", h), w16("tc", h), w16("pd1", h), AL.add)
+            scatter(a("tile"), lambda i, j: a("T2u", i, j), lambda i, j: a("tcol", i, j))
+            tt(a("ohw"), ind(a("wj"), c1("cA")), a("kidx"), AL.is_equal)
+            mm([(bank3("pf"), a("i32"), a("W", 16, 240), True, True)])
+            tt(a("e5"), bank3("pf"), a("ohw"), AL.mult)
             scan(a("sel5"), a("cmask"), a("e5"), AL.mult, AL.add)
-            tt(c1("eq1"), LB, ends("sel5"), AL.subtract)
-            tt(c1("ep"), c1("eq1"), kr14, AL.mult)
-            tt(c1("ee"), c1("ep"), c1("eq1"), AL.subtract)
-            tt(a("l12", 0, NA), ends("sel5"), c1("ep"), AL.add)
-            cp(a("l12u", 0, NA), a("l12", 0, NA))
-            act(a("ynew"), ind(X, a("l12u", 0, NA)))
-            cp(ind(a("rawy"), c1("plu")), a("ynew"))
-            tt(a("tl"), ind(a("ee"), c1("cA")), a("oh"), AL.mult)
+            cp(c1("wwu"), ends("sel5"))
+            act(a("ynew"), ind(X, c1("wwu")))
+            act(c1("ex"), kr14, AF.Identity, scale=-1.0, bias=1.0)
+            tt(c1("eq1"), ends("sel5"), LB, AL.subtract)
+            tt(c1("ee"), c1("eq1"), c1("ex"), AL.mult)
+            tt(a("tl"), ind(a("ee"), c1("cA")), oh, AL.mult)
             mm([(a("pm", 0, M), a("i32"), a("L", 16, 240), True, False), (a("pm", 0, M), a("i32"), a("tl"), False, True)])
             act(a("L", 16, 240), a("pm", 0, M))
-            if r < RO - 2:
-                cp(a("Lu"), ind(a("L", 16, 240), c1("pAK")))
             tt(a("tw"), ind(a("ee"), c1("cA")), a("ohw"), AL.mult)
             mm([(a("pm", 0, M), a("i32"), a("W", 16, 240), True, False), (a("pm", 0, M), a("ni32"), a("tw"), False, True)])
             act(a("W", 16, 240), a("pm", 0, M))
             cp(a("Wu"), ind(a("W", 16, 240), c1("pAK")))
-            tt(a("oh"), ind(a("n4", n1 + 16, n1 + 32), c1("cA")), a("kidx"), AL.is_equal)
+            tt(kb("oh", r + 1), ind(a("n4", n1 + 16, n1 + 32), c1("cA")), a("kidx"), AL.is_equal)
         else:
             ts(c1("k16"), kr14, 16.0, AL.mult)
             tt(c1("bk"), B, c1("k16"), AL.max)
@@ -639,9 +706,9 @@ def build(CY, GA, SC, PE, LAT):
             tt(a("dlt"), a("pd1", 0, M), a("tw"), AL.mult)
             cp(c1("wu"), c1("wj"))
             tt(a("e5"), ind(a("id16"), c1("wu")), a("wsl"), AL.mult)
-            mm([(a("pf", 0, M), a("bo32"), a("e5"), True, True)])
+            mm([(a("pm", 0, M), a("bo32"), a("e5"), True, True)])
             tt(a("tc"), ind(a("id16"), c1("wu")), a("dlt"), AL.mult)
-            tt(a("tl"), a("pf", 0, M), a("mb"), AL.mult)
+            tt(a("tl"), a("pm", 0, M), a("mb"), AL.mult)
             tt(a("ow"), a("tc"), a("pd1", M, 2 * M), AL.add)
             tt(a("ol"), a("tl"), a("pd0", 0, M), AL.add)
             act(a("ob"), ind(a("iot"), a("n4u", n1 + 16, n1 + 16 + NA)))
@@ -679,32 +746,6 @@ def arrange(plans):
             rest[i] = c[i] + lat[0][i] + max([gp + rest[j] for j, gp in succ[i]] + [0.0])
         return rest
 
-    def lay(rest):
-        c0, l0 = cost[0], lat[0]
-        left = [len(p) for p in pred]
-        ready = [0.0] * n
-        free = {e: 0.0 for e in eng}
-        pool = {e: [] for e in eng}
-        for i in range(n):
-            if left[i] == 0:
-                pool[eng[i]].append(i)
-        seq = []
-        for _ in range(n):
-            t, e = min((max(free[e], min(ready[i] for i in p)), e) for e, p in pool.items() if p)
-            same = pool[e]
-            now = max((i for i in same if ready[i] <= t), key=lambda i: rest[i])
-            soon = [i for i in same if t < ready[i] < t + HOLD * c0[now] and rest[i] > rest[now] + c0[now]]
-            pick = max(soon, key=lambda i: rest[i]) if soon else now
-            free[e] = max(t, ready[pick]) + c0[pick]
-            seq.append(pick)
-            same.remove(pick)
-            for j, gp in succ[pick]:
-                ready[j] = max(ready[j], free[e] + l0[pick] + gp)
-                left[j] -= 1
-                if left[j] == 0:
-                    pool[eng[j]].append(j)
-        return seq
-
     def span(seq, k):
         c, l = cost[k], lat[k]
         done = [0.0] * n
@@ -714,41 +755,44 @@ def arrange(plans):
             for d, gp in pred[i]:
                 if done[d] + gp > t:
                     t = done[d] + gp
-            free[eng[i]] = t + c[i]
+            if eng[i] != "R":
+                free[eng[i]] = t + c[i]
             done[i] = t + c[i] + l[i]
         return max(done), done
-
-    def worth(rest):
-        seq = lay(rest)
-        return sum(span(seq, k)[0] for k in range(len(plans))), seq
 
     def pack(prio, back):
         c, l = cost[0], lat[0]
         before, after = (succ, pred) if back else (pred, succ)
         left = [len(p) for p in before]
-        pool = [i for i in range(n) if left[i] == 0]
+        pool = sorted((-prio[i], i) for i in range(n) if left[i] == 0)
         at = [0.0] * n
+        ready = [0.0] * n
         busy = {e: [] for e in eng}
         while pool:
-            i = min(pool, key=lambda j: prio[j])
-            pool.remove(i)
-            if back:
-                t = max([at[d] + c[d] + gp for d, gp in before[i]] + [0.0]) + l[i]
-            else:
-                t = max([at[d] + c[d] + l[d] + gp for d, gp in before[i]] + [0.0])
-            b = busy[eng[i]]
-            k = len(b)
-            while k and b[k - 1][1] > t:
-                k -= 1
-            while k < len(b) and b[k][0] < t + c[i]:
-                t = max(t, b[k][1])
-                k += 1
-            b.insert(k, (t, t + c[i]))
+            i = pool.pop()[1]
+            t, ci = ready[i] + (l[i] if back else 0.0), c[i]
+            if ci:
+                b = busy[eng[i]]
+                k = len(b)
+                while k and b[k - 1][1] > t:
+                    k -= 1
+                while k < len(b) and b[k][0] < t + ci:
+                    if b[k][1] > t:
+                        t = b[k][1]
+                    k += 1
+                b.insert(k, (t, t + ci))
             at[i] = t
+            t += ci + (0.0 if back else l[i])
+            new = False
             for j, gp in after[i]:
+                if t + gp > ready[j]:
+                    ready[j] = t + gp
                 left[j] -= 1
                 if left[j] == 0:
-                    pool.append(j)
+                    pool.append((-prio[j], j))
+                    new = True
+            if new:
+                pool.sort()
         return at
 
     def justify(prio):
@@ -759,43 +803,158 @@ def arrange(plans):
         return sum(span(s, k)[0] for k in range(len(plans))), s, at
 
     rng = np.random.default_rng(7)
-    best, seq = worth(remaining(cost[0]))
-    at = span(seq, 0)[1]
-    at = [at[i] - cost[0][i] - lat[0][i] for i in range(n)]
+    best, seq, at = justify([-t for t in remaining(cost[0])])
     for _ in range(TRIES):
         t0, wide = rng.random() * max(at), rng.choice([3000.0, 8000.0, 20000.0])
         noise = rng.normal(0, rng.choice([300.0, 1000.0, 2500.0]), n)
-        w, s, a2 = justify([at[i] + (float(noise[i]) if t0 <= at[i] < t0 + wide else 0.0) for i in range(n)])
+        if rng.random() < 0.5:
+            prio = [at[i] + (float(noise[i]) if t0 <= at[i] < t0 + wide else 0.0) for i in range(n)]
+        else:
+            i0 = int(rng.integers(n))
+            i1 = i0 + int(rng.choice([3, 10, 30]))
+            prio = [at[i] + (3.0 * float(noise[0]) if i0 <= i < i1 else 0.0) for i in range(n)]
+        w, s, a2 = justify(prio)
         if w <= best:
             best, seq, at = w, s, a2
+
+    def rerun(seq, p0, k, old):
+        c, l = cost[k], lat[k]
+        done = old[:]
+        free = {}
+        for j in range(p0 - 1, -1, -1):
+            i = seq[j]
+            if eng[i] not in free:
+                free[eng[i]] = done[i] - l[i]
+                if len(free) == kinds:
+                    break
+        for j in range(p0, n):
+            i = seq[j]
+            e = eng[i]
+            t = free.get(e, 0.0) if c[i] else 0.0
+            for d, gp in pred[i]:
+                if done[d] + gp > t:
+                    t = done[d] + gp
+            t += c[i]
+            free[e] = t
+            done[i] = t + l[i]
+        return done
+
+    def blocked(seq, k, done):
+        c, l = cost[k], lat[k]
+        before, last = {}, {}
+        for i in seq:
+            before[i] = last.get(eng[i])
+            last[eng[i]] = i
+        i = max(range(n), key=lambda j: done[j])
+        out = []
+        while i is not None:
+            t = done[i] - c[i] - l[i]
+            d = next((d for d, gp in pred[i] if done[d] + gp > t - 0.01), None)
+            if d is None and c[i] and before[i] is not None and t > 0.01:
+                d = before[i]
+                out.append((d, i))
+            i = d
+        return out
+
+    kinds = len(set(eng))
+    need = [{d for d, _ in p} for p in pred]
+    dones = [rerun(seq, 0, k, [0.0] * n) for k in range(len(plans))]
+    now = best = sum(max(d) + EARLY * sum(d) / n for d in dones)
+    top, pairs = seq, []
+    for step in range(MOVES):
+        if not pairs:
+            k = int(rng.integers(len(plans)))
+            pairs = blocked(seq, k, dones[k])
+            place = {i: j for j, i in enumerate(seq)}
+        x, y = pairs.pop(int(rng.integers(len(pairs))))
+        kind = rng.random()
+        up = int(rng.choice([0, 0, 1, 2, 4]))
+        if kind < ANY:
+            x = int(rng.integers(n))
+        if kind < 0.35:
+            y, up = x, int(rng.integers(1, 40))
+        p0, p1 = place[x], place[y]
+        if kind < 0.65:
+            for _ in range(up):
+                p0 = next((j for j in range(p0 - 1, -1, -1) if eng[seq[j]] == eng[y]), p0)
+            take = {y}
+            for j in range(p1, p0 - 1, -1):
+                if seq[j] in take:
+                    take |= need[seq[j]]
+            if seq[p0] in take:
+                continue
+            part = seq[p0:p1 + 1]
+            new = seq[:p0] + [i for i in part if i in take] + [i for i in part if i not in take] + seq[p1 + 1:]
+        else:
+            for _ in range(int(rng.choice([0, 0, 1, 2, 4, 8, 16, 30]))):
+                p1 = next((j for j in range(p1 + 1, n) if eng[seq[j]] == eng[y]), p1)
+            take = {x}
+            for j in range(p0 + 1, p1 + 1):
+                if need[seq[j]] & take:
+                    take.add(seq[j])
+            if y in take:
+                continue
+            part = seq[p0:p1 + 1]
+            new = seq[:p0] + [i for i in part if i not in take] + [i for i in part if i in take] + seq[p1 + 1:]
+        nd = [rerun(new, p0, k, dones[k]) for k in range(len(plans))]
+        w = sum(max(d) + EARLY * sum(d) / n for d in nd)
+        if w <= now + HEAT * (1 - step / MOVES) * -np.log(rng.random() + 1e-9):
+            seq, dones, now, pairs = new, nd, w, []
+            if w < best:
+                best, top = w, new
+    seq = top
     ends_, done = span(seq, 0)
-    order = {}
+    order, closes = {}, {}
     for i in seq:
         order.setdefault(eng[i], []).append(i)
         ops[i]["at"] = done[i] - cost[0][i] - lat[0][i]
+        closes[ops[i]["group"]] = i
+    for group, i in closes.items():
+        if group is not None:
+            name, args, kw = ops[i]["calls"][-1]
+            ops[i]["calls"][-1] = (name, args[:4] + (True,), kw)
     return order, [span(seq, k)[0] for k in range(len(plans))]
 
 
-HOLD, SAME, CROSS = 0.5, 170, 220
+SAME, CROSS = 170, 220
 PLAN = {}
 NE = 8
 
 
 def rank_program(g, core, T, topo):
-    rank = T.rank_of(core)
-    if rank is None:
-        return
+    N = len(T.cores)
+
+    def mask(src, dst, last=False):
+        e = topo.engines(src, dst)
+        return sum(1 << i for i in (e[-NE:] if last else e[:NE]))
+
+    def relay(rank):
+        c = T.cores[rank]
+        free = [k for k in topo.cores_of(c) if T.rank_of(k) is None and topo.die(k) != topo.die(c) and all(topo.may_write(k, d) for d in T.cores)]
+        return free[[k for k in topo.cores_of(c) if T.rank_of(k) is not None].index(c)]
+
     if not PLAN:
         plans = [build(*f) for f in FIGURES]
         PLAN["ops"] = plans[0]
         PLAN["order"], PLAN["end"] = arrange(plans)
     ops, order = PLAN["ops"], PLAN["order"]
-    N = len(T.cores)
+    rank = T.rank_of(core)
+    if rank is None:
+        for i in range(N):
+            if relay(i) == core:
+                hands = [ops[j]["calls"][0][1] for j in order["G"] if ops[j]["calls"][0][0] == "send" and ops[j]["calls"][0][1][3]]
+                for key, src, ways, _ in hands:
+                    to = T.cores[(i + ways[0][0]) % N]
+                    rid, pid, _ = topo.addr(to)
+                    g.wait_ge(T.sem["held_" + key], NE)
+                    g.remote_dma(T[ways[0][1][0]][ways[0][1][1]], T[src[0]][src[1]], T.sem[key], T.sem.sent, pid, rid, mask(core, to))
+                g.wait_ge(T.sem.sent, NE * len(hands))
+        return
     queue = {"V": g.vector, "S": g.scalar, "P": g.tensor, "G": g, "Y": g.sync}
     call = {
         "tensor_copy": g.vector.tensor_copy, "tensor_tensor": g.vector.tensor_tensor, "tensor_scalar": g.vector.tensor_scalar,
         "tensor_tensor_scan": g.vector.tensor_tensor_scan, "memset": g.vector.memset, "transpose": g.vector.transpose,
-        "tensor_reduce": g.vector.tensor_reduce, "activation": g.scalar.activation, "matmul": g.tensor.matmul, "iota": g.iota,
+        "activation": g.scalar.activation, "matmul": g.tensor.matmul, "iota": g.iota,
     }
 
     def real(p):
@@ -805,16 +964,13 @@ def rank_program(g, core, T, topo):
             return real(p[1]).indirect(real(p[2]))
         return T[p[0]][p[1]]
 
-    def peer(msg, r):
-        return T.cores[(rank + HOPS[r]) % N] if msg in ("y", "s") else T.cores[(rank - HOPS[r]) % N]
-
     token = {}
     for eng, lst in order.items():
         c = 0
         for i in lst:
             tag = ops[i]["tag"]
             if tag is not None:
-                token[i] = ("dma%d" % tag[1], 16) if tag[0] == "dma" else (tag[1], NE)
+                token[i] = ("dma%d" % tag[1], 16) if tag[0] == "dma" else (tag[1], NE * tag[2])
             elif ops[i]["calls"][0][0] != "send":
                 c += 1
                 token[i] = ("q" + eng, c)
@@ -831,7 +987,7 @@ def rank_program(g, core, T, topo):
             o = ops[i]
             want = {}
             for d, raw in o["deps"].items():
-                if waits_for(o, ops[d], raw):
+                if d in token and waits_for(o, ops[d], raw):
                     s, c = token[d]
                     want[s] = max(want.get(s, 0), c)
             for s, c in want.items():
@@ -840,12 +996,24 @@ def rank_program(g, core, T, topo):
                     seen[s] = c
             for name, args, kw in o["calls"]:
                 if name == "send":
-                    msg, r, src, dst = args
-                    to = peer(msg, r)
-                    rid, pid, _ = topo.addr(to)
-                    mask = sum(1 << e for e in topo.engines(core, to)[:NE])
-                    g.remote_dma(real(dst), real(src), T.sem["%s%d" % (msg, r)], T.sem.sent, pid, rid, mask)
-                    nsent += NE
+                    key, src, ways, relayed = args
+                    left = "out_" + key if "out_" + key in total else "sent"
+                    nsent += NE * (left == "sent")
+                    if relayed:
+                        to = relay(rank)
+                        rid, pid, _ = topo.addr(to)
+                        g.remote_dma(real(src), real(src), T.sem["held_" + key], T.sem[left], pid, rid, mask(core, to, True))
+                        continue
+                    tos = [T.cores[(rank + hop) % N] for hop, _ in ways]
+                    if len(tos) == 1:
+                        rid, pid, _ = topo.addr(tos[0])
+                        g.remote_dma(real(ways[0][1]), real(src), T.sem[key], T.sem[left], pid, rid, mask(core, tos[0]))
+                    else:
+                        m = mask(core, tos[0])
+                        for to in tos:
+                            m &= topo.mask(core, to)
+                        ids = [DstId(rid=topo.addr(to)[0], pnc=topo.addr(to)[1]) for to in tos]
+                        g.remote_dma_fused([RemoteDMATransfer(dst_ids=ids, dma_engine_mask=m, remote_sem=T.sem[key], srcs=[real(src)], dsts=[real(d) for _, d in ways])], local_sem=T.sem[left])
                     continue
                 fn = q.dma_start if name == "dma_start" else call[name]
                 ins = fn(*[real(p) for p in args], **{k: real(v) for k, v in kw.items()})

import numpy as np
from concourse.bass import DstId, RemoteDMATransfer
from concourse.mybir import dt, AluOpType, AxisListType, ActivationFunctionType

AL = AluOpType
AF = ActivationFunctionType
V, M, RO, NA = 3072, 224, 3, 14
HOPS = [1, 3, 6]
VW = V + 16 + M
VX = VW + M
M7 = 17 * NA
W1 = 65536.0
NV2, NV4, NV5, NV1 = 12, 7, 8, 0
ABS5, REL4 = 1, 0
RC, RC1 = 5, 9
NS, CH1 = 7, 4
DLT_V = False
EW, M3 = 240, 336
XC = 2
BF, F32, I32, U16 = "bfloat16", "float32", "int32", "uint16"

SB = {
    "x": (VW, BF), "xp0": (VX, BF), "xp1": (VX, BF), "xp2": (VX, BF), "tile": (VW, I32), "iot": (VW, F32),
    "lai": (M, I32), "lwi": (M, I32), "bi": (M, I32), "z": (M, BF), "bb": (M, BF), "thf": (4, F32),
    "qi": (4, I32), "qj": (4, I32), "col": (16, F32), "i144": (144, F32), "gm16": (128, F32), "kidx": (M, F32), "k17": (M7, F32),
    "zp": (144, BF), "zn": (144, BF), "z2n": (144, BF), "z8": (144, BF), "bo8": (128, F32), "bo2": (128, BF), "bo32": (128, F32),
    "i32": (128, F32), "ni32": (128, F32), "ib32": (128, F32), "ib": (128, BF), "nib": (128, BF), "nbi": (128, BF), "nq": (128, BF), "mh": (M, BF),
    "kcb": (M, BF), "kc7": (M7, BF), "rst": (M, F32), "rs7": (M7, F32), "cmask": (M, BF), "poison": (M3, F32), "dd0": (M3, F32), "id16": (32, F32),
    "pu3": (32, U16), "rep3": (2, U16), "cA3": (32, U16), "end3": (2, U16), "end7": (4, U16), "l12i": (32, I32), "k16": (16, F32), "bk": (16, F32), "bku": (16, U16),
    "cidx": (16, F32), "t1": (16, F32), "t2": (16, F32), "t3": (16, F32), "ti": (16, I32), "tj": (16, I32),
    "cA": (16, U16), "cS": (16, U16), "pK": (16, U16), "pA": (16, U16), "pAK": (16, U16), "rep4": (4, U16),
    "L": (256, F32), "W": (256, F32), "ssl": (256, F32), "lp": (256, F32), "wp": (256, F32),
    "t12a": (480, F32), "t12b": (480, F32), "t12c": (480, F32), "Lu": (M, U16), "Wu": (M, U16), "oh": (M * RO, BF), "ohw": (M, BF),
    "n4": (64 * (RO + 1), F32), "n4u": (64 * (RO + 1), U16), "n4t": (64, F32), "base4": (64, I32), "delta4": (64, F32), "DP": (48, F32),
    "kp": (16 * (RO + 1), BF), "su": (M, U16), "ed": (EW * RO, U16), "eo": (EW * RO, U16), "xq": (V, BF),
    "rawy": (16 * M, BF), "raws": (16 * M, BF), "D": (16 * M, BF), "D0": (16 * M, BF), "Do": (16 * M, BF),
    "sa": (M, F32), "ywin": (16, F32), "thr16": (M, F32), "xsel": (M, BF),
    "key1": (M7, F32), "run1": (M7, F32), "u1": (M7, F32), "e1": (M7, F32), "sel1": (M7 + 2, F32),
    "key2": (M, F32), "run2": (M, F32), "u2": (M, F32), "e2": (M, F32), "sel2": (M, F32),
    "key5": (M, F32), "run5": (M, F32), "e5": (M, F32), "sel5": (M, F32),
    "bind": (M, BF), "cnt": (M, BF), "nocc": (16, F32), "nd": (16, F32), "need": (4, F32), "need2": (16, F32), "Pu": (16, U16),
    "row": (M3, F32), "eq": (M3, BF), "dsc": (384, F32), "P2": (32, F32), "T2u": (32, U16),
    "ji": (16, I32), "jt": (16, F32), "jt2": (16, F32), "lju": (16, U16), "tlj": (M, F32), "dlt": (M, F32),
    "wi": (16, I32), "wj": (16, I32), "wf": (16, F32), "wu": (16, U16), "wwu": (16, U16), "tc": (M, F32), "tcol": (M, F32),
    "ex": (16, F32), "eq1": (16, F32), "ee": (16, F32), "tl": (M, F32), "tw": (M, F32),
    "nf": (4, F32), "ni": (4, I32), "zsel": (M, BF), "zt": (M, F32),
    "ynew": (M, BF), "mb": (M, F32), "l0": (M, F32), "wsl": (M, F32), "lsl": (M, F32), "ol": (M, F32), "ow": (M, F32), "ob": (M, F32),
}
SHARED = {}
SCRATCH = {}
_fill = {}
for _n, (_w, _d) in SB.items():
    if _w <= 32:
        _o = _fill.get(_d, 0)
        SHARED[_n] = ("small_" + _d, _o)
        _fill[_d] = _o + (_w + 15) // 16 * 16
    else:
        SCRATCH[_n] = ("sbuf", [128, _w], _d)
for _d, _o in _fill.items():
    SCRATCH["small_" + _d] = ("sbuf", [128, _o], _d)
SCRATCH["thi2"] = ("sbuf", [128, 4], I32)
SCRATCH["thb"] = ("sbuf", [128, 4], F32)
SCRATCH["thr"] = ("sbuf", [128, 4 * RO], F32)
for _n in ("m2", "m5", "rawv"):
    SCRATCH[_n] = ("sbuf", [128, M, 16], BF)
SCRATCH["m1"] = ("sbuf", [128, M, 17], BF)
for _n in ("pkb", "pf"):
    SCRATCH[_n] = ("psum", [128, 30, 17], F32)
for _n in ("pd0", "pd1", "pd2", "pd3", "pm", "pka"):
    SCRATCH[_n] = ("psum", [128, 512], F32)
NDMA = 16
RELAYED = ["xc%d" % r for r in range(RO - 1)]
ARRIVE = ["th"] + ["xa%d" % i for i in range(XC)] + ["eo%d" % r for r in range(RO)] + ["xb%d" % r for r in range(RO - 1)] + RELAYED
LEAVE = ["out_xa%d" % i for i in range(XC)]
SEMAPHORES = ["qV", "qS", "qP", "qG", "sent"] + ["dma%d" % i for i in range(NDMA)] + ARRIVE + LEAVE + ["held_" + k for k in RELAYED]
IO = {"xs": [128, V], "sb": [128, V], "la": [128, M], "lw": [128, M], "z0": [128, M], "b0": [8, M], "th": [8, 1],
      "yx": [128, V], "yl": [128, M], "yw": [128, M], "yz": [128, M], "yb": [8, M]}
ALL = slice(None)
FIGURES = [(0.9, 1.56, 3.8, 0.45, 1.2), (0.85, 1.3, 3.0, 0.43, 1.5), (1.15, 1.8, 4.5, 0.58, 1.8)]
HALVES = [(8, NA), (0, 8)]
SPLIT = ""
SETS = {6: ([(0, 4), (1, 8)], [(5, 8), (2, 4), (3, 4)]), 8: ([(0, 4), (1, 4)], [(2, 4), (3, 4)]), 10: ([(0, 4), (1, 4), (2, 8)], [(6, 8), (3, 4)]),
        12: ([(0, 4), (1, 4), (2, 4)], [(3, 4)]), 16: ([(0, 4), (1, 4), (2, 4), (3, 4)], [])}
KEY_S, KEY_P = "1", "25"
THR_PE = False
B4 = "pkb"
TRIES, MOVES, HEAT, ANY, EARLY = 300, 50000, 40.0, 0.2, 1.0


def a(name, lo=None, hi=None, st=None, part=ALL):
    if name in SHARED:
        big, o = SHARED[name]
        return (big, (part, slice(o + (lo or 0), o + (SB[name][0] if hi is None else hi), st)))
    return (name, (part, slice(lo, hi, st)))


def a3(name, i, j):
    return (name, (ALL, i, j))


def ind(win, off):
    return ("*", win, off)


CELLS = {}


def cells(name):
    if name not in CELLS:
        shape = IO[name][1:] if name in IO else SCRATCH[name][1][1:]
        CELLS[name] = np.arange(int(np.prod(shape))).reshape(shape)
    return CELLS[name]


def foot(ap):
    name, idx = ap
    if name not in IO and SCRATCH[name][0] == "psum":
        return cells(name).reshape(-1)
    return cells(name)[idx[1:]].reshape(-1)


def count(ap):
    if ap[0] == "*":
        return 16 * count(ap[2])
    return int(cells(ap[0])[ap[1][1:]].size)


def is_ap(v):
    return isinstance(v, tuple)


def psum(ap):
    return ap[0] in SCRATCH and SCRATCH[ap[0]][0] == "psum"


def narrow(ap):
    return SCRATCH[ap[0]][2] in (BF, U16)


def build(CY, GA, SC, PE, LAT):
    ops = []
    lastw, readers, banks = {}, {}, {}

    def add(eng, calls, outs, ins, cost, lat=0.0, tag=None, after=(), adds=False):
        me = len(ops)
        deps = {d: True for d in after}
        rd, wr = [], []
        for p in ins:
            if is_ap(p):
                rd += [p[1], p[2]] if p[0] == "*" else [p]
        for p in outs:
            if p[0] == "*":
                wr.append(p[1]); rd.append(p[2])
            else:
                wr.append(p)
        group = None
        for b in {p[0] for p in rd + wr if psum(p)}:
            base, more = banks.get(b, ([], []))
            for d in base + ([] if adds else more):
                deps.setdefault(d, False)
            banks[b] = (base, more + [me]) if adds else ([me], [])
            group = base[0] if adds else None
        rd = [p for p in rd if not psum(p)]
        wr = [p for p in wr if not psum(p)]
        for p in rd:
            f = foot(p)
            lw = lastw.get(p[0])
            if lw is not None:
                for d in np.unique(lw[f]):
                    if d >= 0:
                        deps[int(d)] = True
        for p in wr:
            f = foot(p)
            n = cells(p[0]).size
            lw = lastw.setdefault(p[0], np.full(n, -1))
            for d in np.unique(lw[f]):
                if d >= 0:
                    deps[int(d)] = True
            mark = np.zeros(n, bool); mark[f] = True
            left = []
            for (d, rf) in readers.get(p[0], []):
                hit = mark[rf]
                if hit.any():
                    deps[d] = True
                if not hit.all():
                    left.append((d, rf[~hit]))
            readers[p[0]] = left
            lw[f] = me
        for p in rd:
            readers.setdefault(p[0], []).append((me, foot(p)))
        deps.pop(me, None)
        ops.append({"eng": eng, "calls": calls, "deps": deps, "cost": cost, "lat": lat, "tag": tag, "group": group})
        return me

    def vcost(out, ins, plain):
        if out[0] == "*":
            return 50 + count(out) * SC * CY
        if ins[0][0] == "*":
            return 50 + count(out) * GA * CY
        return 30 + max(64, plain) * CY

    def half(*aps):
        return 0.5 if all(p[0] != "*" and narrow(p) for p in aps) else 1.0

    def cp(out, in_):
        return add("V", [("tensor_copy", (out, in_), {})], [out], [in_], vcost(out, [in_], count(out) * half(out, in_)))

    def tt(out, i0, i1, op):
        two = 1.0 if (i0[0] != "*" and (psum(i0) or psum(i1))) else 2.0
        return add("V", [("tensor_tensor", (out, i0, i1, op), {})], [out], [i0, i1], vcost(out, [i0], count(out) * two))

    def ts(out, i0, s1, op0, s2=None, op1=None):
        args = (out, i0, s1, s2, op0) + (() if op1 is None else (op1,))
        return add("V", [("tensor_scalar", args, {})], [out], [i0, s1, s2], vcost(out, [i0], count(out) * half(out, i0)))

    def scan(out, d0, d1, op0, op1):
        return add("V", [("tensor_tensor_scan", (out, d0, d1, 0.0, op0, op1), {})], [out], [d0, d1], vcost(out, [d0], count(out) * half(out, d0, d1)))

    def ms(out, c):
        return add("V", [("memset", (out, c), {})], [out], [], vcost(out, [out], count(out) * half(out)))

    def tr(out, in_):
        return add("V", [("transpose", (out, in_), {})], [out], [in_], vcost(out, [in_], count(out)))

    def act(out, in_, func=AF.Copy, **kw):
        cost = 65 + count(out) * GA * CY if in_[0] == "*" else 65 + max(64, count(out)) * CY
        return add("S", [("activation", (out, in_, func), kw)], [out], [in_] + list(kw.values()), cost)

    def mm(items, adds=False):
        cost = sum(max(64, count(i[2])) * PE * (1 if narrow(i[2]) else 4) for i in items) + 60
        return add("P", [("matmul", i, {}) for i in items], [i[0] for i in items], [i[1] for i in items] + [i[2] for i in items], cost, adds=adds)

    def iota(out, pat, base, cm):
        kw = {} if SCRATCH[out[0]][2] == I32 else {"allow_small_or_imprecise_dtypes": True}
        return add("G", [("iota", (out, pat, base, cm), kw)], [out], [], 130 + 2 * CY * count(out))

    ndma = [0]

    def dma(eng, out, in_, lat, behind=False, after=()):
        ndma[0] += 1
        me = add(eng, [("dma_start", (out, in_), {})], [out], [in_], 60, lat, ("dma", ndma[0] - 1), after)
        if behind:
            ops[me]["behind"] = max(i for i in range(me) if ops[i]["eng"] == eng)
        return me

    def send(key, src, ways, lat, left=0.0, relay=False):
        s = add("G", [("send", (key, src, ways, relay), {})], [], [src], 500)
        if left:
            add("R", [], [], [src], 0, left, ("msg", "out_" + key, 1), after=[s])
        me = add("R", [], [d for _, d in ways], [], 0, lat, ("msg", key, len(ways)), after=[s])
        ops[me]["from"] = key
        return me

    def scatter(win, lst, vals):
        for b in range(NA // 2 - 1, -1, -1):
            cp(ind(win, lst(2 * b, 2 * b + 2)), vals(32 * b, 32 * b + 32))

    def edit(table, msg, r):
        scatter(a(table, 0, VW), lambda i, j: a(msg, EW * r + M + i, EW * r + M + j), lambda i, j: a(msg, EW * r + i, EW * r + j))

    def c1(name):
        return a(name, 0, NA)

    def ends(name):
        return a(name, 15, M, 16)

    def bank3(name, k0=0, k1=16, h=(0, NA)):
        if name == "pka":
            return a(name, 16 * h[0], 16 * h[1])
        return a3(name, slice(*h), slice(k0, k1) if k1 > k0 + 1 else k0)

    def reduce(bank, zw, m, k0, k1):
        mm([(bank3(bank, k0, k1), a(zw, 15 - p, 143 - p), a3(m, slice(p, None, 16), slice(k0, k1) if k1 > k0 + 1 else k0), False, False) for p in range(16)], True)

    turn = [0]

    def diff(ks, plus, minus, func, m, first=0):
        bank = "pd%d" % (first + turn[0] % 2); turn[0] += 1
        n = len(ks)
        it = []
        for i, k in enumerate(ks):
            o = a(bank, i, n * M, n)
            it += [(o, a("ib"), plus(k), True, False), (o, a("nib"), minus(k), False, True)]
        mm(it)
        act(a3(m, ALL, both(ks)), a(bank, 0, n * M), func)

    def both(ks):
        return slice(ks[0], ks[-1] + 1, max(1, ks[-1] - ks[0]))

    def pairs(k0, k1):
        return [list(range(k, min(k + 2, k1))) for k in range(k0, k1, 2)]

    def slots(sets):
        return [k for k0, st in sets for k in range(k0, 16, st)]

    def twos(sets):
        ks = sorted(slots(sets))
        near = [[k, k + 1] for k in ks if k % 2 == 0 and k + 1 in ks]
        far = [k for k in ks if k ^ 1 not in ks]
        return near + [far[i:i + 2] for i in range(0, len(far), 2)]

    def raw(win, lst, sets):
        for ks in twos(sets):
            for k0, n in ([(ks[0], 2)] if ks[-1] == ks[0] + 1 else [(k, 1) for k in ks]):
                act(a("raws", M * k0, M * (k0 + n)), ind(win, a(lst, NA * k0, NA * (k0 + n))))

    def reduce2(zw, m, k0, st):
        mm([(a("pka", k0, M, st), a(zw, 15 - p, 143 - p), a3(m, slice(p, None, 16), slice(k0, 16, st)), False, False) for p in range(16)], True)

    def chunks(k0, k1, n):
        c = -(-(k1 - k0) // n)
        e = [k0 + (k1 - k0) * i // c for i in range(c + 1)] if c else []
        return list(zip(e[:-1], e[1:]))

    def turn16(src, t12):
        tr(a(t12, 0, M), a(src, 16, 240))
        tr(a(t12, M, 480), a(src, 0, 256))

    def gather_y():
        for k0, k1 in chunks(NV1, 16, 2):
            act(a("rawy", M * k0, M * k1), ind(X, a("Lu", NA * k0, NA * k1)))

    def ys(c0, c2, st=1):
        return a("D0", NV4 + 16 * c0, 16 * c2, 16 * st)

    def bound(r):
        act(ys(0, M), ind(X, a("n4u", 64 * r, 64 * r + NA)))
        mm([(a("pm", 0, NA), a("zp", 15 - p, 143 - p), ys(p, M, 16), p == 0, p == 15) for p in range(16)])
        act(c1("ywin"), a("pm", 0, NA))

    def parts(n):
        return HALVES if n in SPLIT else [(0, NA)]

    def w16(name, h, n=16):
        return a(name, n * h[0], n * h[1])

    def e16(name, h, n=16):
        return a(name, n * h[0] + n - 1, n * h[1], n)

    def running(n, bank, w=16):
        for h in parts(n):
            if n not in KEY_P:
                (act if n in KEY_S else cp)(w16("key" + n, h, w), bank3(bank, 0, w, h))
        for h in parts(n):
            scan(w16("run" + n, h, w), w16("rst" if w == 16 else "rs7", h, w), bank3(bank, 0, w, h) if n in KEY_P else w16("key" + n, h, w), AL.min, AL.max)

    def choose(n, bank, w=16, between=lambda: None):
        for h in parts(n):
            tt(w16("u" + n, h, w), w16("run" + n, h, w), bank3(bank, 0, w, h), AL.subtract)
        between()
        for h in parts(n):
            tt(w16("e" + n, h, w), bank3("pf", 0, w, h), w16("u" + n, h, w), AL.subtract)
        for h in parts(n):
            scan(w16("sel" + n, h, w), w16("u" + n, h, w), w16("e" + n, h, w), AL.min, AL.max)

    def slot(n, ti, tj, w=16):
        for h in parts(n):
            ts(a(ti, *h), e16("run" + n, h, w), -1.0 / 4096, AL.mult, 131072.0, AL.add)
            ts(tj(*h), a(ti, *h), 15, AL.bitwise_and)

    LW = 8 if "l" in SPLIT else 16

    def lowest(pw, p14, out):
        for a0, a1 in parts("l"):
            n3, c0, c2 = 3 * (a1 - a0) // 2, 24 * a0, 24 * a1
            win = a(pw, p14 + a0, p14 + a0 + LW)
            cp(a("pu3", 2 * a0, 2 * a0 + 2 * LW), ind(win, a("rep3", 0, LW // 8)))
            tt(a("row", c0, c2), ind(a("iot"), a("pu3", 2 * a0, 2 * a0 + n3)), a("poison", c0, c2), AL.add)
            tt(a("eq", c0, c2), ind(win, a("cA3", 0, n3)), a("row", c0, c2), AL.is_equal)
            scan(a("dsc", c0, c2), a("dd0", c0, c2), a("eq", c0, c2), AL.mult, AL.max)
            tt(a("P2", 2 * a0, 2 * a0 + 16), ind(a("dsc", c0, c0 + 24 * LW), a("end3", 0, 1)), a(pw, p14 + a0, p14 + a0 + 16), AL.max)
            cp(out(a0, a1), a("P2", 2 * a0, a0 + a1))

    X = a("x", 0, V)
    P8 = slice(0, 8)
    whole = lambda n: (n, (ALL, ALL))
    piece = lambda n, i: a(n, V // XC * i, V // XC * (i + 1))
    dma("S", a("thi2", 0, 1, part=P8), whole("th"), 2000)
    for i in range(XC):
        dma("Y", piece("x", i), piece("xs", i), 2200 + 2300 * (i + 1) // XC, i > 0)
    tile = dma("Y", a("tile", 0, V), whole("sb"), 11000, True)
    dma("S", a("lai"), whole("la"), 2500)
    dma("S", a("bi", part=P8), whole("b0"), 2000)
    dma("S", a("z"), whole("z0"), 2500)
    dma("S", a("lwi"), whole("lw"), 2500)
    for i in range(XC):
        send("xa%d" % i, piece("x", i), [(-HOPS[0], piece("xp0", i))], 7000, 6000)
    dma("Y", a("xq"), X, 4500, after=[tile])
    iota(a("qi", 0, 1), [[0, 1]], 0, 1)
    iota(a("i144"), [[1, 144]], 0, 0)
    iota(a("gm16"), [[16, 8], [0, 16]], 0, 0)
    iota(a("kidx"), [[0, NA], [1, 16]], 0, 0)
    iota(a("k17"), [[0, NA], [1, 17]], 0, 0)
    for i in range(8):
        iota(a("iot", VW // 8 * i, VW // 8 * (i + 1)), [[1, VW // 8]], VW // 8 * i, 0)
    cols = ["q", "p", "g16", "g16e", "q16", "q16e", "e", "fl", "ms"]
    C = {n: a("col", i, i + 1) for i, n in enumerate(cols)}
    c14 = a("i144", 0, NA)
    spare = a("DP", 0, NA)
    cp(C["q"], a("qi", 0, 1))
    ts(a("qj", 0, 1), a("qi", 0, 1), 15, AL.bitwise_and)
    cp(C["p"], a("qj", 0, 1))
    tt(C["g16"], C["q"], C["p"], AL.subtract)
    ts(C["g16e"], C["g16"], 15.0, AL.add)
    ts(C["q16"], C["q"], 16.0, AL.mult)
    ts(C["q16e"], C["q"], 16.0, AL.mult, 15.0, AL.add)
    ts(a("qj", 1, 2), a("qi", 0, 1), 4, AL.arith_shift_right, 1, AL.bitwise_and)
    cp(C["e"], a("qj", 1, 2))
    tt(a("qi", 1, 2), C["p"], C["e"], AL.add)
    ts(a("qj", 2, 3), a("qi", 1, 2), 1, AL.bitwise_and)
    ts(C["fl"], a("qj", 2, 3), 240.0, AL.mult)
    ts(c1("cidx"), c14, 16.0, AL.mult, C["p"], AL.add)
    iota(a("DP", NA, 48), [[0, 48 - NA]], 0, 0)
    ts(spare, c1("cidx"), V + 16.0, AL.add)
    cp(c1("cA"), c14)
    ts(c1("ti"), c14, C["e"], AL.add)
    ts(c1("tj"), c1("ti"), 1, AL.bitwise_and)
    ts(c1("t1"), c1("tj"), 240.0, AL.mult)
    tt(c1("t2"), c1("t1"), c1("cidx"), AL.add)
    cp(c1("pA"), c1("t2"))
    ts(c1("ji"), c1("cidx"), -6.5, AL.add, 1.0 / 14, AL.mult)
    ts(c1("jt"), c1("ji"), -223.0, AL.mult)
    ts(c1("jt2"), c1("cidx"), 16.0, AL.mult)
    tt(c1("t3"), c1("jt"), c1("jt2"), AL.add)
    cp(c1("pAK"), c1("t3"))
    ts(c1("pK"), c1("t3"), C["fl"], AL.add)
    ts(a("rep4"), a("i144", 0, 4), 0.0, AL.mult, C["p"], AL.add)
    ts(a("zp"), a("i144"), C["g16e"], AL.is_equal, W1, AL.mult)
    for n, w in (("zn", -1.0), ("z2n", -2.0)):
        act(a(n), a("zp"), AF.Identity, scale=w)
    ts(a("z8"), a("i144"), C["q16e"], AL.is_equal)
    ts(a("bo8"), a("gm16"), C["q16"], AL.is_equal)
    ts(a("bo2"), a("gm16"), C["g16"], AL.is_equal, 2.0, AL.mult)
    ts(a("i32"), a("i144", 0, 128), C["q"], AL.is_equal)
    for n, w in (("ib", 1.0), ("nib", -1.0), ("nbi", -2.0 ** 29), ("nq", -0.25), ("ni32", -1.0), ("ib32", -4096.0)):
        act(a(n), a("i32"), AF.Identity, scale=w)
    act(a("bo32"), a("bo2"), AF.Identity, scale=0.5)
    act(a("kcb"), a("kidx"), AF.Identity, scale=-4096.0)
    act(a("kc7"), a("k17"), AF.Identity, scale=-4096.0)
    iota(a("kc7", 16, M7, 17), [[0, NA]], 0, 0)
    act(a("rst"), a("kidx"), AF.Identity, scale=2.0 ** 32, bias=-2.0 ** 31)
    act(a("rs7"), a("k17"), AF.Identity, scale=2.0 ** 32, bias=-2.0 ** 31)
    act(a("cmask"), a("kidx"), AF.Sign)
    iota(a("row"), [[0, 21], [1, 16]], 0, 0)
    ts(a("poison"), a("row"), C["p"], AL.is_ge, 8192.0, AL.mult)
    for b in range(NA // 2):
        iota(a("poison", 48 * b + 16, 48 * b + 32), [[0, 16]], 0, 0)
    iota(a("dd0"), [[0, M3]], 1, 0)
    iota(a("dd0", 0, M3, 48), [[0, 7]], 0, 0)
    iota(a("dd0", 16, M3, 48), [[0, 7]], 0, 0)
    act(a("dd0", 15, M3, 48), a("DP", 0, NA, 2))
    act(a("dd0", 47, M3, 48), a("DP", 1, NA, 2))
    ts(a("nf", 0, 1), C["p"], 2.0 / 3, AL.mult, -1.0 / 3, AL.add)
    ts(a("wi", 0, 2), a("i144", 0, 2), 32.0 / 3, AL.mult, a("nf", 0, 1), AL.add)
    ts(a("rep3", 0, 2), a("wi", 0, 2), LW - 1.0, AL.min)
    iota(a("dsc", M3, 384), [[0, 384 - M3]], 0, 0)
    ts(a("l12i", 0, 21), a("i144", 0, 21), 2.0 / 3, AL.mult)
    cp(a("cA3", 0, 21), a("l12i", 0, 21))
    ts(a("qj", 3, 4), a("qi", 0, 1), 1, AL.bitwise_and)
    ts(a("nf", 1, 2), a("qj", 3, 4), 8.0, AL.mult, 15.0, AL.add)
    ts(a("nf", 2, 3), C["p"], 24.0, AL.mult, a("nf", 1, 2), AL.add)
    ts(a("end3", 0, 1), a("nf", 2, 3), 24.0 * LW - 1, AL.min)
    ts(a("nf", 3, 4), C["p"], 17.0, AL.mult, 16.0, AL.add)
    ts(a("end7"), a("i144", 0, 4), a("nf", 3, 4), AL.max, M7 - 1.0, AL.min)
    ts(a("id16"), a("i144", 0, 32), C["p"], AL.is_equal)
    fill = lambda p, c=0: iota(p, [[0, count(p)]], c, 0)
    fill(a("mh"), 2)
    for n in ["x", "tile"] + ["xp%d" % r for r in range(RO)]:
        fill(a(n, V, VW))
    for i in (NA, NA + 1):
        ms(a("ed", M + i, EW * RO, EW), 0)
    for n in ("L", "W", "ssl", "lp", "wp"):
        fill(a(n, 0, 16))
        fill(a(n, 240, 256))
    fill(a("kp"), 1)
    for p in (a("ywin"), a("wj"), a("ee"), a("n4", 0, 64), a("base4", 48 + NA, 64)):
        fill(p)
    ts(a("base4", 48, 48 + NA), c1("cidx"), float(VW), AL.add)
    for i in range(4):
        ms(a("D0", 4 * M * i, 4 * M * (i + 1)), 0.0)
    ms(a("D0", 0, None, 16), -1024.0)
    cp(a("thf", 0, 1, part=P8), a("thi2", 0, 1, part=P8))
    mm([(a("pm", 0, 1), a("bo8", part=P8), a("thf", 0, 1, part=P8), True, True)])
    ts(a("thb", 0, 1), a("pm", 0, 1), -W1, AL.mult, 63488.0, AL.add)
    send("th", a("thb", 0, 1), [(-HOPS[r], a("thr", 4 * r, 4 * r + 1)) for r in range(RO)], 5000)
    cp(a("lp", 16, 240), a("lai"))
    turn16("lp", "t12a")
    cp(a("Lu"), ind(a("t12a"), c1("pK")))
    cp(a("L", 16, 240), ind(a("t12a"), c1("pA")))
    cp(a("bb", part=P8), a("bi", part=P8))
    mm([(a("pm", 0, NA), a("z8", 15 - p, 143 - p, part=P8), a("bb", p, M, 16, part=P8), p == 0, p == 15) for p in range(16)])
    cp(a("n4", 16, 16 + NA), a("pm", 0, NA))
    tt(a("oh", 0, M), ind(a("n4", 16, 32), c1("cA")), a("kidx"), AL.is_equal)
    tt(a("tl"), a("oh", 0, M), a("L", 16, 240), AL.mult)
    scan(a("tw"), a("cmask"), a("tl"), AL.mult, AL.add)
    cp(a("n4", 0, NA), ends("tw"))
    cp(a("n4u", 0, 64), a("n4", 0, 64))
    cp(a("wp", 16, 240), a("lwi"))
    turn16("wp", "t12b")
    cp(a("Wu"), ind(a("t12b"), c1("pK")))
    act(a("W", 16, 240), ind(a("t12b"), c1("pA")))
    bound(0)
    gather_y()

    for r in range(RO):
        last = r == RO - 1
        n0, n1 = 64 * r, 64 * (r + 1)
        LB, LBu, B = a("n4", n0, n0 + NA), a("n4u", n0, n0 + NA), a("n4", n0 + 16, n0 + 16 + NA)
        xp = "xp%d" % r
        XP = a(xp, 0, V)
        y, oh, thr = ys(0, M), a("oh", M * r, M * (r + 1)), a("thr", 4 * r, 4 * r + 1)
        need = a("need", r, r + 1) if r else -8.0
        sl = lambda name, k, n=1: a(name, NA * k, NA * (k + n))
        kb = lambda name, k, n=1: a(name, M * k, M * (k + n))
        cp(a("ssl", 16, 240), ind(a("tile"), LBu))
        turn16("ssl", "t12c")
        cp(a("su"), ind(a("t12c"), c1("pK")))
        act(a("sa"), ind(a("t12c"), c1("pA")))
        for ks in pairs(NV1, 16):
            diff(ks, lambda k: kb("rawy", k), lambda k: a("z"), AF.Abs, "m1", 2)
        mm([(bank3("pkb", 0, 17), a("ib"), a("kc7"), True, False)])
        for k in range(NV1):
            tt(a3("rawv", ALL, k), ind(a("xq") if r else X, sl("Lu", k)), a("z"), AL.subtract)
        if r == 1:
            cp(a("Lu"), ind(a("L", 16, 240), c1("pAK")))
        for k0, k1 in chunks(0, NV1, CH1):
            ts(a3("m1", ALL, slice(k0, k1)), a3("rawv", ALL, slice(k0, k1)), 0.0, AL.max)
        if NV1:
            reduce("pkb", "zp", "rawv", 0, NV1)
            reduce("pkb", "z2n", "m1", 0, NV1)
        it = [(bank3("pkb"), a("nbi"), oh, False, False), (bank3("pkb", 16, 17), a("nbi"), a("kp", 16 * r, 16 * r + NA), False, False)]
        if r:
            it += [(bank3("pkb"), a("nbi"), kb("oh", r - 1), False, False), (bank3("pkb", 16, 17), a("ib32"), a("n4", n0 - 48, n0 - 48 + NA), False, False)]
        mm(it, True)
        if r:
            diff([16], lambda k: a("ynew"), lambda k: a("z"), AF.Abs, "m1", 2)
        for k0, k1 in chunks(NV1, 17 if r else 16, RC1):
            reduce("pkb", "zn", "m1", k0, k1)
        if not THR_PE:
            act(a("thr16"), ind(a("ywin"), c1("cA")))
        mm([(a("pka", 0, M), a("ib"), a("kcb"), True, False)])
        cv, cs = SETS[NV2]
        for k in slots(cv):
            tt(a3("m2", ALL, k), ind(XP, sl("su", k)), y, AL.min)
        raw(XP, "su", cs)
        for ks in twos(cs):
            diff(ks, lambda k: y, lambda k: kb("raws", k), AF.Relu, "m2")
        for c in cv:
            reduce2("zp", "m2", *c)
        if cs:
            mm([(a("pka", k, M, 16), a("i32"), c1("ywin"), False, False) for k in slots(cs)], True)
        for c in cs:
            reduce2("zn", "m2", *c)
        running("2", "pka")
        mm([(bank3("pf"), a("i32"), a("sa"), True, True)])
        choose("2", "pka", 16, lambda: [act(w16("bind", h), w16("pka" if "2" in KEY_P else "key2", h), AF.Sign, bias=thr) for h in parts("c")])
        for h in parts("c"):
            scan(w16("cnt", h), w16("cmask", h), w16("bind", h), AL.mult, AL.add)
            ts(a("nd", *h), e16("cnt", h), need, AL.is_lt, float(V), AL.mult)
        for h in parts("2"):
            tt(a("DP", 16 + h[0], 16 + h[1]), e16("sel2", h), a("nd", *h), AL.max)
        ts(c1("need2"), c1("nd"), need, AL.add)
        e0 = EW * r
        for h, bank in zip(parts("x"), (lambda h: w16("pd0", h), lambda h: w16("pd1", h))):
            cp(a("Pu", *h), e16("sel2", h))
            act(w16("xsel", h), ind(XP, a("Pu", *h)))
            mm([(bank(h), a("ib"), w16("xsel", h), True, False), (bank(h), a("nq"), ys(16 * h[0], 16 * h[1]), False, True)])
            ts(a("ed", e0 + 16 * h[0], e0 + 16 * h[1]), bank(h), 0.375, AL.add)
        lowest("DP", 16, lambda i, j: a("ed", e0 + M + i, e0 + M + j))
        ed = a("ed", e0, e0 + EW)
        send("eo%d" % r, ed, [(HOPS[r], a("eo", e0, e0 + EW))], 3000 * LAT)
        edit(xp, "ed", r)
        if not last:
            for key, i in (("xb", 0), ("xc", 1)):
                cut = lambda n: a(n, V // 2 * i, V // 2 * (i + 1))
                send(key + str(r), cut(xp), [(HOPS[r] - HOPS[r + 1], cut("xp%d" % (r + 1)))], 9000 + 4000 * i, 0, i == 1)
        running("1", "pkb", 17)
        mm([(bank3("pf"), a("i32"), a("L", 16, 240), True, False), (bank3("pf", 16, 17), a("i32"), ends("sel5") if r else spare, False, True)])
        choose("1", "pkb", 17)
        cp(a("base4", 0, 48), ind(a("sel1", 0, M7), a("end7", 0, 3)))
        slot("1", "ji", lambda i, j: a("base4", 16 + i, 16 + j), 17)
        tt(a("delta4", 0, 32), a("n4", n0, n0 + 32), a("base4", 0, 32), AL.subtract)
        tt(a("delta4", 32, 64), a("DP", 0, 32), a("base4", 32, 64), AL.subtract)
        cp(c1("lju"), e16("sel1", (0, NA), 17))
        act(a(xp, VW, VX), ind(a("xq"), c1("lju")))
        if not last:
            cp(a("tlj"), ind(a("tile"), c1("lju")))
            if DLT_V:
                tt(a("dlt"), a("ssl", 16, 240), a("tlj"), AL.subtract)
            else:
                mm([(a("pm", 0, M), a("i32"), a("ssl", 16, 240), True, False), (a("pm", 0, M), a("ni32"), a("tlj"), False, True)])
                act(a("dlt"), a("pm", 0, M))
        else:
            turn16("L", "t12a")
            act(a("lsl"), ind(a("t12a"), c1("pA")))
            turn16("W", "t12b")
            act(a("wsl"), ind(a("t12b"), c1("pA")))
            tt(a("tw"), ind(a("iot"), LBu), a("wsl"), AL.subtract)
        edit("x", "eo", r)
        if last:
            dma("Y", whole("yx"), X, 4500)
        else:
            dma("Y", a("xq"), X, 4500)
        for k in range(NV4):
            tt(a("D", k, None, 16), ind(XP, sl("su", k)), y, AL.subtract)
        for k in range(NV4, 16):
            act(a("D", k, None, 16), ind(XP, sl("su", k)))
        for k in range(NV4):
            if k < REL4:
                act(a3("m2", ALL, k), a("D", k, None, 16), AF.Relu, scale=-1.0)
            else:
                ts(a3("m2", ALL, k), a("D", k, None, 16), -1.0, AL.mult, 0.0, AL.max)
        for ks in pairs(NV4, 16):
            diff(ks, lambda k: y, lambda k: a("D", k, None, 16), AF.Relu, "m2")
        for c0, c2 in chunks(0, M, M // NS):
            scan(a("Do", 16 * c0, 16 * c2), a("D0", 16 * c0, 16 * c2), a("D", 16 * c0, 16 * c2), AL.add, AL.max)
        if THR_PE:
            mm([(a(B4, k, M, 16) if B4 == "pka" else bank3(B4, k, k + 1), a("i32"), c1("ywin"), k == 0, False) for k in range(16)])
        else:
            mm([(bank3(B4), a("i32"), a("thr16"), True, False)])
        if B4 == "pka":
            for j in range(4):
                mm([(a(B4, j, M, 4), a("zn", 15 - p, 143 - p), a3("m2", slice(p, None, 16), slice(4 * j, 4 * j + 4)), False, False) for p in range(16)], True)
        else:
            for k0, k1 in [(0, NV4)] + chunks(NV4, 16, RC):
                reduce(B4, "zn", "m2", k0, k1)
        act(a("bind"), bank3(B4), AF.Sign, bias=thr)
        scan(a("cnt"), a("cmask"), a("bind"), AL.mult, AL.add)
        kr, kr14 = a("kp", 16 * r + 16, 16 * r + 32), a("kp", 16 * r + 16, 16 * r + 16 + NA)
        tt(kr14, ends("cnt"), c1("need2"), AL.is_ge)
        fr = a("Do", 15, None, 16)
        cv, cs = SETS[NV5]
        raw(X, "Wu", cs)
        for k in slots(cv):
            tt(a3("rawv", ALL, k), ind(X, sl("Wu", k)), fr, AL.subtract)
        held = list(zip(["pd2", "pd3", "pd0", "pd1"] * 2, twos(cs)))
        pre = lambda bank, ks: mm([(a(bank, i, len(ks) * M, len(ks)), a("ib"), kb("raws", k), i == 0, False) for i, k in enumerate(ks)])
        for bank, ks in held[:4]:
            pre(bank, ks)
        for n, (bank, ks) in enumerate(held):
            if n >= 4:
                pre(bank, ks)
            mm([(a(bank, i, len(ks) * M, len(ks)), a("nib"), fr, False, i == len(ks) - 1) for i in range(len(ks))])
            act(a3("m5", ALL, both(ks)), a(bank, 0, len(ks) * M), AF.Abs)
        mm([(a("pka", 0, M), a("ib"), a("kcb"), True, False)])
        for n, (k0, st) in enumerate(cv):
            if n < ABS5:
                act(a3("m5", ALL, slice(k0, 16, st)), a3("rawv", ALL, slice(k0, 16, st)), AF.Abs)
            else:
                ts(a3("m5", ALL, slice(k0, 16, st)), a3("rawv", ALL, slice(k0, 16, st)), 0.0, AL.max)
        for c in cs:
            reduce2("zn", "m5", *c)
        for n, c in enumerate(cv):
            if n >= ABS5:
                reduce2("zp", "rawv", *c)
            reduce2("zn" if n < ABS5 else "z2n", "m5", *c)
        tt(a("n4t"), ind(kr, a("rep4")), a("delta4"), AL.mult)
        tt(a("n4", n1, n1 + 64), a("n4t"), a("base4"), AL.add)
        cp(a("n4u", n1, n1 + 64), a("n4", n1, n1 + 64))
        if not last:
            mm([(a("pm", 0, 1), a("bo2"), a("kp", 16 * r + 16 + i, 16 * r + 17 + i), i == 0, i == NA - 1) for i in range(NA)])
            ts(a("ni", 0, 1), a("pm", 0, 1), 0.25, AL.mult, 1.75, AL.add)
            ts(a("need", r + 1, r + 2), a("ni", 0, 1), -4.0, AL.mult, a("pm", 0, 1), AL.add)
            lowest("n4", n1 + 32, lambda i, j: a("T2u", i, j))
            bound(r + 1)
            gather_y()
        act(a("zsel"), ind(a(xp), a("n4u", n1 + 48, n1 + 48 + NA)))
        mm([(a("pm", 0, M), a("ib" if n else "nq"), i, n == 0, n == 2) for n, i in enumerate((a("mh"), a("z"), a("zsel")))])
        act(a("zt"), a("pm", 0, M), AF.Identity, bias=1.5 * 2.0 ** 24)
        act(a("z"), a("zt"), AF.Identity, scale=0.5, bias=-1.5 * 2.0 ** 23)
        running("5", "pka")
        slot("5", "wi", lambda i, j: a("wj", i, j))
        if not last:
            mm([(a("pd1", 0, M), a("i32"), a("tlj"), True, True)])
            for h in parts("5"):
                cp(a("wu", *h), a("wj", *h))
                tt(w16("tc", h), ind(a("id16"), a("wu", *h)), w16("dlt", h), AL.mult)
                tt(w16("tcol", h), w16("tc", h), w16("pd1", h), AL.add)
            scatter(a("tile"), lambda i, j: a("T2u", i, j), lambda i, j: a("tcol", i, j))
            tt(a("ohw"), ind(a("wj"), c1("cA")), a("kidx"), AL.is_equal)
            mm([(bank3("pf"), a("i32"), a("W", 16, 240), True, True)])
            tt(a("e5"), bank3("pf"), a("ohw"), AL.mult)
            scan(a("sel5"), a("cmask"), a("e5"), AL.mult, AL.add)
            cp(c1("wwu"), ends("sel5"))
            act(a("ynew"), ind(X, c1("wwu")))
            act(c1("ex"), kr14, AF.Identity, scale=-1.0, bias=1.0)
            tt(c1("eq1"), ends("sel5"), LB, AL.subtract)
            tt(c1("ee"), c1("eq1"), c1("ex"), AL.mult)
            tt(a("tl"), ind(a("ee"), c1("cA")), oh, AL.mult)
            mm([(a("pm", 0, M), a("i32"), a("L", 16, 240), True, False), (a("pm", 0, M), a("i32"), a("tl"), False, True)])
            act(a("L", 16, 240), a("pm", 0, M))
            tt(a("tw"), ind(a("ee"), c1("cA")), a("ohw"), AL.mult)
            mm([(a("pm", 0, M), a("i32"), a("W", 16, 240), True, False), (a("pm", 0, M), a("ni32"), a("tw"), False, True)])
            act(a("W", 16, 240), a("pm", 0, M))
            cp(a("Wu"), ind(a("W", 16, 240), c1("pAK")))
            tt(kb("oh", r + 1), ind(a("n4", n1 + 16, n1 + 32), c1("cA")), a("kidx"), AL.is_equal)
        else:
            ts(c1("k16"), kr14, 16.0, AL.mult)
            tt(c1("bk"), B, c1("k16"), AL.max)
            cp(c1("bku"), c1("bk"))
            act(a("mb"), ind(a("id16"), c1("bku")))
            act(a("tl"), a("mb"), AF.Identity, scale=-1.0, bias=1.0)
            tt(a("l0"), a("lsl"), a("tl"), AL.mult)
            mm([(a("pd0", 0, M), a("i32"), a("l0"), True, True)])
            mm([(a("pd1", 0, M), a("bo32"), a("mb"), True, True), (a("pd1", M, 2 * M), a("i32"), a("wsl"), True, True)])
            tt(a("dlt"), a("pd1", 0, M), a("tw"), AL.mult)
            cp(c1("wu"), c1("wj"))
            tt(a("e5"), ind(a("id16"), c1("wu")), a("wsl"), AL.mult)
            mm([(a("pm", 0, M), a("bo32"), a("e5"), True, True)])
            tt(a("tc"), ind(a("id16"), c1("wu")), a("dlt"), AL.mult)
            tt(a("tl"), a("pm", 0, M), a("mb"), AL.mult)
            tt(a("ow"), a("tc"), a("pd1", M, 2 * M), AL.add)
            tt(a("ol"), a("tl"), a("pd0", 0, M), AL.add)
            act(a("ob"), ind(a("iot"), a("n4u", n1 + 16, n1 + 16 + NA)))
            dma("Y", whole("yb"), a("ob", part=slice(0, 128, 16)), 2000)
            dma("Y", whole("yz"), a("z"), 2200)
            dma("Y", whole("yw"), a("ow"), 2200)
            dma("S", whole("yl"), a("ol"), 2200)
    return ops


def waits_for(o, d, raw):
    if d["tag"] is not None or o["eng"] != d["eng"]:
        return True
    return raw and o["eng"] != "P"


def arrange(plans):
    ops = plans[0]
    n = len(ops)
    eng = [o["eng"] for o in ops]
    cost = [[o["cost"] for o in pl] for pl in plans]
    lat = [[o["lat"] for o in pl] for pl in plans]
    pred = [[(d, 0 if not waits_for(o, ops[d], raw) else (SAME if o["eng"] == eng[d] else CROSS)) for d, raw in o["deps"].items()] for o in ops]
    for i, o in enumerate(ops):
        if "behind" in o:
            pred[i].append((o["behind"], -o["lat"] - lat[0][o["behind"]]))
    succ = [[] for _ in range(n)]
    for i in range(n):
        for d, gp in pred[i]:
            succ[d].append((i, gp))

    def remaining(c):
        rest = [0.0] * n
        for i in range(n - 1, -1, -1):
            rest[i] = c[i] + lat[0][i] + max([gp + rest[j] for j, gp in succ[i]] + [0.0])
        return rest

    def span(seq, k):
        c, l = cost[k], lat[k]
        done = [0.0] * n
        free = {e: 0.0 for e in eng}
        for i in seq:
            t = free[eng[i]]
            for d, gp in pred[i]:
                if done[d] + gp > t:
                    t = done[d] + gp
            if eng[i] != "R":
                free[eng[i]] = t + c[i]
            done[i] = t + c[i] + l[i]
        return max(done), done

    def pack(prio, back):
        c, l = cost[0], lat[0]
        before, after = (succ, pred) if back else (pred, succ)
        left = [len(p) for p in before]
        pool = sorted((-prio[i], i) for i in range(n) if left[i] == 0)
        at = [0.0] * n
        ready = [0.0] * n
        busy = {e: [] for e in eng}
        while pool:
            i = pool.pop()[1]
            t, ci = ready[i] + (l[i] if back else 0.0), c[i]
            if ci:
                b = busy[eng[i]]
                k = len(b)
                while k and b[k - 1][1] > t:
                    k -= 1
                while k < len(b) and b[k][0] < t + ci:
                    if b[k][1] > t:
                        t = b[k][1]
                    k += 1
                b.insert(k, (t, t + ci))
            at[i] = t
            t += ci + (0.0 if back else l[i])
            new = False
            for j, gp in after[i]:
                if t + gp > ready[j]:
                    ready[j] = t + gp
                left[j] -= 1
                if left[j] == 0:
                    pool.append((-prio[j], j))
                    new = True
            if new:
                pool.sort()
        return at

    def justify(prio):
        at = pack(prio, False)
        at = pack([-(at[i] + cost[0][i]) for i in range(n)], True)
        at = pack([-(at[i] + cost[0][i]) for i in range(n)], False)
        s = sorted(range(n), key=lambda i: (at[i], i))
        return sum(span(s, k)[0] for k in range(len(plans))), s, at

    rng = np.random.default_rng(7)
    best, seq, at = justify([-t for t in remaining(cost[0])])
    for _ in range(TRIES):
        t0, wide = rng.random() * max(at), rng.choice([3000.0, 8000.0, 20000.0])
        noise = rng.normal(0, rng.choice([300.0, 1000.0, 2500.0]), n)
        if rng.random() < 0.5:
            prio = [at[i] + (float(noise[i]) if t0 <= at[i] < t0 + wide else 0.0) for i in range(n)]
        else:
            i0 = int(rng.integers(n))
            i1 = i0 + int(rng.choice([3, 10, 30]))
            prio = [at[i] + (3.0 * float(noise[0]) if i0 <= i < i1 else 0.0) for i in range(n)]
        w, s, a2 = justify(prio)
        if w <= best:
            best, seq, at = w, s, a2

    def rerun(seq, p0, k, old):
        c, l = cost[k], lat[k]
        done = old[:]
        free = {}
        for j in range(p0 - 1, -1, -1):
            i = seq[j]
            if eng[i] not in free:
                free[eng[i]] = done[i] - l[i]
                if len(free) == kinds:
                    break
        for j in range(p0, n):
            i = seq[j]
            e = eng[i]
            t = free.get(e, 0.0) if c[i] else 0.0
            for d, gp in pred[i]:
                if done[d] + gp > t:
                    t = done[d] + gp
            t += c[i]
            free[e] = t
            done[i] = t + l[i]
        return done

    def blocked(seq, k, done):
        c, l = cost[k], lat[k]
        before, last = {}, {}
        for i in seq:
            before[i] = last.get(eng[i])
            last[eng[i]] = i
        i = max(range(n), key=lambda j: done[j])
        out = []
        while i is not None:
            t = done[i] - c[i] - l[i]
            d = next((d for d, gp in pred[i] if done[d] + gp > t - 0.01), None)
            if d is None and c[i] and before[i] is not None and t > 0.01:
                d = before[i]
                out.append((d, i))
            i = d
        return out

    kinds = len(set(eng))
    need = [{d for d, _ in p} for p in pred]
    dones = [rerun(seq, 0, k, [0.0] * n) for k in range(len(plans))]
    now = best = sum(max(d) + EARLY * sum(d) / n for d in dones)
    top, pairs = seq, []
    for step in range(MOVES):
        if not pairs:
            k = int(rng.integers(len(plans)))
            pairs = blocked(seq, k, dones[k])
            place = {i: j for j, i in enumerate(seq)}
        x, y = pairs.pop(int(rng.integers(len(pairs))))
        kind = rng.random()
        up = int(rng.choice([0, 0, 1, 2, 4]))
        if kind < ANY:
            x = int(rng.integers(n))
        if kind < 0.35:
            y, up = x, int(rng.integers(1, 40))
        p0, p1 = place[x], place[y]
        if kind < 0.65:
            for _ in range(up):
                p0 = next((j for j in range(p0 - 1, -1, -1) if eng[seq[j]] == eng[y]), p0)
            take = {y}
            for j in range(p1, p0 - 1, -1):
                if seq[j] in take:
                    take |= need[seq[j]]
            if seq[p0] in take:
                continue
            part = seq[p0:p1 + 1]
            new = seq[:p0] + [i for i in part if i in take] + [i for i in part if i not in take] + seq[p1 + 1:]
        else:
            for _ in range(int(rng.choice([0, 0, 1, 2, 4, 8, 16, 30]))):
                p1 = next((j for j in range(p1 + 1, n) if eng[seq[j]] == eng[y]), p1)
            take = {x}
            for j in range(p0 + 1, p1 + 1):
                if need[seq[j]] & take:
                    take.add(seq[j])
            if y in take:
                continue
            part = seq[p0:p1 + 1]
            new = seq[:p0] + [i for i in part if i not in take] + [i for i in part if i in take] + seq[p1 + 1:]
        nd = [rerun(new, p0, k, dones[k]) for k in range(len(plans))]
        w = sum(max(d) + EARLY * sum(d) / n for d in nd)
        if w <= now + HEAT * (1 - step / MOVES) * -np.log(rng.random() + 1e-9):
            seq, dones, now, pairs = new, nd, w, []
            if w < best:
                best, top = w, new
    seq = top
    ends_, done = span(seq, 0)
    order, closes = {}, {}
    for i in seq:
        order.setdefault(eng[i], []).append(i)
        ops[i]["at"] = done[i] - cost[0][i] - lat[0][i]
        closes[ops[i]["group"]] = i
    for group, i in closes.items():
        if group is not None:
            name, args, kw = ops[i]["calls"][-1]
            ops[i]["calls"][-1] = (name, args[:4] + (True,), kw)
    return order, [span(seq, k)[0] for k in range(len(plans))]


SAME, CROSS = 170, 220
PLAN = {}
NE = 8


def rank_program(g, core, T, topo):
    N = len(T.cores)

    def mask(src, dst, last=False):
        e = topo.engines(src, dst)
        return sum(1 << i for i in (e[-NE:] if last else e[:NE]))

    def relay(rank):
        c = T.cores[rank]
        free = [k for k in topo.cores_of(c) if T.rank_of(k) is None and topo.die(k) != topo.die(c) and all(topo.may_write(k, d) for d in T.cores)]
        return free[[k for k in topo.cores_of(c) if T.rank_of(k) is not None].index(c)]

    if not PLAN:
        plans = [build(*f) for f in FIGURES]
        PLAN["ops"] = plans[0]
        PLAN["order"], PLAN["end"] = arrange(plans)
    ops, order = PLAN["ops"], PLAN["order"]
    rank = T.rank_of(core)
    if rank is None:
        for i in range(N):
            if relay(i) == core:
                hands = [ops[j]["calls"][0][1] for j in order["G"] if ops[j]["calls"][0][0] == "send" and ops[j]["calls"][0][1][3]]
                for key, src, ways, _ in hands:
                    to = T.cores[(i + ways[0][0]) % N]
                    rid, pid, _ = topo.addr(to)
                    g.wait_ge(T.sem["held_" + key], NE)
                    g.remote_dma(T[ways[0][1][0]][ways[0][1][1]], T[src[0]][src[1]], T.sem[key], T.sem.sent, pid, rid, mask(core, to))
                g.wait_ge(T.sem.sent, NE * len(hands))
        return
    queue = {"V": g.vector, "S": g.scalar, "P": g.tensor, "G": g, "Y": g.sync}
    call = {
        "tensor_copy": g.vector.tensor_copy, "tensor_tensor": g.vector.tensor_tensor, "tensor_scalar": g.vector.tensor_scalar,
        "tensor_tensor_scan": g.vector.tensor_tensor_scan, "memset": g.vector.memset, "transpose": g.vector.transpose,
        "activation": g.scalar.activation, "matmul": g.tensor.matmul, "iota": g.iota,
    }

    def real(p):
        if not is_ap(p):
            return p
        if p[0] == "*":
            return real(p[1]).indirect(real(p[2]))
        return T[p[0]][p[1]]

    token = {}
    for eng, lst in order.items():
        c = 0
        for i in lst:
            tag = ops[i]["tag"]
            if tag is not None:
                token[i] = ("dma%d" % tag[1], 16) if tag[0] == "dma" else (tag[1], NE * tag[2])
            elif ops[i]["calls"][0][0] != "send":
                c += 1
                token[i] = ("q" + eng, c)
    total = {}
    for s, c in token.values():
        total[s] = max(total.get(s, 0), c)
    nsent = 0
    for eng, lst in order.items():
        if eng == "R":
            continue
        q = queue[eng]
        seen = {}
        for i in lst:
            o = ops[i]
            want = {}
            for d, raw in o["deps"].items():
                if d in token and waits_for(o, ops[d], raw):
                    s, c = token[d]
                    want[s] = max(want.get(s, 0), c)
            for s, c in want.items():
                if seen.get(s, 0) < c:
                    q.wait_ge(T.sem[s], c)
                    seen[s] = c
            for name, args, kw in o["calls"]:
                if name == "send":
                    key, src, ways, relayed = args
                    left = "out_" + key if "out_" + key in total else "sent"
                    nsent += NE * (left == "sent")
                    if relayed:
                        to = relay(rank)
                        rid, pid, _ = topo.addr(to)
                        g.remote_dma(real(src), real(src), T.sem["held_" + key], T.sem[left], pid, rid, mask(core, to, True))
                        continue
                    tos = [T.cores[(rank + hop) % N] for hop, _ in ways]
                    if len(tos) == 1:
                        rid, pid, _ = topo.addr(tos[0])
                        g.remote_dma(real(ways[0][1]), real(src), T.sem[key], T.sem[left], pid, rid, mask(core, tos[0]))
                    else:
                        m = mask(core, tos[0])
                        for to in tos:
                            m &= topo.mask(core, to)
                        ids = [DstId(rid=topo.addr(to)[0], pnc=topo.addr(to)[1]) for to in tos]
                        g.remote_dma_fused([RemoteDMATransfer(dst_ids=ids, dma_engine_mask=m, remote_sem=T.sem[key], srcs=[real(src)], dsts=[real(d) for _, d in ways])], local_sem=T.sem[left])
                    continue
                fn = q.dma_start if name == "dma_start" else call[name]
                ins = fn(*[real(p) for p in args], **{k: real(v) for k, v in kw.items()})
            if i in token:
                ins.then_inc(T.sem[token[i][0]], 16 if o["tag"] else 1)
    for s, c in total.items():
        g.sync.wait_ge(T.sem[s], c)
    g.sync.wait_ge(T.sem.sent, nsent)
